import numpy as np, ml_dtypes
CORES = [23,119,17,113]
N = 4
BF = ml_dtypes.bfloat16
def gentries(a):
    return np.ascontiguousarray(a.reshape(8, 16, -1).transpose(0, 2, 1)).reshape(8, -1)
def gtable(e):
    e = np.asarray(e); return np.ascontiguousarray(e.reshape(8, -1, 16).transpose(0, 2, 1)).reshape(128, -1).astype(np.int32)
L, T, B, RO = 2048, 4, 384, 2
W = L + T * B
def forest(rng, way):
    k = np.zeros((N, 8, RO, T, 2 * B), np.int64)
    for q in range(N):
        for g in range(8):
            for r in range(RO):
                free = np.ones(W, bool); m = int(way[q, g, r])
                for t in range(T):
                    pool = np.flatnonzero(free[:L + t * B])
                    if m == 0: p = rng.permutation(pool)[:2 * B]
                    elif m == 1: p = pool[:2 * B]
                    else: p = pool[len(pool) - 2 * B:]
                    if m > 0 and rng.random() < 0.5: p = rng.permutation(p)
                    free[p] = False; k[q, g, r, t] = p
    return k
def planned(rng, m, s):
    free = np.ones(W, bool); k = np.zeros((T, 2 * B), np.int64); order = rng.permutation(16); seq = None
    for t in range(T):
        pool = rng.permutation(np.flatnonzero(free[:L + t * B])); node = pool >= L; p = pool[:2 * B]
        if m == 0:
            late = node if t < 2 and t < T - 1 else ~node
            p = rng.permutation(pool[np.argsort(late, kind="stable")][:2 * B])
        elif m == 1 and t == 1:
            p = np.concatenate([pool[node], pool[~node][:B]])
        elif m == 2 and t == 1:
            p = np.concatenate([pool[~node][:B], pool[node]])
        elif m == 3:
            if t == 0:
                near = 128 * int(rng.integers(0, L // 128)) + rng.permutation(128); at = np.arange(2 * B)
                put = rng.permutation(np.flatnonzero(at % N == int(rng.integers(0, N))))[:128]
                rest = np.ones(2 * B, bool); rest[put] = False
                seq = np.zeros(2 * B, np.int64); seq[put] = near; seq[rest] = pool[~np.isin(pool, near)][:2 * B - 128]
            n = len(seq) // 2; slot = np.arange(n) if t == T - 1 else rng.permutation(B)[:n]
            p = np.zeros(2 * B, np.int64); rest = np.ones(2 * B, bool)
            rest[slot] = False; rest[B + slot] = False; p[slot] = seq[0::2]; p[B + slot] = seq[1::2]
            p[rest] = pool[~np.isin(pool, seq)][:2 * B - 2 * n]; seq = L + t * B + slot
        elif m == 4:
            two = np.isin(pool % 16, order[:2]); late = two if t < T - 1 else ~two
            p = rng.permutation(pool[np.argsort(late, kind="stable")][:2 * B])
        elif m == 5 and t == 0:
            p = rng.permutation(pool[np.argsort(order[pool % 16], kind="stable")][:2 * B])
        elif m == 6 and t == 0 and s is not None:
            p = p[np.argsort(s[p], kind="stable")]; i = rng.permutation(B); p = np.concatenate([p[:B][i], p[B:][i]])
        free[p] = False; k[t] = p
    return k
def parts(rng, way=None):
    x = rng.integers(-128, 128, (N, 8, 16, L)); k = forest(rng, np.zeros((N, 8, RO)) if way is None else way)
    a = rng.integers(-1, 2, (N, 8, 16, 16)); b = rng.integers(-1, 2, (N, 8, 16, 16)); w = rng.integers(-127, 128, (N, 8, 16))
    return x, k, a, b, w
def blocks(m):
    o = np.zeros((N, 8, 16, 8, 16), np.float32)
    for g in range(8): o[:, g, :, g, :] = m[:, g]
    return o.reshape(N, 128, 128).astype(BF)
def pack(x, k, a, b, w):
    return {"x": np.ascontiguousarray(x.reshape(N, 128, L)).astype(np.float32).astype(BF), "kids": np.stack([gtable(e.reshape(8, -1)) for e in k]),
            "ml": blocks(a), "mr": blocks(b), "w": w.reshape(N, 128, 1).astype(np.float32).astype(BF)}
def setup_inputs(rng):
    return pack(*parts(rng))
def setup_inputs_runs(rng):
    way = rng.choice(np.array([0, 1, 1, 2, 2]), (N, 8, RO)); i = rng.permutation(8); way[:, i[0]] = 1; way[:, i[1]] = 2
    return pack(*parts(rng, way))
def setup_inputs_ends(rng):
    x, k, a, b, w = parts(rng)
    x = rng.choice(np.array([-128, -127, -1, 0, 1, 126, 127]), (N, 8, 16, L))
    x[:, 0] = rng.integers(126, 128, (N, 16, L)); x[:, 1] = rng.integers(-128, -126, (N, 16, L)); a[:, :2] = 1; b[:, :2] = 1
    x[:, 2] = rng.choice(np.array([-128, 127]), (N, 1, L)); x[:, 2, 0] = rng.integers(-128, 128, (N, L)); a[:, 2] = 1; b[:, 2] = -1
    x[:, 3] = rng.integers(-2, 3, (N, 16, L))
    return pack(x, k, a, b, rng.choice(np.array([-127, 127]), (N, 8, 16)))
def setup_inputs_ties(rng):
    x, k, a, b, w = parts(rng)
    w[:, 0::4] = 0
    w[:, 1::4] = 0; w[:, 1::4, 0] = rng.integers(1, 128, (N, 2)); x[:, 1::4, 0] = rng.integers(-4, 5, (N, 2, L))
    for m in (a, b):
        m[:, 1::4, :, 0] = 0; m[:, 1::4, 0, 0] = 1
    v = rng.integers(-128, 128, (N, 2, 16, 1)); o = np.argsort(rng.random((N, 2, 16, L)), axis=2)
    x[:, 2::4] = np.take_along_axis(np.ascontiguousarray(np.broadcast_to(v, (N, 2, 16, L))), o, 2); w[:, 2::4] = rng.integers(1, 128, (N, 2, 1))
    x[:, 3::4, 2:] = 127; x[:, 3::4, 1] = rng.integers(-1, 2, (N, 2, L)); w[:, 3::4] = 127; w[:, 3::4, 0] = 0; w[:, 3::4, 1] = 1
    return pack(x, k, a, b, w)
def setup_inputs_crowd(rng):
    x, k, a, b, w = parts(rng); o = [int(g) for g in rng.permutation(8)]
    for i, v, c in ((2, 127, -1), (7, -127, 1)):
        x[:, o[i]] = np.where(rng.random((N, 1, L)) < 0.25, -128, rng.integers(-128, -99, (N, 16, L))); w[:, o[i]] = v; a[:, o[i]] = c; b[:, o[i]] = c
    w[:, o[3]] = 0
    for q in range(N):
        for i in range(8):
            s = np.add.reduce(w[q, o[i]][:, None] * x[q, o[i]], axis=0)
            for r in range(RO): k[q, o[i], r] = planned(rng, i if i < 7 else 1, s if r == 0 else None)
    return pack(x, k, a, b, w)
def setup_inputs_spread(rng):
    x, k, a, b, w = parts(rng)
    x = np.rint(127 * rng.uniform(-1, 1, (N, 8, 16, L)) * np.exp2(-rng.integers(0, 7, (N, 8, 1, L)).astype(np.float64))).astype(np.int64) * (rng.random((N, 8, 1, L)) > 0.0625)
    w = np.rint(127 * rng.uniform(-1, 1, (N, 8, 16)) * np.exp2(-rng.integers(0, 7, (N, 8, 16)).astype(np.float64))).astype(np.int64)
    s = rng.uniform(0.2, 1, (N, 8, 1, 1)); a = a * (rng.random(a.shape) < s); b = b * (rng.random(b.shape) < s)
    return pack(x, k, a, b, w)
def check_inputs(d):
    bad = []; own = np.kron(np.eye(8), np.ones((16, 16))) > 0
    for n, lo, hi in (("x", -128, 127), ("ml", -1, 1), ("mr", -1, 1), ("w", -127, 127)):
        v = np.asarray(d[n]).astype(np.float32)
        if not np.all((v == np.floor(v)) & (v >= lo) & (v <= hi)): bad.append("whole numbers of " + n)
        if n in ("ml", "mr") and not np.all(v[:, ~own] == 0): bad.append("zeros of " + n)
    k = np.stack([gentries(e) for e in d["kids"]]).astype(np.int64).reshape(N, 8, RO, T, 2 * B)
    for t in range(T):
        if np.min(k[:, :, :, t]) < 0 or np.max(k[:, :, :, t]) >= L + t * B: bad.append("range of kids")
    if not np.all(np.diff(np.sort(k.reshape(N, 8, RO, -1), axis=3), axis=3) > 0): bad.append("kids used twice")
    return bad
def reference(x, kids, ml, mr, w):
    leaf = x.astype(np.float64).reshape(N, 8, 16, L); ws = w.astype(np.float64).reshape(N, 8, 16, 1)
    cl, cr = [np.stack([m.astype(np.float64)[:, 16 * g:16 * g + 16, 16 * g:16 * g + 16] for g in range(8)], axis=1).transpose(0, 1, 3, 2) for m in (ml, mr)]
    kk = np.stack([gentries(e) for e in kids]).astype(np.int64).reshape(N, 8, RO, T, 2, B)
    for r in range(RO):
        h = np.zeros((N, 8, 16, W)); h[..., :L] = leaf
        size = np.ones((N, 8, W), np.int64); root = np.ones((N, 8, W), bool); order = []
        for t in range(T):
            a, b = kk[:, :, r, t, 0], kk[:, :, r, t, 1]; lo = L + t * B
            ha = np.take_along_axis(h, a[:, :, None, :], 3); hb = np.take_along_axis(h, b[:, :, None, :], 3)
            h[..., lo:lo + B] = np.clip(np.floor((np.matmul(cl, ha) + np.matmul(cr, hb)) * 0.25), -127, 127)
            size[..., lo:lo + B] = np.take_along_axis(size, a, 2) + np.take_along_axis(size, b, 2)
            swap = np.add.reduce(ws * ha, axis=2) < np.add.reduce(ws * hb, axis=2)
            np.put_along_axis(root, a, False, 2); np.put_along_axis(root, b, False, 2)
            order.append((np.where(swap, b, a), np.where(swap, a, b)))
        rs = np.where(root, size, 0); start = np.add.accumulate(rs, axis=2) - rs
        for t in range(T - 1, -1, -1):
            one, two = order[t]; s = start[..., L + t * B:L + t * B + B].copy()
            np.put_along_axis(start, one, s, 2); np.put_along_axis(start, two, s + np.take_along_axis(size, one, 2), 2)
        at = np.argsort(start[..., :L], axis=2)
        new = np.take_along_axis(leaf, at[:, :, None, :], 3).reshape(N, 8, 16, L // N, N)
        leaf = np.ascontiguousarray(new.transpose(4, 1, 2, 0, 3)).reshape(N, 8, 16, L)
    return {"y": leaf.reshape(N, 128, L).astype(np.float32).astype(BF)}

@@ -1,0 +1,516 @@
+from concourse.bass import DstId, RemoteDMATransfer
+from concourse.mybir import dt, AluOpType, ActivationFunctionType
+
+A = AluOpType
+AF = ActivationFunctionType
+L, NT, B, RO = 2048, 4, 384, 2
+K = 2 * B
+C = B // 2
+SLOT = 16
+EDGE = SLOT + 16 * 72
+TW = EDGE + NT * K
+MAGIC = 12582912.0
+PART = ((0, 64), (64, 128))
+
+SCRATCH = {
+    "KI": ("sbuf", [128, 384], "int32"), "K16": ("sbuf", [128, 384], "uint16"),
+    "ZA": ("sbuf", [128, 384], "int32"), "ZB": ("sbuf", [128, 384], "int32"), "SG": ("sbuf", [128, 384], "uint16"),
+    "VAL": ("sbuf", [128, NT * K], "float32"), "ZZ": ("sbuf", [128, 256], "float32"),
+    "SZ": ("sbuf", [128, L + NT * B], "bfloat16"), "TAB": ("sbuf", [128, TW], "float32"),
+    "IDN": ("sbuf", [128, 128], "bfloat16"), "NID": ("sbuf", [128, 128], "bfloat16"),
+    "BLA": ("sbuf", [128, 128], "bfloat16"), "BLK": ("sbuf", [128, 128], "bfloat16"), "TRI": ("sbuf", [128, 128], "bfloat16"),
+    "EQ": ("sbuf", [128, 2048], "bfloat16"), "DQ": ("sbuf", [128, 2048], "bfloat16"),
+    "C72": ("sbuf", [128, 16], "bfloat16"), "CI": ("sbuf", [128, 72], "float32"), "CT": ("sbuf", [128, 72], "float32"),
+    "CB": ("sbuf", [128, 128], "bfloat16"),
+    "MI": ("sbuf", [128, 256], "bfloat16"), "WI": ("sbuf", [128, 1], "bfloat16"), "MM": ("sbuf", [128, 256], "bfloat16"),
+    "WP": ("sbuf", [128, 128], "bfloat16"), "WN": ("sbuf", [128, 128], "bfloat16"),
+    "F16": ("sbuf", [128, B], "float16"), "DX": ("sbuf", [128, NT * K], "float32"),
+    "UX": ("sbuf", [128, B], "float32"), "UB": ("sbuf", [128, K], "bfloat16"),
+    "PR": ("sbuf", [128, 2048], "float16"), "QA": ("sbuf", [128, 128], "int32"), "QB": ("sbuf", [128, 128], "int32"),
+    "QL": ("sbuf", [128, 128], "uint16"),
+    "YL": ("sbuf", [128, L], "bfloat16"),
+}
+for _t in range(NT):
+    SCRATCH["G%d" % _t] = ("sbuf", [128, K], "bfloat16")
+for _r in range(RO):
+    SCRATCH.update({
+        "H%d" % _r: ("sbuf", [128, L + 3 * B], "bfloat16"),
+        "PW%d" % _r: ("sbuf", [128, 4096], "float32"), "PL%d" % _r: ("sbuf", [128, 256], "float32"),
+        "NA%d" % _r: ("sbuf", [128, 72], "float32"), "PT%d" % _r: ("sbuf", [128, 200], "uint16"),
+        "RS%d" % _r: ("sbuf", [128, 224], "bfloat16"), "INC%d" % _r: ("sbuf", [128, 224], "float32"),
+        "RL%d" % _r: ("sbuf", [128, 224], "float16"), "RM%d" % _r: ("sbuf", [128, 128], "float16"),
+        "SR%d" % _r: ("sbuf", [128, 3 * K], "bfloat16"), "WB%d" % _r: ("sbuf", [128, L], "bfloat16"),
+    })
+for _b in range(8):
+    SCRATCH["b%d" % _b] = ("psum", [128, 512], "float32")
+PSUM = ["b%d" % i for i in range(8)]
+
+SEMAPHORES = ["qv", "qs", "qp", "qg", "sent", "arr0"] + ["arr1_%d" % i for i in range(4)] + ["d%d" % i for i in range(16)]
+
+
+def rank_program(g, core, T, topo):
+    me = T.rank_of(core)
+    if me is None:
+        return
+    cores = list(T.cores)
+    eng = {"v": g.vector, "s": g.scalar, "p": g.tensor, "g": g, "y": g.sync}
+    known = {q: {} for q in eng}
+    total = {}
+    acc = {}
+    ndma = [0]
+
+    def span(x):
+        if isinstance(x, str):
+            return x, 0, SCRATCH[x][1][1]
+        return x
+
+    def learn(q, sem, n, snap):
+        k = known[q]
+        if k.get(sem, 0) < n:
+            k[sem] = n
+        for s2, n2 in snap.items():
+            if k.get(s2, 0) < n2:
+                k[s2] = n2
+
+    def sync_for(q, reads, writes):
+        need = {}
+        for kind, lst in (("r", reads), ("w", writes)):
+            for x in lst:
+                b, lo, hi = span(x)
+                ps = b in PSUM
+                for rk, rlo, rhi, rq, sem, n, snap in acc.get(b, []):
+                    if ps:
+                        if rq == q and (q == "p" or (kind == "r" and rk == "r")):
+                            continue
+                    elif rhi <= lo or rlo >= hi or (kind == "r" and rk == "r"):
+                        continue
+                    if known[q].get(sem, 0) >= n:
+                        continue
+                    if sem not in need or need[sem][0] < n:
+                        need[sem] = (n, snap)
+        for sem in sorted(need, key=lambda s: -len(need[s][1])):
+            n, snap = need[sem]
+            if known[q].get(sem, 0) < n:
+                eng[q].wait_ge(T.sem[sem], n)
+                learn(q, sem, n, snap)
+
+    def note(q, reads, writes, sem, n):
+        snap = dict(known[q])
+        for kind, lst in (("r", reads), ("w", writes)):
+            for x in lst:
+                b, lo, hi = span(x)
+                old = acc.setdefault(b, [])
+                if kind == "w" and b not in PSUM:
+                    old[:] = [o for o in old if not (o[1] >= lo and o[2] <= hi)]
+                old.append((kind, lo, hi, q, sem, n, snap))
+
+    def op(q, reads, writes, call):
+        sync_for(q, reads, writes)
+        sem = "q" + q
+        total[sem] = total.get(sem, 0) + 1
+        call().then_inc(T.sem[sem], 1)
+        note(q, reads, writes, sem, total[sem])
+
+    def dma(q, reads, writes, out, in_):
+        sync_for(q, reads, writes)
+        sem = "d%d" % ndma[0]
+        ndma[0] += 1
+        total[sem] = 16
+        eng[q].dma_start(out=out, in_=in_).then_inc(T.sem[sem], 16)
+        note(q, reads, writes, sem, 16)
+
+    V, S, P = g.vector, g.scalar, g.tensor
+
+    def ts(b_out, lo, hi, in_ap, reads, s1, s2, o0, o1=None):
+        o = T[b_out][:, lo:hi]
+        if o1 is None:
+            op("v", reads, [(b_out, lo, hi)], lambda: V.tensor_scalar(o, in_ap, s1, None, o0))
+        else:
+            op("v", reads, [(b_out, lo, hi)], lambda: V.tensor_scalar(o, in_ap, s1, s2, o0, o1))
+
+    def tt(b_out, lo, hi, a0, a1, reads, o0):
+        op("v", reads, [(b_out, lo, hi)], lambda: V.tensor_tensor(T[b_out][:, lo:hi], a0, a1, o0))
+
+    def vcopy(b_out, lo, hi, in_ap, reads):
+        op("v", reads, [(b_out, lo, hi)], lambda: V.tensor_copy(T[b_out][:, lo:hi], in_ap))
+
+    def fill(b, lo, hi, c):
+        op("v", [], [(b, lo, hi)], lambda: V.memset(T[b][:, lo:hi], c))
+
+    def act(b_out, lo, hi, in_ap, reads, func, scale=None, bias=None):
+        o = T[b_out][:, lo:hi]
+        if bias is not None:
+            op("s", reads, [(b_out, lo, hi)], lambda: S.activation(o, in_ap, func, bias=bias, scale=scale))
+        elif scale is None:
+            op("s", reads, [(b_out, lo, hi)], lambda: S.activation(o, in_ap, func))
+        else:
+            op("s", reads, [(b_out, lo, hi)], lambda: S.activation(o, in_ap, func, scale=scale))
+
+    def copy(q, b_out, lo, hi, in_ap, reads):
+        if q == "v":
+            vcopy(b_out, lo, hi, in_ap, reads)
+        else:
+            act(b_out, lo, hi, in_ap, reads, AF.Copy)
+
+    def mm(bank, out_ap, lhs, lo, rhs_ap, reads, start, stop):
+        op("p", [(lhs, lo, lo + 128)] + reads, [bank], lambda: P.matmul(out_ap, T[lhs][:, lo:lo + 128], rhs_ap, start, stop))
+
+    def iota(b, lo, hi, pattern, base, cm, flag=True):
+        if flag:
+            op("g", [], [(b, lo, hi)], lambda: g.iota(T[b][:, lo:hi], pattern, base, cm, allow_small_or_imprecise_dtypes=True))
+        else:
+            op("g", [], [(b, lo, hi)], lambda: g.iota(T[b][:, lo:hi], pattern, base, cm))
+
+    def select(b_out, b_in, n, pattern, cmp, base, cm):
+        op("g", [(b_in, 0, n)], [(b_out, 0, n)], lambda: g.affine_select(T[b_out][:, 0:n], T[b_in][:, 0:n], pattern, cmp, 0.0, base, cm))
+
+    def lists(r):
+        lo, hi = 192 * r, 192 * r + 192
+        ki = T.KI[:, lo:hi]
+        ts("ZA", lo, hi, ki, [("KI", lo, hi)], 4097, None, A.mult)
+        vcopy("K16", lo, hi, ki, [("KI", lo, hi)])
+        ts("ZB", lo, hi, T.ZA[:, lo:hi], [("ZA", lo, hi)], 4, 4095, A.arith_shift_right, A.bitwise_and)
+        vcopy("SG", lo, hi, T.ZB[:, lo:hi], [("ZB", lo, hi)])
+
+    def scat(r, t):
+        b, c = "PW%d" % r, 192 * r + 48 * t
+        op("s", [("SG", c, c + 48), ("VAL", K * t, K * t + K)], [b],
+           lambda: S.activation(T[b][:, :].indirect(T.SG[:, c:c + 48]), T.VAL[:, K * t:K * t + K], AF.Silu))
+
+    def conv(r):
+        b, o = "PW%d" % r, "PL%d" % r
+        dma("y", [b], [o], T[o][:, :], T[b][0:128:16, :])
+
+    def size_gather(r, t, q):
+        w, c, lo = L + B * t, 192 * r + 48 * t, K * (t - 1)
+        copy(q, "SR%d" % r, lo, lo + K, T.SZ[:, 0:w].indirect(T.K16[:, c:c + 48]), [("SZ", 0, w), ("K16", c, c + 48)])
+
+    def size_add(r, t):
+        sr, lo = "SR%d" % r, K * (t - 1)
+        for i in range(2):
+            c = lo + B * i
+            mm("b5", T.b5[:, 0:B], "IDN", 0, T[sr][:, c:c + B], [(sr, c, c + B)], i == 0, i == 1)
+
+    def size_store(r, t, q):
+        copy(q, "SZ", L + B * t, L + B * t + B, T.b5[:, 0:B], ["b5"])
+
+    def size_list(r):
+        for q in range(16):
+            mm("b6", T.b6[:, 0:96], "DQ", 128 * q, T.SZ[:, L + q:L + 4 * B:16], [("SZ", L, L + 4 * B)], q == 0, q == 15)
+
+    def root_flags(r):
+        pl, rs = "PL%d" % r, "RS%d" % r
+        act(rs, 0, 224, T[pl][:, 0:224], [pl], AF.Relu, -1.0, 1.0)
+
+    def root_sizes(r):
+        rs, na = "RS%d" % r, "NA%d" % r
+        tt(na, 0, 72, T[rs][:, 128:200], T.CT[:, :], [(rs, 128, 200), "CT"], A.mult)
+        tt(rs, 128, 224, T[rs][:, 128:224], T.b6[:, 0:96], [(rs, 128, 224), "b6"], A.mult)
+
+    def root_starts(r):
+        pl, rs, na, pt, inc, rl = ["%s%d" % (n, r) for n in ("PL", "RS", "NA", "PT", "INC", "RL")]
+        mm("b6", T.b6[:, 224:448], "BLK", 0, T[rs][:, :], [rs], True, True)
+        mm("b6", T.b6[:, 0:224], "TRI", 0, T[rs][:, :], [rs], True, True)
+        tt(pl, 128, 200, T[na][:, :], T[pl][:, 128:200], [na, (pl, 128, 200)], A.add)
+        op("v", ["b6", rs], [inc], lambda: V.tensor_tensor_scan(T[inc][:, :], T.b6[:, 224:448], T[rs][:, :], 0.0, A.add, A.max))
+        tt(rl, 0, 224, T[inc][:, :], T.b6[:, 0:224], [inc, "b6"], A.subtract)
+        ts(pt, 0, 200, T[pl][:, 0:200], [pl], 0.25, None, A.add)
+
+    def root_rows3(r):
+        rl = "RL%d" % r
+        for q in range(16):
+            mm("b6", T.b6[:, q:B:16], "EQ", 128 * q, T[rl][:, 200:224], [(rl, 200, 224)], True, True)
+
+    def root_rows(r, es):
+        rl = "RL%d" % r
+        for bank, qs, e in (("b5", range(0, 6), es[0]), ("b4", range(6, 12), es[1]), ("b2", range(12, 16), es[2])):
+            for i, q in enumerate(qs):
+                mm(bank, T[bank][:, 72 * i:72 * i + 72], "EQ", 128 * q, T[rl][:, 128:200], [(rl, 128, 200)], True, True)
+            c = SLOT + 72 * qs[0]
+            copy(e, "TAB", c, c + 72 * len(qs), T[bank][:, 0:72 * len(qs)], [bank])
+            if bank == "b5":
+                root_rows3(r)
+
+    def root_leaves(r):
+        rl, rs = "RL%d" % r, "RS%d" % r
+        tt("RM%d" % r, 0, 128, T[rl][:, 0:128], T[rs][:, 0:128], [(rl, 0, 128), (rs, 0, 128)], A.mult)
+
+    def bias():
+        for b in ("b0", "b1"):
+            mm(b, T[b][:, 0:C], "CB", 0, T.SZ[:, 0:C], [("SZ", 0, C)], True, False)
+
+    def gather(r, t, side, h, q):
+        hb, w, c, o = "H%d" % r, L + B * t, 192 * r + 48 * t + 24 * side + 12 * h, B * side + C * h
+        copy(q, "G%d" % t, o, o + C, T[hb][:, 0:w].indirect(T.K16[:, c:c + 12]), [(hb, 0, w), ("K16", c, c + 12)])
+
+    def sums(t):
+        gb = "G%d" % t
+        for h, b in enumerate(("b0", "b1")):
+            for side in range(2):
+                o = B * side + C * h
+                mm(b, T[b][:, 0:C], "MM", 128 * side, T[gb][:, o:o + C], [(gb, o, o + C)], False, side == 1)
+
+    def dbank(t):
+        return ("b2", "b7", "b4", "b0")[t]
+
+    def rbank(t):
+        return ("b3", "b3", "b1", "b3")[t]
+
+    def diff(t):
+        b, gb = dbank(t), "G%d" % t
+        mm(b, T[b][:, 0:B], "WN", 0, T[gb][:, 0:B], [(gb, 0, B)], True, False)
+        mm(b, T[b][:, 0:B], "WP", 0, T[gb][:, B:K], [(gb, B, K)], False, True)
+
+    def vectors(r, t):
+        for h, b in enumerate(("b0", "b1")):
+            ts("F16", C * h, C * h + C, T[b][:, 0:C], [b], -127.0, 127.0, A.max, A.min)
+        for h in range(2):
+            lo = L + B * t + C * h
+            ts("H%d" % r, lo, lo + C, T.F16[:, C * h:C * h + C], [("F16", C * h, C * h + C)], MAGIC, MAGIC, A.add, A.subtract)
+
+    def moves0_a():
+        act("UX", 0, B, T.b2[:, 0:B], ["b2"], AF.Relu, -1.0, 1.0)
+
+    def moves0_b():
+        act("DX", 0, B, T.UX[:, 0:B], [("UX", 0, B)], AF.Relu, -1.0, 1.0)
+        act("DX", B, K, T.DX[:, 0:B], [("DX", 0, B)], AF.Relu, -1.0, 1.0)
+
+    def moves1_w():
+        for bank, idn, o in (("b7", "NID", B), ("b5", "IDN", 0)):
+            mm(bank, T[bank][:, 0:B], idn, 0, T.SR1[:, o:o + B], [("SR1", o, o + B)], True, False)
+
+    def moves1_x(i):
+        bank = ("b7", "b5")[i]
+        mm(bank, T[bank][:, 0:B], "WN", 0, T.G1[:, 0:B], [("G1", 0, B)], False, False)
+        mm(bank, T[bank][:, 0:B], "WP", 0, T.G1[:, B:K], [("G1", B, K)], False, True)
+
+    def moves1_y():
+        act("UB", 0, B, T.b7[:, 0:B], ["b7"], AF.Relu, -1.0)
+        act("UB", B, K, T.b5[:, 0:B], ["b5"], AF.Relu, 1.0, -16.0)
+
+    def moves1_z():
+        for i, bank, o in ((0, "b7", B), (1, "b5", 0)):
+            mm(bank, T[bank][:, 0:B], "IDN", 0, T.SR1[:, o:o + B], [("SR1", o, o + B)], True, False)
+            mm(bank, T[bank][:, 0:B], "NID", 0, T.UB[:, B * i:B * i + B], [("UB", B * i, B * i + B)], False, True)
+            act("DX", K + B * i, K + B * i + B, T[bank][:, 0:B], [bank], AF.Relu)
+
+    def relus(t):
+        b, rb = dbank(t), rbank(t)
+        act(rb, 0, B, T[b][:, 0:B], [b], AF.Relu, -1.0, 16.0)
+        act(b, 0, B, T[b][:, 0:B], [b], AF.Relu)
+
+    def mins(r, t):
+        sr, o = "SR%d" % r, K * (t - 1)
+        for i, b in ((1, rbank(t)), (0, dbank(t))):
+            c = o + B - B * i
+            tt("DX", K * t + B * i, K * t + B * i + B, T[b][:, 0:B], T[sr][:, c:c + B], [b, (sr, c, c + B)], A.min)
+
+    def down(r):
+        tab = "TAB"
+        pt, h, wb, rm = ["%s%d" % (n, r) for n in ("PT", "H", "WB", "RM")]
+        for i in (1, 0):
+            d = K * 3 + B * i
+            tt(tab, EDGE + B * i, EDGE + B * i + B, T.b6[:, 0:B], T.DX[:, d:d + B], ["b6", ("DX", d, d + B)], A.add)
+        for t in (2, 1, 0):
+            w = EDGE + K * (3 - t)
+            c = 128 + 24 * t
+            for i in range(2):
+                d = K * t + B * i
+                tt(tab, w + B * i, w + B * i + B, T[tab][:, 0:w].indirect(T[pt][:, c:c + 24]), T.DX[:, d:d + B],
+                   [(tab, 0, w), (pt, c, c + 24), ("DX", d, d + B)], A.add)
+        for k, (lo, hi) in enumerate(PART):
+            vcopy("PR", 16 * lo, 16 * hi, T[tab][:, :].indirect(T[pt][:, lo:hi]), [tab, (pt, lo, hi)])
+            b = "b%d" % (4 + k)
+            mm(b, T[b][:, 0:hi - lo], "IDN", 0, T[rm][:, lo:hi], [(rm, lo, hi)], True, False)
+            for q in range(16):
+                mm(b, T[b][:, 0:hi - lo], "DQ", 128 * q, T.PR[:, 16 * lo + q:16 * hi:16], [("PR", 16 * lo, 16 * hi)], False, q == 15)
+        for k, (lo, hi) in enumerate(PART):
+            b = "b%d" % (4 + k)
+            ts("QA", lo, hi, T[b][:, 0:hi - lo], [b], 2049.0, None, A.mult)
+            ts("QB", lo, hi, T.QA[:, lo:hi], [("QA", lo, hi)], 2, 2047, A.arith_shift_right, A.bitwise_and)
+            vcopy("QL", lo, hi, T.QB[:, lo:hi], [("QB", lo, hi)])
+            op("v", [("QL", lo, hi), (h, 16 * lo, 16 * hi)], [wb],
+               lambda: V.tensor_copy(T[wb][:, :].indirect(T.QL[:, lo:hi]), T[h][:, 16 * lo:16 * hi]))
+
+    def plan(src):
+        s = cores[src]
+        off = [d for d in range(4) if d != src and topo.chip(cores[d]) != topo.chip(s)]
+        on = [d for d in range(4) if d != src and topo.chip(cores[d]) == topo.chip(s)]
+        oe = topo.engines(s, cores[off[0]])
+        n = len(oe) // len(off)
+        res = {d: oe[n * i:n * i + n] for i, d in enumerate(off)}
+        for d in on:
+            res[d] = [e for e in topo.engines(s, cores[d]) if e not in oe]
+        return res
+
+    def exchange(r):
+        wb = "WB%d" % r
+        dst = ("H1", "YL")[r]
+        sem = "arr0" if r == 0 else "arr1_%d" % me
+        tr = []
+        n = 0
+        for d, es in plan(me).items():
+            rid, pid, _se = topo.addr(cores[d])
+            m = sum(1 << e for e in es)
+            n += len(es)
+            tr.append(RemoteDMATransfer(dst_ids=[DstId(rid=rid, pnc=pid)], dma_engine_mask=m, remote_sem=T.sem[sem],
+                                        src=T[wb][:, 512 * d:512 * d + 512], dst=T[dst][:, 512 * me:512 * me + 512]))
+        sync_for("g", [wb], [])
+        g.remote_dma_fused(tr, local_sem=T.sem["sent"])
+        total["sent"] = total.get("sent", 0) + n
+        note("g", [wb], [], "sent", total["sent"])
+        others = [s for s in range(4) if s != me]
+        got = sum(len(plan(s)[me]) for s in others)
+        for s in others:
+            sem, n = ("arr0", got) if r == 0 else ("arr1_%d" % s, len(plan(s)[me]))
+            total[sem] = n
+            acc.setdefault(dst, []).append(("w", 512 * s, 512 * s + 512, "x", sem, n, {}))
+        if r == 0:
+            vcopy(dst, 512 * me, 512 * me + 512, T[wb][:, 512 * me:512 * me + 512], [wb])
+
+    dma("y", [], [("KI", 0, 192)], T.KI[:, 0:192], T.kids[:, 0:192])
+    dma("s", [], [("H0", 0, L)], T.H0[:, 0:L], T.x[:, :])
+    dma("y", [], [("MI", 0, 128)], T.MI[:, 0:128], T.ml[:, :])
+    dma("y", [], [("MI", 128, 256)], T.MI[:, 128:256], T.mr[:, :])
+    dma("y", [], ["WI"], T.WI[:, :], T.w[:, :])
+    dma("y", [], [("KI", 192, 384)], T.KI[:, 192:384], T.kids[:, 192:384])
+
+    def val(t):
+        iota("VAL", K * t, K * t + K, [[1, K]], EDGE + K * (3 - t), 0)
+
+    fill("ZZ", 0, 256, 0.0)
+    for r in range(RO):
+        dma("sy"[r], ["ZZ"], ["PW%d" % r], T["PW%d" % r][0:128:16, :], T.ZZ[:, :])
+    fill("SZ", 0, L, 1.0)
+    act("TAB", 0, 16, T.SZ[:, 0:16], [("SZ", 0, 16)], AF.Silu, 0.0)
+    val(0)
+    select("BLA", "SZ", 128, [[-16, 8], [0, 16]], A.is_ge, 0, 1)
+    select("BLK", "BLA", 128, [[16, 8], [0, 16]], A.is_ge, 15, -1)
+    val(1)
+    select("IDN", "SZ", 128, [[-1, 128]], A.is_equal, 0, 1)
+    val(2)
+    val(3)
+    select("DQ", "SZ", 2048, [[-1024, 16], [-16, 8], [1023, 16]], A.is_equal, 0, 1)
+    select("TRI", "BLK", 128, [[-1, 128]], A.is_ge, 0, 1)
+    iota("C72", 0, 16, [[0, 16]], 72, 0)
+    iota("CI", 0, 72, [[1, 72]], SLOT + 16 * 72, 0)
+    select("EQ", "SZ", 2048, [[-1, 16], [-16, 8], [0, 16]], A.is_equal, 0, 1)
+    fill("SZ", L, L + B, 2.0)
+    fill("CB", 0, 128, -0.375 / 128)
+    lists(0)
+    ts("MM", 0, 256, T.MI[:, :], ["MI"], 0.25, None, A.mult)
+    ts("WP", 0, 128, T.BLK[:, :], ["BLK", "WI"], T.WI[:, 0:1], 16.0, A.mult, A.mult)
+    ts("WN", 0, 128, T.BLK[:, :], ["BLK", "WI"], T.WI[:, 0:1], -16.0, A.mult, A.mult)
+    lists(1)
+
+    for t in range(4):
+        scat(0, t)
+    conv(0)
+
+    def up0(t, q):
+        for h in range(2):
+            gather(0, t, 0, h, q)
+            gather(0, t, 1, h, q)
+        if t < 3:
+            sums(t)
+
+    bias()
+    up0(0, "v")
+    diff(0)
+    vectors(0, 0)
+    bias()
+    size_gather(0, 1, "v")
+    size_add(0, 1)
+    up0(1, "v")
+    size_store(0, 1, "v")
+    diff(1)
+    vectors(0, 1)
+    bias()
+    size_gather(0, 2, "v")
+    size_add(0, 2)
+    relus(1)
+    up0(2, "v")
+    size_store(0, 2, "v")
+    diff(2)
+    vectors(0, 2)
+    mm("b6", T.b6[:, 0:16], "TRI", 0, T.C72[:, :], ["C72"], True, True)
+    size_gather(0, 3, "v")
+    size_add(0, 3)
+    op("v", ["CI", "b6"], ["CT"], lambda: V.tensor_scalar(T.CT[:, :], T.CI[:, :], T.b6[:, 0:1], None, A.subtract))
+    mins(0, 1)
+    size_store(0, 3, "v")
+    relus(2)
+    mins(0, 2)
+    up0(3, "s")
+    size_list(0)
+    diff(3)
+    root_flags(0)
+    relus(3)
+    moves0_a()
+    root_sizes(0)
+    root_starts(0)
+    mins(0, 3)
+    moves0_b()
+    root_rows(0, "sss")
+    root_leaves(0)
+    size_gather(1, 1, "s")
+    scat(1, 0)
+    size_add(1, 1)
+    size_store(1, 1, "s")
+    size_gather(1, 2, "s")
+    scat(1, 1)
+    scat(1, 2)
+    scat(1, 3)
+    conv(1)
+    down(0)
+    size_add(1, 2)
+    size_store(1, 2, "s")
+    size_gather(1, 3, "s")
+    size_add(1, 3)
+    size_store(1, 3, "s")
+    exchange(0)
+    size_list(1)
+    root_flags(1)
+    root_sizes(1)
+    root_starts(1)
+    bias()
+    root_rows(1, "svs")
+    root_leaves(1)
+    act("NID", 0, 128, T.IDN[:, :], ["IDN"], AF.Copy, -1.0)
+    moves1_w()
+
+    for t in range(NT):
+        for h in range(2):
+            gather(1, t, 0, h, "v")
+            gather(1, t, 1, h, "s")
+        if t < 3:
+            sums(t)
+        if t == 1:
+            moves0_a()
+            moves1_x(0)
+        else:
+            diff(t)
+        if t == 2:
+            moves0_b()
+            moves1_x(1)
+        if t < 3:
+            vectors(1, t)
+        if t < 2:
+            bias()
+    tt("UX", 0, B, T.b4[:, 0:B], T.SR1[:, K + B:K + K], ["b4", ("SR1", K + B, K + K)], A.min)
+    act("b1", 0, B, T.b4[:, 0:B], ["b4"], AF.Relu, -1.0, 16.0)
+    tt("DX", 2 * K + B, 3 * K, T.b1[:, 0:B], T.SR1[:, K:K + B], ["b1", ("SR1", K, K + B)], A.min)
+    relus(3)
+    mins(1, 3)
+    act("DX", 2 * K, 2 * K + B, T.UX[:, 0:B], [("UX", 0, B)], AF.Relu)
+    moves1_y()
+    moves1_z()
+    down(1)
+    exchange(1)
+    dma("s", [("WB1", 512 * me, 512 * me + 512)], [], T.y[:, 512 * me:512 * me + 512], T.WB1[:, 512 * me:512 * me + 512])
+    for i, s in enumerate([s for s in range(4) if topo.chip(cores[s]) == topo.chip(core) and s != me] +
+                          [s for s in range(4) if topo.chip(cores[s]) != topo.chip(core)]):
+        dma("ysy"[i], [("YL", 512 * s, 512 * s + 512)], [], T.y[:, 512 * s:512 * s + 512], T.YL[:, 512 * s:512 * s + 512])
+    for sem in sorted(total):
+        if known["g"].get(sem, 0) < total[sem]:
+            g.wait_ge(T.sem[sem], total[sem])

@@ -1,31 +1,50 @@
 from concourse.bass import DstId, RemoteDMATransfer
-from concourse.mybir import dt, AluOpType, ActivationFunctionType
+from concourse.mybir import dt, AluOpType, ActivationFunctionType, AxisListType
 
 A = AluOpType
 AF = ActivationFunctionType
 L, NT, B, RO = 2048, 4, 384, 2
 K = 2 * B
 C = B // 2
-SLOT = 16
-EDGE = SLOT + 16 * 72
-TW = EDGE + NT * K
-MAGIC = 12582912.0
+N3 = 3 * B
+EDGE = L + N3
+CUT = L - 16
+TW = EDGE + K - CUT
+BASE, TURN, MASK = 72.0, 16.0, 8.0
+CODE = 96
+BIG = 4096.0
+RUN = N3 // 16
 PART = ((0, 64), (64, 128))
+SIZE, D3L, START, D3R, D2L, D2R, EVEN, ODD = 0, 1, 2, 3, 4, 6, 8, 9
+MATS = ["ZM", "Z1", "DM1", "DQZ", "DQS", "NR2", "NR3", "ST", "S3L", "S3R",
+        "X1L", "X1R", "WP2", "WN2", "WP3", "BI2", "BI3"]
+EARLY = 144 * 10
+U, BF, SS, VV, AT, AP = 0, 4, 8, 12, 16, 20
+WS, E0, LO, Z0, Z2, E2, HC, CR, RF, I0, HT, NB, A3, NCR, TS, TB, WF, WG, C1, BG, BH = range(24, 45)
 
 SCRATCH = {
-    "KI": ("sbuf", [128, 384], "int32"), "K16": ("sbuf", [128, 384], "uint16"),
-    "ZA": ("sbuf", [128, 384], "int32"), "ZB": ("sbuf", [128, 384], "int32"), "SG": ("sbuf", [128, 384], "uint16"),
-    "VAL": ("sbuf", [128, NT * K], "float32"), "ZZ": ("sbuf", [128, 256], "float32"),
-    "SZ": ("sbuf", [128, L + NT * B], "bfloat16"), "TAB": ("sbuf", [128, TW], "float32"),
-    "IDN": ("sbuf", [128, 128], "bfloat16"), "NID": ("sbuf", [128, 128], "bfloat16"),
+    "KI": ("sbuf", [128, 384], "int32"), "K16": ("sbuf", [128, 384], "uint16"), "KS": ("sbuf", [128, 384], "uint16"),
+    "PI": ("sbuf", [128, 8], "int32"), "CO": ("sbuf", [128, 48], "float32"),
+    "M0": ("sbuf", [128, EDGE + K], "float32"), "M1": ("sbuf", [128, EDGE], "float32"), "B72": ("sbuf", [128, 640], "float32"),
+    "MB": ("sbuf", [128, L], "float16"), "PRE": ("sbuf", [128, B], "float32"),
+    "STEP": ("sbuf", [128, B], "bfloat16"), "S0": ("sbuf", [128, RUN], "bfloat16"),
+    "NC": ("sbuf", [128, RUN], "float32"), "OWH": ("sbuf", [128, RUN], "float32"), "RL0": ("sbuf", [128, RUN], "float32"),
+    "TAB": ("sbuf", [128, TW], "float32"),
+    "MAT": ("sbuf", [128, 144 * len(MATS)], "bfloat16"), "ONE": ("sbuf", [128, 512], "bfloat16"),
+    "IDN": ("sbuf", [128, 128], "bfloat16"), "YM": ("sbuf", [128, 6 * 128], "bfloat16"),
     "BLA": ("sbuf", [128, 128], "bfloat16"), "BLK": ("sbuf", [128, 128], "bfloat16"), "TRI": ("sbuf", [128, 128], "bfloat16"),
-    "EQ": ("sbuf", [128, 2048], "bfloat16"), "DQ": ("sbuf", [128, 2048], "bfloat16"),
-    "C72": ("sbuf", [128, 16], "bfloat16"), "CI": ("sbuf", [128, 72], "float32"), "CT": ("sbuf", [128, 72], "float32"),
-    "CB": ("sbuf", [128, 128], "bfloat16"),
+    "BLS": ("sbuf", [128, 128], "bfloat16"), "EQ": ("sbuf", [128, 16 * 128], "bfloat16"),
+    "TRS": ("sbuf", [128, 128], "bfloat16"), "SGB": ("sbuf", [128, 128], "bfloat16"), "SD1": ("sbuf", [128, 128], "bfloat16"),
+    "CN": ("sbuf", [128, B], "bfloat16"), "OWN": ("sbuf", [128, RUN], "float32"),
     "MI": ("sbuf", [128, 256], "bfloat16"), "WI": ("sbuf", [128, 1], "bfloat16"), "MM": ("sbuf", [128, 256], "bfloat16"),
     "WP": ("sbuf", [128, 128], "bfloat16"), "WN": ("sbuf", [128, 128], "bfloat16"),
-    "F16": ("sbuf", [128, B], "float16"), "DX": ("sbuf", [128, NT * K], "float32"),
-    "UX": ("sbuf", [128, B], "float32"), "UB": ("sbuf", [128, K], "bfloat16"),
+    "WP1": ("sbuf", [128, 128], "bfloat16"), "WN1": ("sbuf", [128, 128], "bfloat16"),
+    "F16": ("sbuf", [128, B], "float16"), "SR": ("sbuf", [128, 2 * N3], "bfloat16"), "RG": ("sbuf", [128, N3], "bfloat16"),
+    "DG": ("sbuf", [128, B], "bfloat16"), "XS": ("sbuf", [128, B], "bfloat16"),
+    "XB2": ("sbuf", [128, B], "bfloat16"), "XB3": ("sbuf", [128, B], "float32"),
+    "F": ("sbuf", [128, RUN + 8], "bfloat16"), "RS": ("sbuf", [128, RUN], "bfloat16"), "OFS": ("sbuf", [128, 8], "float32"),
+    "INC": ("sbuf", [128, RUN + 8], "float16"), "RL1": ("sbuf", [128, RUN], "float16"), "IX": ("sbuf", [128, B], "float16"),
+    "FL": ("sbuf", [128, 128], "bfloat16"), "IL": ("sbuf", [128, 128], "float32"),
     "PR": ("sbuf", [128, 2048], "float16"), "QA": ("sbuf", [128, 128], "int32"), "QB": ("sbuf", [128, 128], "int32"),
     "QL": ("sbuf", [128, 128], "uint16"),
     "YL": ("sbuf", [128, L], "bfloat16"),
@@ -34,18 +53,14 @@ for _t in range(NT):
     SCRATCH["G%d" % _t] = ("sbuf", [128, K], "bfloat16")
 for _r in range(RO):
     SCRATCH.update({
-        "H%d" % _r: ("sbuf", [128, L + 3 * B], "bfloat16"),
-        "PW%d" % _r: ("sbuf", [128, 4096], "float32"), "PL%d" % _r: ("sbuf", [128, 256], "float32"),
-        "NA%d" % _r: ("sbuf", [128, 72], "float32"), "PT%d" % _r: ("sbuf", [128, 200], "uint16"),
-        "RS%d" % _r: ("sbuf", [128, 224], "bfloat16"), "INC%d" % _r: ("sbuf", [128, 224], "float32"),
-        "RL%d" % _r: ("sbuf", [128, 224], "float16"), "RM%d" % _r: ("sbuf", [128, 128], "float16"),
-        "SR%d" % _r: ("sbuf", [128, 3 * K], "bfloat16"), "WB%d" % _r: ("sbuf", [128, L], "bfloat16"),
+        "H%d" % _r: ("sbuf", [128, L + N3], "bfloat16"), "PT%d" % _r: ("sbuf", [128, 128], "uint16"),
+        "RM%d" % _r: ("sbuf", [128, 128], "float16"), "WB%d" % _r: ("sbuf", [128, L], "bfloat16"),
     })
 for _b in range(8):
     SCRATCH["b%d" % _b] = ("psum", [128, 512], "float32")
 PSUM = ["b%d" % i for i in range(8)]
 
-SEMAPHORES = ["qv", "qs", "qp", "qg", "sent", "arr0"] + ["arr1_%d" % i for i in range(4)] + ["d%d" % i for i in range(16)]
+SEMAPHORES = ["qv", "qs", "qp", "qg", "sent", "arr0"] + ["arr1_%d" % i for i in range(4)] + ["d%d" % i for i in range(24)]
 
 
 def rank_program(g, core, T, topo):
@@ -121,216 +136,309 @@ def rank_program(g, core, T, topo):
 
     V, S, P = g.vector, g.scalar, g.tensor
 
-    def ts(b_out, lo, hi, in_ap, reads, s1, s2, o0, o1=None):
-        o = T[b_out][:, lo:hi]
+    def ap(x):
+        if len(x) == 6:
+            return T[x[0]][:, x[1]:x[2]].indirect(T[x[3]][:, x[4]:x[5]])
+        return T[x[0]][:, x[1]:x[2]:x[3]] if len(x) == 4 else T[x[0]][:, x[1]:x[2]]
+
+    def use(*xs):
+        r = []
+        for x in xs:
+            if isinstance(x, tuple):
+                r.append(x[:3])
+                if len(x) == 6:
+                    r.append(x[3:])
+        return r
+
+    def outs(o):
+        return [o[:3]]
+
+    def ins(o, *xs):
+        return use(*xs) + ([o[3:]] if len(o) == 6 else [])
+
+    def val(x):
+        return ap(x) if isinstance(x, tuple) else x
+
+    def co(j, n=1):
+        return ("CO", j, j + n)
+
+    def ts(o, x, s1, o0, s2=None, o1=None):
         if o1 is None:
-            op("v", reads, [(b_out, lo, hi)], lambda: V.tensor_scalar(o, in_ap, s1, None, o0))
+            op("v", ins(o, x, s1), outs(o), lambda: V.tensor_scalar(ap(o), ap(x), val(s1), None, o0))
         else:
-            op("v", reads, [(b_out, lo, hi)], lambda: V.tensor_scalar(o, in_ap, s1, s2, o0, o1))
+            op("v", ins(o, x, s1, s2), outs(o), lambda: V.tensor_scalar(ap(o), ap(x), val(s1), val(s2), o0, o1))
 
-    def tt(b_out, lo, hi, a0, a1, reads, o0):
-        op("v", reads, [(b_out, lo, hi)], lambda: V.tensor_tensor(T[b_out][:, lo:hi], a0, a1, o0))
+    def tt(o, x, y, o0):
+        op("v", ins(o, x, y), outs(o), lambda: V.tensor_tensor(ap(o), ap(x), ap(y), o0))
 
-    def vcopy(b_out, lo, hi, in_ap, reads):
-        op("v", reads, [(b_out, lo, hi)], lambda: V.tensor_copy(T[b_out][:, lo:hi], in_ap))
+    def scan(o, x, y, init, o1=A.max):
+        op("v", use(x, y, init), outs(o), lambda: V.tensor_tensor_scan(ap(o), ap(x), ap(y), val(init), A.add, o1))
 
-    def fill(b, lo, hi, c):
-        op("v", [], [(b, lo, hi)], lambda: V.memset(T[b][:, lo:hi], c))
+    def reduce(o, x, o0, neg=False):
+        op("v", use(x), outs(o), lambda: V.tensor_reduce(ap(o), ap(x), AxisListType.X, o0, negate=neg))
 
-    def act(b_out, lo, hi, in_ap, reads, func, scale=None, bias=None):
-        o = T[b_out][:, lo:hi]
-        if bias is not None:
-            op("s", reads, [(b_out, lo, hi)], lambda: S.activation(o, in_ap, func, bias=bias, scale=scale))
-        elif scale is None:
-            op("s", reads, [(b_out, lo, hi)], lambda: S.activation(o, in_ap, func))
+    def fill(o, c):
+        op("v", [], outs(o), lambda: V.memset(ap(o), c))
+
+    def act(o, x, func, scale=1.0, bias=None):
+        if bias is None and scale == 1.0:
+            op("s", ins(o, x), outs(o), lambda: S.activation(ap(o), ap(x), func))
+        elif bias is None:
+            op("s", ins(o, x, scale), outs(o), lambda: S.activation(ap(o), ap(x), func, scale=val(scale)))
         else:
-            op("s", reads, [(b_out, lo, hi)], lambda: S.activation(o, in_ap, func, scale=scale))
+            op("s", ins(o, x, scale, bias), outs(o), lambda: S.activation(ap(o), ap(x), func, bias=val(bias), scale=val(scale)))
 
-    def copy(q, b_out, lo, hi, in_ap, reads):
+    def copy(q, o, x):
         if q == "v":
-            vcopy(b_out, lo, hi, in_ap, reads)
+            op("v", ins(o, x), outs(o), lambda: V.tensor_copy(ap(o), ap(x)))
         else:
-            act(b_out, lo, hi, in_ap, reads, AF.Copy)
+            act(o, x, AF.Copy)
 
-    def mm(bank, out_ap, lhs, lo, rhs_ap, reads, start, stop):
-        op("p", [(lhs, lo, lo + 128)] + reads, [bank], lambda: P.matmul(out_ap, T[lhs][:, lo:lo + 128], rhs_ap, start, stop))
-
-    def iota(b, lo, hi, pattern, base, cm, flag=True):
-        if flag:
-            op("g", [], [(b, lo, hi)], lambda: g.iota(T[b][:, lo:hi], pattern, base, cm, allow_small_or_imprecise_dtypes=True))
+    def lin(q, o, x, a, b=None):
+        if q == "s":
+            act(o, x, AF.Identity, a, b)
+        elif b is None:
+            ts(o, x, a, A.mult)
+        elif a == 1.0:
+            ts(o, x, b, A.add)
         else:
-            op("g", [], [(b, lo, hi)], lambda: g.iota(T[b][:, lo:hi], pattern, base, cm))
+            ts(o, x, a, A.mult, b, A.add)
 
-    def select(b_out, b_in, n, pattern, cmp, base, cm):
-        op("g", [(b_in, 0, n)], [(b_out, 0, n)], lambda: g.affine_select(T[b_out][:, 0:n], T[b_in][:, 0:n], pattern, cmp, 0.0, base, cm))
+    def relu(q, o, x, bias=None):
+        if q == "s":
+            act(o, x, AF.Relu, 1.0, bias)
+        elif bias is None:
+            ts(o, x, 0.0, A.max)
+        else:
+            ts(o, x, bias, A.add, 0.0, A.max)
+
+    def mm(o, lhs, x, start, stop):
+        op("p", use(lhs, x), outs(o), lambda: P.matmul(ap(o), ap(lhs), ap(x), start, stop))
+
+    def iota(o, pattern, base, cm):
+        if SCRATCH[o[0]][2] == "int32":
+            op("g", [], outs(o), lambda: g.iota(ap(o), pattern, base, cm))
+        else:
+            op("g", [], outs(o), lambda: g.iota(ap(o), pattern, base, cm, allow_small_or_imprecise_dtypes=True))
+
+    def select(o, x, pattern, cmp, c, base, cm):
+        op("g", use(x), outs(o), lambda: g.affine_select(ap(o), ap(x), pattern, cmp, c, base, cm))
+
+    def mat(name, to=15):
+        c = 144 * MATS.index(name) + 15 - to
+        return ("MAT", c, c + 128)
+
+    def paint(m, src, dst, c):
+        x = (m[0], m[1] + dst, m[1] + 128, 16)
+        select(x, x, [[-16, 8]], A.not_equal, c, -src, 1)
+
+    def column(m, row, c):
+        lin("s", (m[0], m[1] + row, m[1] + 128, 16), ("BLK", row, 128, 16), c)
+
+    def whole(b):
+        return (b, 0, SCRATCH[b][1][1])
+
+    def bank(b, n=B, lo=0):
+        return (b, lo, lo + n)
+
+    def kids(r, t, side, h=None, b="K16"):
+        c = 192 * r + 48 * t + 24 * side
+        return (b, c, c + 24) if h is None else (b, c + 12 * h, c + 12 * h + 12)
+
+    def node(b, t):
+        c = L + B * t - (CUT if b == "TAB" else 0)
+        return (b, c, c + B)
+
+    def edge(side):
+        return node("TAB", 3 + side)
+
+    def sr(t, side):
+        c = N3 * side + B * (t - 1)
+        return ("SR", c, c + B)
+
+    def rg(t):
+        return ("RG", B * (t - 1), B * t)
+
+    def vec(t, side):
+        return ("G%d" % t, B * side, B * side + B)
+
+    IDN, BLK, TRI, CN = whole("IDN"), whole("BLK"), whole("TRI"), whole("CN")
+
+    def ym(i):
+        return ("YM", 128 * i, 128 * i + 128)
+
+    def eq(q):
+        return ("EQ", 128 * q, 128 * q + 128)
 
     def lists(r):
-        lo, hi = 192 * r, 192 * r + 192
-        ki = T.KI[:, lo:hi]
-        ts("ZA", lo, hi, ki, [("KI", lo, hi)], 4097, None, A.mult)
-        vcopy("K16", lo, hi, ki, [("KI", lo, hi)])
-        ts("ZB", lo, hi, T.ZA[:, lo:hi], [("ZA", lo, hi)], 4, 4095, A.arith_shift_right, A.bitwise_and)
-        vcopy("SG", lo, hi, T.ZB[:, lo:hi], [("ZB", lo, hi)])
+        x = ("KI", 192 * r, 192 * r + 192)
+        copy("v", ("K16",) + x[1:], x)
 
-    def scat(r, t):
-        b, c = "PW%d" % r, 192 * r + 48 * t
-        op("s", [("SG", c, c + 48), ("VAL", K * t, K * t + K)], [b],
-           lambda: S.activation(T[b][:, :].indirect(T.SG[:, c:c + 48]), T.VAL[:, K * t:K * t + K], AF.Silu))
+    def tab_lists(r):
+        x = ("KI", 192 * r + 48, 192 * r + 192)
+        ts(("KS",) + x[1:], x, float(CUT), A.subtract)
 
-    def conv(r):
-        b, o = "PW%d" % r, "PL%d" % r
-        dma("y", [b], [o], T[o][:, :], T[b][0:128:16, :])
+    def own(t):
+        scan(node("M0", t), whole("STEP"), whole("STEP"), co(I0) if t == 0 else ("M0", L + B * t - 1, L + B * t))
 
-    def size_gather(r, t, q):
-        w, c, lo = L + B * t, 192 * r + 48 * t, K * (t - 1)
-        copy(q, "SR%d" % r, lo, lo + K, T.SZ[:, 0:w].indirect(T.K16[:, c:c + 48]), [("SZ", 0, w), ("K16", c, c + 48)])
+    def turn(r, t, q):
+        lin(q, whole("PRE"), node("M%d" % r, t), 1.0, co(AT + t))
 
-    def size_add(r, t):
-        sr, lo = "SR%d" % r, K * (t - 1)
-        for i in range(2):
-            c = lo + B * i
-            mm("b5", T.b5[:, 0:B], "IDN", 0, T[sr][:, c:c + B], [(sr, c, c + B)], i == 0, i == 1)
+    def hand(r, t, side, q):
+        m = "M%d" % r
+        x = node("M0", 3 + side) if t == 3 else whole("PRE") if side else node(m, t)
+        if q == "s":
+            act((m, 0, L + B * t) + kids(r, t, side), x, AF.Silu)
+        else:
+            copy(q, (m, 0, L + B * t) + kids(r, t, side), x)
 
-    def size_store(r, t, q):
-        copy(q, "SZ", L + B * t, L + B * t + B, T.b5[:, 0:B], ["b5"])
+    def narrow(r, k):
+        lo, hi = PART[k]
+        ts(("MB", 16 * lo, 16 * hi), ("M%d" % r, 16 * lo, 16 * hi), co(NB), A.add, 0.0, A.max)
 
-    def size_list(r):
+    def leaf_codes(b, k):
+        lo, hi = PART[k]
         for q in range(16):
-            mm("b6", T.b6[:, 0:96], "DQ", 128 * q, T.SZ[:, L + q:L + 4 * B:16], [("SZ", L, L + 4 * B)], q == 0, q == 15)
+            mm(bank(b, hi - lo, lo), mat("Z1", q), ("MB", 16 * lo + q, 16 * hi, 16), q == 0, q == 15)
 
-    def root_flags(r):
-        pl, rs = "PL%d" % r, "RS%d" % r
-        act(rs, 0, 224, T[pl][:, 0:224], [pl], AF.Relu, -1.0, 1.0)
+    def runs(t):
+        return [(q, max(B * t - RUN * q, 0), min(B * t + B - RUN * q, RUN), max(RUN * q - B * t, 0))
+                for q in range(B * t // RUN, -(-(B * t + B) // RUN))]
 
-    def root_sizes(r):
-        rs, na = "RS%d" % r, "NA%d" % r
-        tt(na, 0, 72, T[rs][:, 128:200], T.CT[:, :], [(rs, 128, 200), "CT"], A.mult)
-        tt(rs, 128, 224, T[rs][:, 128:224], T.b6[:, 0:96], [(rs, 128, 224), "b6"], A.mult)
+    def node_codes(r):
+        m = "M%d" % r
+        dma("y", [(m, L, EDGE)], ["NC"], T.NC[:, :], T[m][SIZE:128:16, L:EDGE])
 
-    def root_starts(r):
-        pl, rs, na, pt, inc, rl = ["%s%d" % (n, r) for n in ("PL", "RS", "NA", "PT", "INC", "RL")]
-        mm("b6", T.b6[:, 224:448], "BLK", 0, T[rs][:, :], [rs], True, True)
-        mm("b6", T.b6[:, 0:224], "TRI", 0, T[rs][:, :], [rs], True, True)
-        tt(pl, 128, 200, T[na][:, :], T[pl][:, 128:200], [na, (pl, 128, 200)], A.add)
-        op("v", ["b6", rs], [inc], lambda: V.tensor_tensor_scan(T[inc][:, :], T.b6[:, 224:448], T[rs][:, :], 0.0, A.add, A.max))
-        tt(rl, 0, 224, T[inc][:, :], T.b6[:, 0:224], [inc, "b6"], A.subtract)
-        ts(pt, 0, 200, T[pl][:, 0:200], [pl], 0.25, None, A.add)
+    def sizes(t):
+        for side in range(2):
+            mm(bank("b7"), mat("Z1", SIZE), sr(t, side), side == 0, side == 1)
 
-    def root_rows3(r):
-        rl = "RL%d" % r
-        for q in range(16):
-            mm("b6", T.b6[:, q:B:16], "EQ", 128 * q, T[rl][:, 200:224], [(rl, 200, 224)], True, True)
+    def node_sizes(t):
+        if t == 0:
+            for q, lo, hi, c in runs(0):
+                mm(bank("b6", hi), mat("Z1", q), ("S0", 0, hi), q == 0, False)
+            return
+        for side in range(2):
+            for q, lo, hi, c in runs(t):
+                c += sr(t, side)[1]
+                mm(bank("b6", hi - lo, lo), mat("DQZ", q), ("SR", c, c + hi - lo), False, side + q == 16)
 
-    def root_rows(r, es):
-        rl = "RL%d" % r
-        for bank, qs, e in (("b5", range(0, 6), es[0]), ("b4", range(6, 12), es[1]), ("b2", range(12, 16), es[2])):
-            for i, q in enumerate(qs):
-                mm(bank, T[bank][:, 72 * i:72 * i + 72], "EQ", 128 * q, T[rl][:, 128:200], [(rl, 128, 200)], True, True)
-            c = SLOT + 72 * qs[0]
-            copy(e, "TAB", c, c + 72 * len(qs), T[bank][:, 0:72 * len(qs)], [bank])
-            if bank == "b5":
-                root_rows3(r)
+    def node_flags():
+        tt(("F", 0, RUN), whole("NC"), whole("OWH"), A.is_lt)
+        mm(bank("b5", RUN + 1), BLK, ("F", 0, RUN + 1), True, True)
 
-    def root_leaves(r):
-        rl, rs = "RL%d" % r, "RS%d" % r
-        tt("RM%d" % r, 0, 128, T[rl][:, 0:128], T[rs][:, 0:128], [(rl, 0, 128), (rs, 0, 128)], A.mult)
+    def root_leaves():
+        reduce(("OFS", 0, 1), bank("b5", RUN + 1), A.add, True)
 
-    def bias():
-        for b in ("b0", "b1"):
-            mm(b, T[b][:, 0:C], "CB", 0, T.SZ[:, 0:C], [("SZ", 0, C)], True, False)
+    def root_sizes():
+        tt(whole("RS"), ("F", 0, RUN), bank("b6", RUN), A.mult)
+
+    def run_sums():
+        scan(("INC", 1, RUN + 1), whole("RS"), whole("RS"), 0.0)
+        mm(bank("b6", 1, 300), whole("TRS"), ("INC", RUN, RUN + 1), True, True)
+        mm(bank("b6", 1, 301), BLK, ("INC", RUN, RUN + 1), True, True)
+
+    def node_starts(r):
+        ts(whole("RL%d" % r), ("INC", 0, RUN), bank("b6", 1, 300), A.add, ("OFS", 0, 1), A.add)
+        ts(("OFS", 1, 2), bank("b6", 1, 301), ("OFS", 0, 1), A.add, -1.0 if r else 1 / 256, A.mult)
+
+    def start_rows(b, t):
+        for q, lo, hi, c in runs(t):
+            mm(bank(b, hi - lo, c), eq(q), ("RL1", lo, hi), False, False)
+
+    def leaf_list(r, b, k):
+        lo, hi = PART[k]
+        ts(("PT%d" % r, lo, hi), bank(b, hi - lo, lo), float(CODE), A.subtract)
+
+    def leaf_flag(b, lo, hi):
+        ts(("FL", lo, hi), bank(b, hi - lo, lo), float(CODE), A.is_lt)
+
+    def leaf_flags(b, done=0):
+        leaf_flag(b, done, 128)
+        mm(bank(b, 128, 128), BLK, whole("FL"), True, True)
+        mm(bank(b, 128, 256), TRI, whole("FL"), True, True)
+
+    def leaf_starts(r, b, step):
+        if step == 0:
+            scan(whole("IL"), bank(b, 128, 128), whole("FL"), 0.0)
+        elif step == 1:
+            tt(whole("IL"), whole("IL"), bank(b, 128, 256), A.subtract)
+        else:
+            tt(whole("RM%d" % r), whole("IL"), whole("FL"), A.mult)
 
     def gather(r, t, side, h, q):
-        hb, w, c, o = "H%d" % r, L + B * t, 192 * r + 48 * t + 24 * side + 12 * h, B * side + C * h
-        copy(q, "G%d" % t, o, o + C, T[hb][:, 0:w].indirect(T.K16[:, c:c + 12]), [(hb, 0, w), ("K16", c, c + 12)])
+        o = B * side + C * h
+        x = ("H%d" % r, 0, L + B * t) + kids(r, t, side, h)
+        if q == "d":
+            tt(("G%d" % t, o, o + C), x, ("G%d" % t, o - B, o - B + C), A.subtract)
+        else:
+            copy(q, ("G%d" % t, o, o + C), x)
 
-    def sums(t):
-        gb = "G%d" % t
-        for h, b in enumerate(("b0", "b1")):
-            for side in range(2):
-                o = B * side + C * h
-                mm(b, T[b][:, 0:C], "MM", 128 * side, T[gb][:, o:o + C], [(gb, o, o + C)], False, side == 1)
+    def rows(r, t, side, q, o=None):
+        copy(q, o or sr(t, side), ("TAB", 0, L + B * t - CUT) + kids(r, t, side, None, "KS"))
 
-    def dbank(t):
-        return ("b2", "b7", "b4", "b0")[t]
+    def sums(t, h):
+        for side in range(2):
+            o = B * side + C * h
+            mm(bank("b%d" % h, C), ("MM", 128 * side, 128 * side + 128), ("G%d" % t, o, o + C), side == 0, side == 1)
 
-    def rbank(t):
-        return ("b3", "b3", "b1", "b3")[t]
+    def diff(t, b, start=True):
+        mm(bank(b), whole("WN"), vec(t, 0), start, False)
+        mm(bank(b), whole("WP"), vec(t, 1), False, True)
 
-    def diff(t):
-        b, gb = dbank(t), "G%d" % t
-        mm(b, T[b][:, 0:B], "WN", 0, T[gb][:, 0:B], [(gb, 0, B)], True, False)
-        mm(b, T[b][:, 0:B], "WP", 0, T[gb][:, B:K], [(gb, B, K)], False, True)
+    def floor(h):
+        ts(("F16", C * h, C * h + C), bank("b%d" % h, C), 1536 - 0.375, A.add, 1536.0 - 127, A.max)
 
-    def vectors(r, t):
-        for h, b in enumerate(("b0", "b1")):
-            ts("F16", C * h, C * h + C, T[b][:, 0:C], [b], -127.0, 127.0, A.max, A.min)
-        for h in range(2):
-            lo = L + B * t + C * h
-            ts("H%d" % r, lo, lo + C, T.F16[:, C * h:C * h + C], [("F16", C * h, C * h + C)], MAGIC, MAGIC, A.add, A.subtract)
+    def clamp(r, t, h):
+        lo = L + B * t + C * h
+        ts(("H%d" % r, lo, lo + C), ("F16", C * h, C * h + C), 1536.0 + 127, A.min, 1536.0, A.subtract)
 
-    def moves0_a():
-        act("UX", 0, B, T.b2[:, 0:B], ["b2"], AF.Relu, -1.0, 1.0)
+    def tie_break():
+        mm(bank("b2"), whole("SGB"), CN, True, False)
 
-    def moves0_b():
-        act("DX", 0, B, T.UX[:, 0:B], [("UX", 0, B)], AF.Relu, -1.0, 1.0)
-        act("DX", B, K, T.DX[:, 0:B], [("DX", 0, B)], AF.Relu, -1.0, 1.0)
+    def store0():
+        ts(node("TAB", 0), bank("b2"), co(LO), A.max, co(HC), A.min)
 
-    def moves1_w():
-        for bank, idn, o in (("b7", "NID", B), ("b5", "IDN", 0)):
-            mm(bank, T[bank][:, 0:B], idn, 0, T.SR1[:, o:o + B], [("SR1", o, o + B)], True, False)
+    def others1(b):
+        mm(bank(b), mat("Z1", EVEN), sr(1, 0), True, False)
+        mm(bank(b), mat("Z1", ODD), sr(1, 1), False, True)
 
-    def moves1_x(i):
-        bank = ("b7", "b5")[i]
-        mm(bank, T[bank][:, 0:B], "WN", 0, T.G1[:, 0:B], [("G1", 0, B)], False, False)
-        mm(bank, T[bank][:, 0:B], "WP", 0, T.G1[:, B:K], [("G1", B, K)], False, True)
+    def pick(t, b, start, stop=False, y=0):
+        for side in range(2):
+            mm(bank(b), ym(2 * (t - 1) + y + side), sr(t, side), start and side == 0, stop and side == 1)
 
-    def moves1_y():
-        act("UB", 0, B, T.b7[:, 0:B], ["b7"], AF.Relu, -1.0)
-        act("UB", B, K, T.b5[:, 0:B], ["b5"], AF.Relu, 1.0, -16.0)
+    def edge_sizes(b, stop):
+        for side in range(2):
+            mm(bank(b), mat(("S3L", "S3R")[side]), sr(3, side), side == 0, stop and side == 1)
 
-    def moves1_z():
-        for i, bank, o in ((0, "b7", B), (1, "b5", 0)):
-            mm(bank, T[bank][:, 0:B], "IDN", 0, T.SR1[:, o:o + B], [("SR1", o, o + B)], True, False)
-            mm(bank, T[bank][:, 0:B], "NID", 0, T.UB[:, B * i:B * i + B], [("UB", B * i, B * i + B)], False, True)
-            act("DX", K + B * i, K + B * i + B, T[bank][:, 0:B], [bank], AF.Relu)
+    def edge_sums(r):
+        if r == 0:
+            scan(whole("IX"), sr(3, 0), sr(3, 1), ("OFS", 1, 2), A.add)
+        else:
+            scan(whole("IX"), bank("b0"), ("ONE", 0, B), ("OFS", 1, 2), A.min)
 
-    def relus(t):
-        b, rb = dbank(t), rbank(t)
-        act(rb, 0, B, T[b][:, 0:B], [b], AF.Relu, -1.0, 16.0)
-        act(b, 0, B, T[b][:, 0:B], [b], AF.Relu)
+    def edge_starts(r):
+        mm(bank("b5"), mat("ST") if r else mat("DQZ", START), whole("IX"), False, r == 1)
 
-    def mins(r, t):
-        sr, o = "SR%d" % r, K * (t - 1)
-        for i, b in ((1, rbank(t)), (0, dbank(t))):
-            c = o + B - B * i
-            tt("DX", K * t + B * i, K * t + B * i + B, T[b][:, 0:B], T[sr][:, c:c + B], [b, (sr, c, c + B)], A.min)
+    def edge_store(side, b):
+        tt(edge(side), edge(side), bank(b), A.max)
 
-    def down(r):
-        tab = "TAB"
-        pt, h, wb, rm = ["%s%d" % (n, r) for n in ("PT", "H", "WB", "RM")]
-        for i in (1, 0):
-            d = K * 3 + B * i
-            tt(tab, EDGE + B * i, EDGE + B * i + B, T.b6[:, 0:B], T.DX[:, d:d + B], ["b6", ("DX", d, d + B)], A.add)
-        for t in (2, 1, 0):
-            w = EDGE + K * (3 - t)
-            c = 128 + 24 * t
-            for i in range(2):
-                d = K * t + B * i
-                tt(tab, w + B * i, w + B * i + B, T[tab][:, 0:w].indirect(T[pt][:, c:c + 24]), T.DX[:, d:d + B],
-                   [(tab, 0, w), (pt, c, c + 24), ("DX", d, d + B)], A.add)
-        for k, (lo, hi) in enumerate(PART):
-            vcopy("PR", 16 * lo, 16 * hi, T[tab][:, :].indirect(T[pt][:, lo:hi]), [tab, (pt, lo, hi)])
-            b = "b%d" % (4 + k)
-            mm(b, T[b][:, 0:hi - lo], "IDN", 0, T[rm][:, lo:hi], [(rm, lo, hi)], True, False)
-            for q in range(16):
-                mm(b, T[b][:, 0:hi - lo], "DQ", 128 * q, T.PR[:, 16 * lo + q:16 * hi:16], [("PR", 16 * lo, 16 * hi)], False, q == 15)
-        for k, (lo, hi) in enumerate(PART):
-            b = "b%d" % (4 + k)
-            ts("QA", lo, hi, T[b][:, 0:hi - lo], [b], 2049.0, None, A.mult)
-            ts("QB", lo, hi, T.QA[:, lo:hi], [("QA", lo, hi)], 2, 2047, A.arith_shift_right, A.bitwise_and)
-            vcopy("QL", lo, hi, T.QB[:, lo:hi], [("QB", lo, hi)])
-            op("v", [("QL", lo, hi), (h, 16 * lo, 16 * hi)], [wb],
-               lambda: V.tensor_copy(T[wb][:, :].indirect(T.QL[:, lo:hi]), T[h][:, 16 * lo:16 * hi]))
+    def sum_up(r, k):
+        lo, hi = PART[k]
+        tt(("PR", 16 * lo, 16 * hi), ("TAB", 0, TW, "PT%d" % r, lo, hi), ("MB", 16 * lo, 16 * hi), A.mult)
+        for q in range(16):
+            mm(bank("b%d" % k, hi - lo), mat("DQS", q), ("PR", 16 * lo + q, 16 * hi, 16), q == 0, False)
+
+    def add_roots(r, k):
+        lo, hi = PART[k]
+        mm(bank("b%d" % k, hi - lo), IDN, ("RM%d" % r, lo, hi), False, True)
+
+    def places(r, k):
+        lo, hi = PART[k]
+        ts(("QA", lo, hi), bank("b%d" % k, hi - lo), 2049.0, A.mult)
+        ts(("QB", lo, hi), ("QA", lo, hi), 2, A.arith_shift_right, 2047, A.bitwise_and)
+        copy("v", ("QL", lo, hi), ("QB", lo, hi))
+        copy("v", ("WB%d" % r, 0, L, "QL", lo, hi), ("H%d" % r, 16 * lo, 16 * hi))
 
     def plan(src):
         s = cores[src]
@@ -366,146 +474,362 @@ def rank_program(g, core, T, topo):
             total[sem] = n
             acc.setdefault(dst, []).append(("w", 512 * s, 512 * s + 512, "x", sem, n, {}))
         if r == 0:
-            vcopy(dst, 512 * me, 512 * me + 512, T[wb][:, 512 * me:512 * me + 512], [wb])
+            dma("y", [wb], [(dst, 512 * me, 512 * me + 512)], T[dst][:, 512 * me:512 * me + 512], T[wb][:, 512 * me:512 * me + 512])
 
     dma("y", [], [("KI", 0, 192)], T.KI[:, 0:192], T.kids[:, 0:192])
-    dma("s", [], [("H0", 0, L)], T.H0[:, 0:L], T.x[:, :])
+    dma("y", [], [("H0", 0, L)], T.H0[:, 0:L], T.x[:, :])
     dma("y", [], [("MI", 0, 128)], T.MI[:, 0:128], T.ml[:, :])
     dma("y", [], [("MI", 128, 256)], T.MI[:, 128:256], T.mr[:, :])
     dma("y", [], ["WI"], T.WI[:, :], T.w[:, :])
     dma("y", [], [("KI", 192, 384)], T.KI[:, 192:384], T.kids[:, 192:384])
 
-    def val(t):
-        iota("VAL", K * t, K * t + K, [[1, K]], EDGE + K * (3 - t), 0)
+    R = ("PI", 5, 6)
+    ones = ("ONE", 0, 128)
+    fill(whole("ONE"), 1.0)
+    iota(("PI", 0, 1), [[0, 1]], 0, 1)
+    iota(whole("S0"), [[0, RUN]], 2, 0)
+    select(whole("BLA"), ones, [[-16, 8], [0, 16]], A.is_ge, 0.0, 0, 1)
+    select(BLK, whole("BLA"), [[16, 8], [0, 16]], A.is_ge, 0.0, 15, -1)
+    select(whole("BLS"), BLK, [[0, 8], [1, 16]], A.is_ge, 0.0, -EVEN, 0)
+    select(IDN, ones, [[-1, 128]], A.is_equal, 0.0, 0, 1)
+    iota(whole("OWN"), [[1, RUN]], 16 + CODE, 0)
+    iota(whole("B72"), [[0, 640]], int(BASE), 0)
+    iota(("MAT", 0, EARLY), [[0, EARLY]], 0, 0)
+    paint(mat("Z1"), SIZE, 15, 1.0)
+    for i, (pattern, base) in enumerate((([[0, 8], [1, 4], [0, 4]], -2), ([[0, 8], [1, 4], [0, 4]], -3),
+                                         ([[0, 32], [1, 2], [0, 2]], 0), ([[0, 32], [1, 2], [0, 2]], -1))):
+        select(ym(i), IDN, pattern, A.is_equal, 0.0, base, 0)
+        if i != 2:
+            paint(ym(i), SIZE, SIZE, 1.0)
+    select(mat("DM1"), mat("DM1"), [[-16, 8], [1, 4], [0, 4]], A.not_equal, 1.0, -11, 1)
+    paint(mat("DQZ"), SIZE, 15, 256.0)
+    paint(ym(2), SIZE, D2R, 1.0)
+    paint(ym(3), START, START, 0.0)
+    paint(ym(3), SIZE, D2L, 1.0)
+    paint(mat("NR2"), EVEN, D2L, -1.0)
+    paint(mat("NR2"), ODD, D2R, -1.0)
+    iota(("F", RUN, RUN + 8), [[0, 8]], -8, 0)
+    select(whole("TRS"), BLK, [[1, 128]], A.is_gt, 0.0, 0, -1)
+    for m, row in (("S3L", D3R), ("S3R", D3L)):
+        paint(mat(m), SIZE, row, 1.0)
+        paint(mat(m), SIZE, START, -256.0)
+    paint(mat("ST"), START, START, -1.0)
+    paint(mat("NR3"), EVEN, D3L, -1.0)
+    paint(mat("NR3"), ODD, D3R, -1.0)
+    select(TRI, BLK, [[-1, 128]], A.is_ge, 0.0, 0, 1)
+    iota(("MAT", EARLY, 144 * len(MATS)), [[0, 144 * len(MATS) - EARLY]], 0, 0)
+    select(mat("X1L"), mat("X1L"), [[-16, 8], [1000, 4], [0, 4]], A.not_equal, 1.0, -3000, 1)
+    select(mat("X1R"), mat("X1R"), [[-16, 8], [1000, 4], [0, 4]], A.not_equal, 1.0, -2000, 1)
+    paint(mat("BI2"), SIZE, D2R, -1.0)
+    iota(whole("EQ"), [[0, 16 * 128]], 0, 0)
+    select(("EQ", START, 16 * 128, 16), ("EQ", START, 16 * 128, 16), [[-1, 16], [-16, 8]], A.not_equal, 1.0, 0, 1)
+    select(mat("BI3"), mat("BI3"), [[-16, 8], [0, 16]], A.not_equal, -32 * BIG, 0, 1)
+    paint(mat("BI3"), SIZE, D3L, 0.0)
+    paint(mat("BI3"), SIZE, D3R, -1.0)
+    select(ym(4), IDN, [[0, 32], [1, 2], [0, 2]], A.is_equal, 0.0, 0, 0)
+    select(ym(5), IDN, [[0, 32], [1, 2], [0, 2]], A.is_equal, 0.0, -1, 0)
+    paint(ym(5), START, START, 0.0)
 
-    fill("ZZ", 0, 256, 0.0)
-    for r in range(RO):
-        dma("sy"[r], ["ZZ"], ["PW%d" % r], T["PW%d" % r][0:128:16, :], T.ZZ[:, :])
-    fill("SZ", 0, L, 1.0)
-    act("TAB", 0, 16, T.SZ[:, 0:16], [("SZ", 0, 16)], AF.Silu, 0.0)
-    val(0)
-    select("BLA", "SZ", 128, [[-16, 8], [0, 16]], A.is_ge, 0, 1)
-    select("BLK", "BLA", 128, [[16, 8], [0, 16]], A.is_ge, 15, -1)
-    val(1)
-    select("IDN", "SZ", 128, [[-1, 128]], A.is_equal, 0, 1)
-    val(2)
-    val(3)
-    select("DQ", "SZ", 2048, [[-1024, 16], [-16, 8], [1023, 16]], A.is_equal, 0, 1)
-    select("TRI", "BLK", 128, [[-1, 128]], A.is_ge, 0, 1)
-    iota("C72", 0, 16, [[0, 16]], 72, 0)
-    iota("CI", 0, 72, [[1, 72]], SLOT + 16 * 72, 0)
-    select("EQ", "SZ", 2048, [[-1, 16], [-16, 8], [0, 16]], A.is_equal, 0, 1)
-    fill("SZ", L, L + B, 2.0)
-    fill("CB", 0, 128, -0.375 / 128)
+    for j, bit in enumerate((0, 2, 1, 3)):
+        ts(("PI", 1 + j, 2 + j), ("PI", 0, 1), bit, A.arith_shift_right, 1, A.bitwise_and)
+    ts(R, ("PI", 0, 1), 15, A.bitwise_and)
+    ts(("PI", 6, 7), ("PI", 0, 1), 13, A.bitwise_and)
+    copy("v", co(BF, 4), ("PI", 1, 5))
+    ts(co(E0), R, float(SIZE), A.is_equal)
+    fill(CN, -1 / 32)
+    ts(whole("STEP"), ("ONE", 0, B), co(E0), A.mult)
+    ts(co(I0), co(E0), CODE + 15 - BASE, A.mult, BASE, A.add)
+    ts(co(SS + 3), ("PI", 6, 7), 1.0, A.is_equal, TURN, A.mult)
+    act(("M0", 0, 512), whole("ONE"), AF.Silu, BASE)
+    tt(co(SS + 2), co(BF + 3), co(BF + 1), A.max)
+    own(0)
+    lin("s", ("M0", 1536, 2048), whole("ONE"), BASE)
+    ts(co(U, 4), ("PI", 1, 5), 2.0, A.mult, -1.0, A.add)
+    lin("s", ("M0", 512, 1024), whole("ONE"), BASE)
+    lin("s", co(SS, 2), co(BF, 2), 0.0, co(BF + 3))
+    ts(co(RF), R, float(RUN), A.mult)
+    own(1)
+    lin("s", co(AT + 3), co(SS + 3), co(U + 2))
     lists(0)
-    ts("MM", 0, 256, T.MI[:, :], ["MI"], 0.25, None, A.mult)
-    ts("WP", 0, 128, T.BLK[:, :], ["BLK", "WI"], T.WI[:, 0:1], 16.0, A.mult, A.mult)
-    ts("WN", 0, 128, T.BLK[:, :], ["BLK", "WI"], T.WI[:, 0:1], -16.0, A.mult, A.mult)
+    own(2)
+    lin("v", ("SGB", 0, 128, 2), ("BLS", 0, 128, 2), -1 / 16)
+    lin("s", ("M0", 1024, 1536), whole("ONE"), BASE)
+    own(3)
+    lin("s", ("SGB", 1, 128, 2), ("BLS", 1, 128, 2), 1 / 16)
+
+    hand(0, 3, 0, "s")
+    lin("v", co(A3), co(E0), float(B), co(AT + 3))
+    lin("s", co(LO), co(E0), 2 / 256)
+    ts(co(E2), R, float(START), A.is_equal, BIG, A.mult)
+    ts(whole("OWH"), whole("OWN"), co(RF), A.add, 0.5, A.add)
+    tt(co(VV, 3), co(SS, 3), co(U, 3), A.mult)
+    lin("v", node("M0", 4), node("M0", 3), 1.0, co(A3))
+    tab_lists(0)
+    tie_break()
+    hand(0, 3, 1, "s")
+    lin("s", co(HT), co(BF + 3), 1 / 256, co(LO))
+    ts(co(Z0), R, float(SIZE), A.not_equal)
+    lin("s", co(CR), co(U), -1 / 32)
+    gather(0, 0, 0, 0, "v")
+    gather(0, 0, 0, 1, "v")
+    lin("v", whole("MM"), whole("MI"), 0.25)
+    gather(0, 0, 1, 0, "v")
+    sums(0, 0)
+    lin("s", co(AT + 1, 2), co(VV + 1, 2), TURN)
+    lin("s", co(AT), co(VV), -TURN)
+    lin("s", co(HC), co(HT), 1.0, co(E2))
+    ts(whole("WP"), whole("SGB"), whole("WI"), A.mult)
+    gather(0, 0, 1, 1, "v")
+    lin("s", ("TAB", 0, 16), ("STEP", 0, 16), 1 / 256)
+    ts(co(Z2), R, float(START), A.not_equal, 256 / MASK, A.mult)
+    lin("v", whole("WN"), whole("WP"), -1.0)
+    sums(0, 1)
+    turn(0, 2, "s")
+    lin("s", whole("OWN"), whole("OWN"), 1.0, co(RF))
+    floor(0)
+    floor(1)
+    diff(0, "b2", False)
+    clamp(0, 0, 0)
+    node_sizes(0)
+    clamp(0, 0, 1)
+    gather(0, 1, 0, 0, "s")
+    hand(0, 2, 0, "v")
+    gather(0, 1, 0, 1, "v")
+    gather(0, 1, 1, 0, "s")
+    gather(0, 1, 1, 1, "s")
+    store0()
+    sums(1, 0)
+    floor(0)
+    hand(0, 2, 1, "s")
+    rows(0, 1, 0, "v")
+    sums(1, 1)
+    floor(1)
+    diff(1, "b7")
+    rows(0, 1, 1, "s")
+    clamp(0, 1, 0)
+    lin("s", co(WG), whole("WI"), -1 / 16)
+    relu("s", rg(1), bank("b7"), co(CR))
+    clamp(0, 1, 1)
+    others1("b2")
+    pick(1, "b3", True)
+    hand(0, 1, 0, "v")
+    relu("s", co(AP, 4), co(AT, 4))
+    tt(whole("DG"), rg(1), bank("b2"), A.min)
+    mm(bank("b3"), mat("DM1"), whole("DG"), False, True)
+    turn(0, 1, "s")
+    gather(0, 2, 1, 0, "v")
+    gather(0, 2, 0, 0, "s")
+    hand(0, 1, 1, "s")
+    gather(0, 2, 0, 1, "v")
+    gather(0, 2, 1, 1, "v")
+    ts(("INC", 0, 1), co(E0), 0.0, A.mult)
+    copy("s", node("TAB", 1), bank("b3"))
+    ts(co(WS), co(Z2), 1 / MASK, A.max, co(Z0), A.mult)
+    reduce(co(TS), co(AP, 4), A.add)
+    sums(2, 0)
+    turn(0, 0, "s")
+    rows(0, 2, 0, "s")
+    for c in range(0, EDGE, 640):
+        dma("y", ["B72"], [("M1", c, c + 640)], T.M1[:, c:c + 640], T.B72[:, :])
+    sums(2, 1)
+    floor(0)
+    diff(2, "b7")
+    rows(0, 2, 1, "s")
+    node_sizes(1)
+    floor(1)
+    relu("s", rg(2), bank("b7"), co(CR))
+    pick(2, "b4", True)
+    node_codes(0)
+    clamp(0, 2, 0)
+    hand(0, 0, 0, "v")
+    lin("s", co(TB), co(TS), -1.0, MASK - BASE)
+    clamp(0, 2, 1)
+    mm(bank("b4"), mat("NR2"), rg(2), False, True)
+    node_sizes(2)
+    gather(0, 3, 1, 0, "s")
+    hand(0, 0, 1, "v")
+    node_flags()
+    relu("s", node("TAB", 2), bank("b4"))
+    gather(0, 3, 0, 1, "v")
+    gather(0, 3, 1, 1, "v")
+    lin("v", co(NB), co(TB), co(Z0))
+    gather(0, 3, 0, 0, "s")
+    rows(0, 3, 0, "s")
+    root_sizes()
+    root_leaves()
+    diff(3, "b7")
+    run_sums()
+    narrow(0, 0)
+    node_starts(0)
+    dma("y", ["OWN"], [("M1", L, EDGE)], T.M1[SIZE:128:16, L:EDGE], T.OWN[:, :])
+    rows(0, 3, 1, "s")
+    edge_sizes("b5", False)
     lists(1)
+    rows(0, 3, 1, "s", edge(1))
+    rows(0, 3, 0, "s", edge(0))
+    dma("y", ["RL0"], [("TAB", 16, 16 + N3)], T.TAB[START:128:16, 16:16 + N3], T.RL0[:, :])
+    edge_sums(0)
+    column(mat("DQS"), 15, co(WS))
+    narrow(0, 1)
+    relu("s", rg(3), bank("b7"), co(CR))
+    tab_lists(1)
+    leaf_codes("b2", 0)
+    edge_starts(0)
+    hand(1, 3, 0, "s")
+    mm(bank("b5"), mat("NR3"), rg(3), False, True)
+    ts(co(BH), R, float(D2L), A.not_equal, BIG, A.mult)
+    edge_store(0, "b5")
+    ts(co(BG), R, float(D2R), A.not_equal, co(BH), A.mult)
+    lin("v", whole("SD1"), IDN, co(VV + 1))
+    leaf_codes("b4", 1)
+    edge_store(1, "b5")
+    leaf_list(0, "b2", 0)
+    leaf_list(0, "b4", 1)
+    node_sizes(0)
+    mm(bank("b3"), mat("ZM"), CN, True, False)
+    lin("s", co(NCR), co(U + 1), -1 / 32)
+    leaf_flag("b2", 0, 64)
+    leaf_flags("b4", 64)
 
-    for t in range(4):
-        scat(0, t)
-    conv(0)
-
-    def up0(t, q):
-        for h in range(2):
-            gather(0, t, 0, h, q)
-            gather(0, t, 1, h, q)
-        if t < 3:
-            sums(t)
-
-    bias()
-    up0(0, "v")
-    diff(0)
-    vectors(0, 0)
-    bias()
-    size_gather(0, 1, "v")
-    size_add(0, 1)
-    up0(1, "v")
-    size_store(0, 1, "v")
-    diff(1)
-    vectors(0, 1)
-    bias()
-    size_gather(0, 2, "v")
-    size_add(0, 2)
-    relus(1)
-    up0(2, "v")
-    size_store(0, 2, "v")
-    diff(2)
-    vectors(0, 2)
-    mm("b6", T.b6[:, 0:16], "TRI", 0, T.C72[:, :], ["C72"], True, True)
-    size_gather(0, 3, "v")
-    size_add(0, 3)
-    op("v", ["CI", "b6"], ["CT"], lambda: V.tensor_scalar(T.CT[:, :], T.CI[:, :], T.b6[:, 0:1], None, A.subtract))
-    mins(0, 1)
-    size_store(0, 3, "v")
-    relus(2)
-    mins(0, 2)
-    up0(3, "s")
-    size_list(0)
-    diff(3)
-    root_flags(0)
-    relus(3)
-    moves0_a()
-    root_sizes(0)
-    root_starts(0)
-    mins(0, 3)
-    moves0_b()
-    root_rows(0, "sss")
-    root_leaves(0)
-    size_gather(1, 1, "s")
-    scat(1, 0)
-    size_add(1, 1)
-    size_store(1, 1, "s")
-    size_gather(1, 2, "s")
-    scat(1, 1)
-    scat(1, 2)
-    scat(1, 3)
-    conv(1)
-    down(0)
-    size_add(1, 2)
-    size_store(1, 2, "s")
-    size_gather(1, 3, "s")
-    size_add(1, 3)
-    size_store(1, 3, "s")
+    sum_up(0, 0)
+    hand(1, 3, 1, "s")
+    leaf_starts(0, "b4", 0)
+    rows(1, 1, 0, "s")
+    turn(1, 2, "s")
+    hand(1, 2, 0, "s")
+    leaf_starts(0, "b4", 1)
+    leaf_starts(0, "b4", 2)
+    lin("s", co(WF), whole("WI"), 1 / 16)
+    hand(1, 2, 1, "s")
+    mm(bank("b4", 128), BLK, whole("SD1"), True, True)
+    rows(1, 1, 1, "s")
+    add_roots(0, 0)
+    lin("s", whole("WP1"), bank("b4", 128), co(WG))
+    hand(1, 1, 0, "s")
+    sizes(1)
+    sum_up(0, 1)
+    mm(bank("b2"), mat("X1L"), sr(1, 0), True, False)
+    add_roots(0, 1)
+    lin("s", whole("WN1"), bank("b4", 128), co(WF))
+    copy("s", node("TAB", 1), bank("b7"))
+    places(0, 0)
+    turn(1, 1, "s")
+    rows(1, 2, 0, "s")
+    node_sizes(1)
+    hand(1, 1, 1, "s")
+    places(0, 1)
+    rows(1, 2, 1, "s")
+    mm(bank("b4"), mat("Z1", D2R), sr(2, 0), True, False)
+    node_sizes(2)
+    node_codes(1)
     exchange(0)
-    size_list(1)
-    root_flags(1)
-    root_sizes(1)
-    root_starts(1)
-    bias()
-    root_rows(1, "svs")
-    root_leaves(1)
-    act("NID", 0, 128, T.IDN[:, :], ["IDN"], AF.Copy, -1.0)
-    moves1_w()
+    hand(1, 0, 0, "s")
+    sizes(2)
+    mm(bank("b4"), mat("Z1", D2L), sr(2, 1), False, True)
+    node_flags()
+    mm(bank("b2"), mat("X1R"), sr(1, 1), False, True)
+    copy("v", node("TAB", 2), bank("b7"))
+    turn(1, 0, "s")
+    lin("s", whole("XB2"), bank("b4"), 1.0, co(BG))
+    mm(bank("b4"), mat("BI2"), CN, True, False)
+    hand(1, 0, 1, "s")
+    root_sizes()
+    rows(1, 3, 0, "v")
+    run_sums()
+    root_leaves()
+    rows(1, 3, 1, "v")
+    column(mat("WN2"), D2L, co(WG))
+    node_starts(1)
+    edge_sizes("b0", True)
+    edge_sizes("b5", False)
+    narrow(1, 0)
+    lin("s", whole("XS"), bank("b2"), 1.0, co(NCR))
+    narrow(1, 1)
+    edge_sums(1)
+    start_rows("b3", 1)
+    start_rows("b4", 2)
+    lin("v", co(C1), co(U + 1), 1 / 32)
+    column(mat("WP2"), D2L, co(WF))
+    tie_break()
+    leaf_codes("b6", 0)
+    leaf_codes("b6", 1)
+    edge_starts(1)
 
-    for t in range(NT):
-        for h in range(2):
-            gather(1, t, 0, h, "v")
-            gather(1, t, 1, h, "s")
-        if t < 3:
-            sums(t)
-        if t == 1:
-            moves0_a()
-            moves1_x(0)
-        else:
-            diff(t)
-        if t == 2:
-            moves0_b()
-            moves1_x(1)
-        if t < 3:
-            vectors(1, t)
-        if t < 2:
-            bias()
-    tt("UX", 0, B, T.b4[:, 0:B], T.SR1[:, K + B:K + K], ["b4", ("SR1", K + B, K + K)], A.min)
-    act("b1", 0, B, T.b4[:, 0:B], ["b4"], AF.Relu, -1.0, 16.0)
-    tt("DX", 2 * K + B, 3 * K, T.b1[:, 0:B], T.SR1[:, K:K + B], ["b1", ("SR1", K, K + B)], A.min)
-    relus(3)
-    mins(1, 3)
-    act("DX", 2 * K, 2 * K + B, T.UX[:, 0:B], [("UX", 0, B)], AF.Relu)
-    moves1_y()
-    moves1_z()
-    down(1)
+    gather(1, 0, 1, 0, "s")
+    leaf_list(1, "b6", 0)
+    leaf_list(1, "b6", 1)
+    start_rows("b2", 0)
+    gather(1, 0, 1, 1, "s")
+    leaf_flags("b6")
+    gather(1, 0, 0, 0, "v")
+    gather(1, 0, 0, 1, "v")
+    leaf_starts(1, "b6", 0)
+    column(mat("WN2"), D2R, co(WF))
+    copy("s", whole("XB3"), bank("b5"))
+    sums(0, 0)
+    floor(0)
+    sums(0, 1)
+    clamp(1, 0, 0)
+    floor(1)
+    diff(0, "b2", False)
+    column(mat("WP3"), D3L, co(WF))
+    mm(bank("b5"), mat("BI3"), CN, True, False)
+    clamp(1, 0, 1)
+    gather(1, 1, 0, 0, "v")
+    store0()
+    gather(1, 1, 1, 0, "s")
+    gather(1, 1, 0, 1, "s")
+    sums(1, 0)
+    gather(1, 1, 1, 1, "v")
+    sums(1, 1)
+    leaf_starts(1, "b6", 1)
+    floor(0)
+    leaf_starts(1, "b6", 2)
+    floor(1)
+    clamp(1, 1, 0)
+    rows(1, 1, 0, "s")
+    rows(1, 1, 1, "s")
+    mm(bank("b7"), whole("WN1"), vec(1, 0), True, False)
+    clamp(1, 1, 1)
+    mm(bank("b7"), whole("WP1"), vec(1, 1), False, True)
+    tt(whole("XS"), bank("b7"), whole("XS"), A.min)
+    gather(1, 2, 0, 1, "v")
+    pick(1, "b3", False, True)
+    gather(1, 2, 0, 0, "s")
+    relu("v", whole("DG"), whole("XS"), co(C1))
+    tt(node("TAB", 1), whole("DG"), bank("b3"), A.add)
+    gather(1, 2, 1, 0, "s")
+    sums(2, 0)
+    gather(1, 2, 1, 1, "s")
+    sums(2, 1)
+    floor(0)
+    mm(bank("b4"), mat("WN2"), vec(2, 0), False, False)
+    column(mat("WP3"), D3R, co(WG))
+    floor(1)
+    column(mat("WP2"), D2R, co(WG))
+    clamp(1, 2, 0)
+    clamp(1, 2, 1)
+    rows(1, 2, 1, "v")
+    rows(1, 2, 0, "s")
+    mm(bank("b4"), mat("WP2"), vec(2, 1), False, False)
+    gather(1, 3, 0, 1, "s")
+    pick(2, "b4", False, True, 2)
+    gather(1, 3, 0, 0, "s")
+    gather(1, 3, 1, 1, "d")
+    gather(1, 3, 1, 0, "d")
+    tt(node("TAB", 2), bank("b4"), whole("XB2"), A.min)
+    rows(1, 3, 0, "s", edge(0))
+    rows(1, 3, 1, "s", edge(1))
+    mm(bank("b5"), mat("WP3"), vec(3, 1), False, True)
+    relu("s", node("TAB", 2), node("TAB", 2))
+    tt(bank("b7"), bank("b5"), whole("XB3"), A.min)
+    edge_store(0, "b7")
+    edge_store(1, "b7")
+    for k in range(2):
+        sum_up(1, k)
+        add_roots(1, k)
+    places(1, 0)
+    places(1, 1)
     exchange(1)
     dma("s", [("WB1", 512 * me, 512 * me + 512)], [], T.y[:, 512 * me:512 * me + 512], T.WB1[:, 512 * me:512 * me + 512])
     for i, s in enumerate([s for s in range(4) if topo.chip(cores[s]) == topo.chip(core) and s != me] +

@@ -7,8 +7,14 @@ L, NT, B, RO = 2048, 4, 384, 2
 K = 2 * B
 C = B // 2
 N3 = 3 * B
-EDGE = L + N3
+NB = (L + N3) // 16
 CUT = L - 16
+V1 = L + B
+RANK = 128.0
+LOW, HIGH, SMALL = 2.0 ** -7, 2.0 ** 5, 2.0 ** -12
+MATS = ["Z1", "DM1", "DQZ", "DQS", "NR2", "NR3", "S3L", "S3R",
+        "UL", "SL", "UR", "SR", "UP", "SP", "US", "SS", "SC", "Z3", "EX", "SUM", "M0", "TA", "TB", "M2"]
+EDGE = L + N3
 TW = EDGE + K - CUT
 BASE, TURN, MASK = 72.0, 16.0, 8.0
 CODE = 96
@@ -16,51 +22,62 @@ BIG = 4096.0
 RUN = N3 // 16
 PART = ((0, 64), (64, 128))
 SIZE, D3L, START, D3R, D2L, D2R, EVEN, ODD = 0, 1, 2, 3, 4, 6, 8, 9
-MATS = ["ZM", "Z1", "DM1", "DQZ", "DQS", "NR2", "NR3", "ST", "S3L", "S3R",
-        "X1L", "X1R", "WP2", "WN2", "WP3", "BI2", "BI3"]
-EARLY = 144 * 10
 U, BF, SS, VV, AT, AP = 0, 4, 8, 12, 16, 20
-WS, E0, LO, Z0, Z2, E2, HC, CR, RF, I0, HT, NB, A3, NCR, TS, TB, WF, WG, C1, BG, BH = range(24, 45)
+WS, E0, LO, Z0, Z2, E2, HC, CR, RF, HT, MB, TS, TB, E1, RW, RN, RH, TN, TH, NC, WA, WB, I0 = range(24, 47)
 
 SCRATCH = {
-    "KI": ("sbuf", [128, 384], "int32"), "K16": ("sbuf", [128, 384], "uint16"), "KS": ("sbuf", [128, 384], "uint16"),
-    "PI": ("sbuf", [128, 8], "int32"), "CO": ("sbuf", [128, 48], "float32"),
-    "M0": ("sbuf", [128, EDGE + K], "float32"), "M1": ("sbuf", [128, EDGE], "float32"), "B72": ("sbuf", [128, 640], "float32"),
-    "MB": ("sbuf", [128, L], "float16"), "PRE": ("sbuf", [128, B], "float32"),
-    "STEP": ("sbuf", [128, B], "bfloat16"), "S0": ("sbuf", [128, RUN], "bfloat16"),
-    "NC": ("sbuf", [128, RUN], "float32"), "OWH": ("sbuf", [128, RUN], "float32"), "RL0": ("sbuf", [128, RUN], "float32"),
-    "TAB": ("sbuf", [128, TW], "float32"),
-    "MAT": ("sbuf", [128, 144 * len(MATS)], "bfloat16"), "ONE": ("sbuf", [128, 512], "bfloat16"),
-    "IDN": ("sbuf", [128, 128], "bfloat16"), "YM": ("sbuf", [128, 6 * 128], "bfloat16"),
-    "BLA": ("sbuf", [128, 128], "bfloat16"), "BLK": ("sbuf", [128, 128], "bfloat16"), "TRI": ("sbuf", [128, 128], "bfloat16"),
-    "BLS": ("sbuf", [128, 128], "bfloat16"), "EQ": ("sbuf", [128, 16 * 128], "bfloat16"),
-    "TRS": ("sbuf", [128, 128], "bfloat16"), "SGB": ("sbuf", [128, 128], "bfloat16"), "SD1": ("sbuf", [128, 128], "bfloat16"),
-    "CN": ("sbuf", [128, B], "bfloat16"), "OWN": ("sbuf", [128, RUN], "float32"),
-    "MI": ("sbuf", [128, 256], "bfloat16"), "WI": ("sbuf", [128, 1], "bfloat16"), "MM": ("sbuf", [128, 256], "bfloat16"),
+    "KI": ("sbuf", [128, 384], "int32"), "K16": ("sbuf", [128, 384], "uint16"), "KS": ("sbuf", [128, 192], "uint16"),
+    "KZ": ("sbuf", [128, 96], "uint16"), "M": ("sbuf", [128, EDGE + K], "float32"), "MB": ("sbuf", [128, L], "float16"),
+    "PRE": ("sbuf", [128, B], "float32"), "STEP": ("sbuf", [128, B], "float32"), "S0": ("sbuf", [128, RUN], "bfloat16"),
+    "NCO": ("sbuf", [128, RUN], "float32"), "OWH": ("sbuf", [128, RUN], "float32"), "RL": ("sbuf", [128, RUN], "float32"),
+    "OWN": ("sbuf", [128, RUN], "float32"), "TAB": ("sbuf", [128, TW], "float32"), "YM": ("sbuf", [128, 4 * 128], "bfloat16"),
+    "BLS": ("sbuf", [128, 128], "bfloat16"), "SGB": ("sbuf", [128, 128], "bfloat16"), "CN": ("sbuf", [128, B], "bfloat16"),
+    "WP0": ("sbuf", [128, 128], "bfloat16"), "WN0": ("sbuf", [128, 128], "bfloat16"), "SR": ("sbuf", [128, 2 * N3], "bfloat16"),
+    "DG": ("sbuf", [128, B], "bfloat16"), "F": ("sbuf", [128, RUN + 8], "bfloat16"), "RS": ("sbuf", [128, RUN], "bfloat16"),
+    "OFS": ("sbuf", [128, 8], "float32"), "INC": ("sbuf", [128, RUN + 8], "float16"), "IX": ("sbuf", [128, B], "float16"),
+    "PT": ("sbuf", [128, 128], "uint16"), "RM": ("sbuf", [128, 128], "float16"), "FL": ("sbuf", [128, 128], "bfloat16"),
+    "IL": ("sbuf", [128, 128], "float32"), "FS": ("sbuf", [128, 4096], "float32"),
+    "KA": ("sbuf", [128, 192], "int32"), "KB": ("sbuf", [128, 192], "int32"), "KP": ("sbuf", [128, 192], "uint16"),
+    "KF": ("sbuf", [128, 48], "float16"), "GE": ("sbuf", [128, 48], "bfloat16"), "KT": ("sbuf", [128, 48], "float32"),
+    "KU": ("sbuf", [128, 48], "int32"), "K1": ("sbuf", [128, 48], "uint16"),
+    "PI": ("sbuf", [128, 8], "int32"), "CO": ("sbuf", [128, 52], "float32"),
+    "ONE": ("sbuf", [128, 512], "bfloat16"), "ONF": ("sbuf", [128, 256], "float32"),
+    "ZF": ("sbuf", [128, K], "float32"), "ZB": ("sbuf", [128, K], "bfloat16"),
+    "MAT": ("sbuf", [128, 144 * len(MATS)], "bfloat16"), "EQ": ("sbuf", [128, 16 + 16 * 128], "bfloat16"),
+    "IDN": ("sbuf", [128, 128], "bfloat16"), "BLA": ("sbuf", [128, 128], "bfloat16"), "BLK": ("sbuf", [128, 128], "bfloat16"),
+    "TRI": ("sbuf", [128, 128], "bfloat16"), "TRS": ("sbuf", [128, 128], "bfloat16"), "TRB": ("sbuf", [128, 256], "bfloat16"),
+    "TRF": ("sbuf", [128, 256], "float32"), "IM": ("sbuf", [128, 256], "bfloat16"), "NG": ("sbuf", [128, 128], "bfloat16"),
+    "DUP": ("sbuf", [128, 128], "bfloat16"), "MG": ("sbuf", [128, 256], "bfloat16"),
+    "LA": ("sbuf", [128, 128], "bfloat16"), "LN": ("sbuf", [128, 128], "bfloat16"),
+    "VA": ("sbuf", [128, 128], "bfloat16"), "VB": ("sbuf", [128, 256], "bfloat16"), "VC": ("sbuf", [128, 1024], "bfloat16"),
+    "MT": ("sbuf", [128, 1184], "bfloat16"), "CT": ("sbuf", [128, 208], "bfloat16"), "JJ": ("sbuf", [128, 128], "bfloat16"),
+    "BJ": ("sbuf", [128, 8], "float32"), "RAMP": ("sbuf", [128, 128], "float32"),
+    "MI": ("sbuf", [128, 256], "bfloat16"), "WI": ("sbuf", [128, 1], "bfloat16"), "MM": ("sbuf", [128, 384], "bfloat16"),
     "WP": ("sbuf", [128, 128], "bfloat16"), "WN": ("sbuf", [128, 128], "bfloat16"),
-    "WP1": ("sbuf", [128, 128], "bfloat16"), "WN1": ("sbuf", [128, 128], "bfloat16"),
-    "F16": ("sbuf", [128, B], "float16"), "SR": ("sbuf", [128, 2 * N3], "bfloat16"), "RG": ("sbuf", [128, N3], "bfloat16"),
-    "DG": ("sbuf", [128, B], "bfloat16"), "XS": ("sbuf", [128, B], "bfloat16"),
-    "XB2": ("sbuf", [128, B], "bfloat16"), "XB3": ("sbuf", [128, B], "float32"),
-    "F": ("sbuf", [128, RUN + 8], "bfloat16"), "RS": ("sbuf", [128, RUN], "bfloat16"), "OFS": ("sbuf", [128, 8], "float32"),
-    "INC": ("sbuf", [128, RUN + 8], "float16"), "RL1": ("sbuf", [128, RUN], "float16"), "IX": ("sbuf", [128, B], "float16"),
-    "FL": ("sbuf", [128, 128], "bfloat16"), "IL": ("sbuf", [128, 128], "float32"),
-    "PR": ("sbuf", [128, 2048], "float16"), "QA": ("sbuf", [128, 128], "int32"), "QB": ("sbuf", [128, 128], "int32"),
-    "QL": ("sbuf", [128, 128], "uint16"),
-    "YL": ("sbuf", [128, L], "bfloat16"),
+    "FB": ("sbuf", [128, 256], "float32"),
+    "CP": ("sbuf", [128, 208], "float16"), "RK": ("sbuf", [128, 208], "bfloat16"), "JK": ("sbuf", [128, 8 * NB], "bfloat16"),
+    "CA": ("sbuf", [128, 8], "float32"), "CL": ("sbuf", [128, 8], "uint16"),
+    "SZ": ("sbuf", [128, 16 + N3], "bfloat16"), "SZB": ("sbuf", [128, 208], "bfloat16"), "SG": ("sbuf", [128, K], "bfloat16"),
+    "OH": ("sbuf", [128, 128], "bfloat16"), "SO": ("sbuf", [128, 128], "bfloat16"), "CC": ("sbuf", [128, 144], "bfloat16"),
+    "DS": ("sbuf", [128, 512], "bfloat16"), "SV": ("sbuf", [128, 512], "float16"), "AB": ("sbuf", [128, 96], "float16"),
+    "PL": ("sbuf", [128, 32], "uint16"), "SCN": ("sbuf", [128, 136], "float32"), "YI": ("sbuf", [128, 128], "int32"),
+    "YA": ("sbuf", [128, 128], "int32"), "YB": ("sbuf", [128, 128], "int32"),
+    "UN": ("sbuf", [128, 128], "uint16"), "CK": ("sbuf", [128, 128], "uint16"), "KM": ("sbuf", [128, L], "bfloat16"),
+    "LR": ("sbuf", [128, B], "float16"), "X0": ("sbuf", [128, B], "float16"),
+    "TI": ("sbuf", [128, V1 + L + NT * B], "float32"), "SI": ("sbuf", [128, 2 * N3], "float16"),
+    "F16": ("sbuf", [128, B], "float16"), "RG": ("sbuf", [128, N3], "bfloat16"), "AL": ("sbuf", [128, B], "bfloat16"),
+    "PR": ("sbuf", [128, L], "float16"), "QA": ("sbuf", [128, 128], "int32"), "QB": ("sbuf", [128, 128], "int32"),
+    "QL": ("sbuf", [128, 128], "uint16"), "YL": ("sbuf", [128, L], "bfloat16"), "WD": ("sbuf", [128, L], "bfloat16"),
 }
 for _t in range(NT):
     SCRATCH["G%d" % _t] = ("sbuf", [128, K], "bfloat16")
 for _r in range(RO):
-    SCRATCH.update({
-        "H%d" % _r: ("sbuf", [128, L + N3], "bfloat16"), "PT%d" % _r: ("sbuf", [128, 128], "uint16"),
-        "RM%d" % _r: ("sbuf", [128, 128], "float16"), "WB%d" % _r: ("sbuf", [128, L], "bfloat16"),
-    })
+    SCRATCH.update({"H%d" % _r: ("sbuf", [128, L + N3], "bfloat16"), "WB%d" % _r: ("sbuf", [128, L], "bfloat16")})
 for _b in range(8):
     SCRATCH["b%d" % _b] = ("psum", [128, 512], "float32")
 PSUM = ["b%d" % i for i in range(8)]
 
-SEMAPHORES = ["qv", "qs", "qp", "qg", "sent", "arr0"] + ["arr1_%d" % i for i in range(4)] + ["d%d" % i for i in range(24)]
+SEMAPHORES = ["qv", "qs", "qp", "qg", "sent", "arr0"] + ["arr1_%d" % i for i in range(4)] + ["d%d" % i for i in range(40)]
 
 
 def rank_program(g, core, T, topo):
@@ -126,13 +143,17 @@ def rank_program(g, core, T, topo):
         call().then_inc(T.sem[sem], 1)
         note(q, reads, writes, sem, total[sem])
 
-    def dma(q, reads, writes, out, in_):
+    def beside(q, reads, writes, copies):
         sync_for(q, reads, writes)
         sem = "d%d" % ndma[0]
         ndma[0] += 1
-        total[sem] = 16
-        eng[q].dma_start(out=out, in_=in_).then_inc(T.sem[sem], 16)
-        note(q, reads, writes, sem, 16)
+        total[sem] = 16 * len(copies)
+        for out, in_ in copies:
+            eng[q].dma_start(out=out, in_=in_).then_inc(T.sem[sem], 16)
+        note(q, reads, writes, sem, total[sem])
+
+    def dma(q, reads, writes, out, in_):
+        beside(q, reads, writes, [(out, in_)])
 
     V, S, P = g.vector, g.scalar, g.tensor
 
@@ -171,7 +192,7 @@ def rank_program(g, core, T, topo):
     def tt(o, x, y, o0):
         op("v", ins(o, x, y), outs(o), lambda: V.tensor_tensor(ap(o), ap(x), ap(y), o0))
 
-    def scan(o, x, y, init, o1=A.max):
+    def scan(o, x, y, o1=A.add, init=0.0):
         op("v", use(x, y, init), outs(o), lambda: V.tensor_tensor_scan(ap(o), ap(x), ap(y), val(init), A.add, o1))
 
     def reduce(o, x, o0, neg=False):
@@ -199,20 +220,18 @@ def rank_program(g, core, T, topo):
             act(o, x, AF.Identity, a, b)
         elif b is None:
             ts(o, x, a, A.mult)
-        elif a == 1.0:
-            ts(o, x, b, A.add)
         else:
             ts(o, x, a, A.mult, b, A.add)
 
-    def relu(q, o, x, bias=None):
+    def relu(q, o, x, scale=None, bias=None):
         if q == "s":
-            act(o, x, AF.Relu, 1.0, bias)
-        elif bias is None:
-            ts(o, x, 0.0, A.max)
+            act(o, x, AF.Relu, scale or 1.0, bias)
+        elif scale or bias:
+            ts(o, x, scale or bias, A.mult if scale else A.add, 0.0, A.max)
         else:
-            ts(o, x, bias, A.add, 0.0, A.max)
+            ts(o, x, 0.0, A.max)
 
-    def mm(o, lhs, x, start, stop):
+    def mm(o, lhs, x, start=True, stop=True):
         op("p", use(lhs, x), outs(o), lambda: P.matmul(ap(o), ap(lhs), ap(x), start, stop))
 
     def iota(o, pattern, base, cm):
@@ -232,8 +251,9 @@ def rank_program(g, core, T, topo):
         x = (m[0], m[1] + dst, m[1] + 128, 16)
         select(x, x, [[-16, 8]], A.not_equal, c, -src, 1)
 
-    def column(m, row, c):
-        lin("s", (m[0], m[1] + row, m[1] + 128, 16), ("BLK", row, 128, 16), c)
+    def column(q, name, row, c):
+        m = mat(name)
+        lin(q, (m[0], m[1] + row, m[1] + 128, 16), ("BLK", row, 128, 16), c)
 
     def whole(b):
         return (b, 0, SCRATCH[b][1][1])
@@ -241,60 +261,283 @@ def rank_program(g, core, T, topo):
     def bank(b, n=B, lo=0):
         return (b, lo, lo + n)
 
-    def kids(r, t, side, h=None, b="K16"):
+    def kids(r, t, side, h=None):
         c = 192 * r + 48 * t + 24 * side
-        return (b, c, c + 24) if h is None else (b, c + 12 * h, c + 12 * h + 12)
+        return ("K16", c, c + 24) if h is None else ("K16", c + 12 * h, c + 12 * h + 12)
+
+    def ki(r, lo, hi):
+        return ("KI", 192 * r + lo, 192 * r + hi)
+
+    def vec(t, side):
+        return ("G%d" % t, B * side, B * side + B)
+
+    def ti(t, v=1):
+        c = V1 * v + L + B * t
+        return ("TI", c, c + B)
+
+    def si(t, side):
+        c = N3 * side + B * (t - 1)
+        return ("SI", c, c + B)
+
+    def sz(t):
+        return ("SZ", 16 + B * t, 16 + B * t + B)
+
+    def rg(t):
+        return ("RG", B * (t - 1), B * t)
+
+    IDN, BLK, TRI, TRS = whole("IDN"), whole("BLK"), whole("TRI"), whole("TRS")
+    ones = ("ONE", 0, 128)
+    CN = whole("CN")
+    R = ("PI", 5, 6)
+
+    def zero(b, lo, hi, z="ZB"):
+        beside("y", [z], [(b, lo, hi)], [(T[b][:, c:min(c + K, hi)], T[z][:, 0:min(K, hi - c)]) for c in range(lo, hi, K)])
+
+    def ramps(v, rows):
+        beside("y", ["RAMP"], [("TI", V1 * v, V1 * v + L)], [(T.TI[row:128:16, V1 * v:V1 * v + L], T.RAMP[:, :]) for row in rows])
+
+    def diagonal(m, blk, src, d, c):
+        x = (m, 4 * blk, 4 * blk + 4)
+        select(x, x, [[-d, 4]], A.not_equal, c, -src, 1)
+
+    def double(q, m, n):
+        copy(q, (m, n, 2 * n), (m, 0, n))
+
+    def second_view():
+        g.wait_ge(T.sem["qg"], total["qg"])
+        learn("g", "qg", total["qg"], {})
+        op("g", ["ONE"], ["VA"], lambda: g.affine_select(T.VA[32:64, :], T.ONE[32:64, 0:128], [[-1, 8], [1, 16]], A.is_equal, 0.0, 3, -1))
+        g.wait_ge(T.sem["qg"], total["qg"])
+        learn("g", "qg", total["qg"], {})
+
+    def views():
+        beside("y", ["VA", "VB"], ["VC"], [x for j in range(8) for x in (
+            (T.VC[0:64, 128 * j:128 * j + 128], T.VA[0:64, :]), (T.VC[64:96, 128 * j:128 * j + 128], T.VB[64:96, 16 * j + 16:16 * j + 144]))])
+
+    def merging(b):
+        for side in range(2):
+            for j, m in enumerate(("TA", "TB")):
+                mm(bank(b, 128, 128 * side), whole("DUP"), mat(m, 7 + 8 * (side ^ j)), side + j == 0, side + j == 2)
+
+    def lists(r):
+        copy("v", ("K16", 192 * r, 192 * r + 192), ki(r, 0, 192))
+
+    def flag_lists(r, step):
+        if step == 0:
+            ts(whole("KA"), ki(r, 0, 192), 4097.0, A.mult)
+        elif step == 1:
+            ts(whole("KB"), whole("KA"), 4, A.arith_shift_right, 4095, A.bitwise_and)
+        else:
+            copy("v", whole("KP"), whole("KB"))
+
+    def flags(t):
+        act(("FS", 0, 4096, "KP", 48 * t, 48 * t + 48), whole("ZF"), AF.Silu)
+
+    def level1_sizes(r):
+        ts(whole("GE"), ki(r, 48, 96), float(L), A.is_ge, 1.0, A.add)
+        tt(("SZB", 152, 176), ("GE", 0, 24), ("GE", 24, 48), A.add)
+
+    def level1_lists(r):
+        for side in range(2):
+            ts(("KT", 24 * side, 24 * side + 24), ki(r, 72 - 24 * side, 96 - 24 * side), float(L), A.is_lt, float(V1), A.mult)
+        tt(whole("KU"), ki(r, 48, 96), whole("KT"), A.add)
+        copy("v", whole("K1"), whole("KU"))
+
+    def to_rows(b, i):
+        x = (("SZB", 152, 176), ("KF", 0, 24), ("KF", 24, 48))[i]
+        for q in range(16):
+            c = 16 + 128 * q - i
+            mm((b, q, B, 16), ("EQ", c, c + 128), x, i < 2 and q == 0, i != 1 and q == 15)
+
+    def extract(b, m, x, n, lo=0, hi=16):
+        for q in range(lo, hi):
+            mm(bank(b, n), mat(m, q), (x[0], x[1] + q, x[1] + 16 * n, 16), q == 0, q == 15)
+
+    def kid_sizes(t, q):
+        copy(q, whole("SG"), ("SZ", 0, 16 + B * t, "KZ", 48 * (t - 2), 48 * (t - 1)))
+
+    def ranks(b1, b2):
+        mm(bank(b1, NB), BLK, ("CP", 1, NB + 1))
+        mm(bank(b2, NB), ("TRB", 0, 128), ("CP", 1, NB + 1), True, False)
+        mm(bank(b2, NB), ("TRB", 128, 256), ("CP", 0, NB), False, True)
+
+    def count(b, lo, hi):
+        for m in range(lo, hi):
+            o = ("JK", NB * m, NB * m + NB)
+            op("s", [b, "BJ"], [o, ("CA", m, m + 1)],
+               lambda: S.activation(ap(o), T[b][:, 0:NB], AF.Sign, bias=T.BJ[:, m:m + 1], scale=-1.0, accum_out=T.CA[:, m:m + 1]))
+
+    def steps(b, part):
+        if part == 0:
+            for side, (m0, m1) in enumerate((("UL", "SL"), ("UR", "SR"))):
+                mm(bank(b, B, 128), mat(m0), ("SG", B * side, B * side + B), side == 0, False)
+                mm(bank(b, B - 1, 129), mat(m1), ("SG", B * side, B * side + B - 1), False, False)
+            return
+        m0, m1, x = ((mat("UP"), mat("SP"), "OH"), (mat("Z1", 0), mat("SC"), "CC"), (mat("US"), mat("SS"), "SO"))[part - 1]
+        n = 129 if x == "CC" else 128
+        mm(bank(b, n), m0, (x, 0, n), False, False)
+        mm(bank(b, 128, 1), m1, (x, 0, 128), False, part == 3)
+
+    def spots(b, step):
+        if step == 0:
+            ts(("AB", 0, 32), bank(b, 32), 16.0, A.mult)
+            ts(("AB", 32, 64), bank(b, 32), 0.25, A.mult, 1025 - 0.375, A.add)
+            ts(("AB", 64, 96), bank(b, 32), 1 / 64, A.mult, 1025 - 63 / 128, A.add)
+        elif step == 1:
+            for j, m in enumerate((IDN, ("IM", 0, 128), ("IM", 128, 256))):
+                mm(bank(b, 32), m, ("AB", 32 * j, 32 * j + 32), j == 0, j == 2)
+        else:
+            ts(whole("PL"), bank(b, 32), 15 * 1025.0, A.add)
+
+    def drop():
+        copy("v", ("WD", 0, L, "PL", 0, 32), whole("DS"))
+
+    def dropped(b, lo, hi):
+        extract(b, "EX", ("WD", 0), 128, lo, hi)
+
+    def before(b):
+        mm(bank(b, 32), ("TRF", 0, 128), ("SCN", 7, 132, 4), True, False)
+        mm(bank(b, 32), ("TRF", 128, 256), ("SCN", 3, 128, 4), False, True)
+
+    def totals(b):
+        for i, d in enumerate(turns(me)):
+            tt(("YI", 32 * i, 32 * i + 32), ("SCN", 4 + d, 132, 4), bank(b, 32), A.add)
+
+    def masks(i, q):
+        copy(q, ("KM", 512 * i, 512 * i + 512), ("MT", 0, 1184, "CK", 32 * i, 32 * i + 32))
+
+    def gather(r, t, side, h, q):
+        o = B * side + C * h
+        x = ("H%d" % r, 0, L + B * t) + kids(r, t, side, h)
+        if q == "d":
+            tt(("G%d" % t, o, o + C), x, ("G%d" % t, o - B, o - B + C), A.subtract)
+        else:
+            copy(q, ("G%d" % t, o, o + C), x)
+
+    def sums(t, h, d=0):
+        for side in range(2):
+            o, m = B * side + C * h, 128 * side or 256 * d
+            mm(bank("b%d" % h, C), ("MM", m, m + 128), ("G%d" % t, o, o + C), side == 0, side == 1)
+
+    def floor(h):
+        ts(("F16", C * h, C * h + C), bank("b%d" % h, C), 1536 - 0.375, A.add, 1536.0 - 127, A.max)
+
+    def clamp(r, t, h):
+        lo = L + B * t + C * h
+        ts(("H%d" % r, lo, lo + C), ("F16", C * h, C * h + C), 1536.0 + 127, A.min, 1536.0, A.subtract)
+
+    def signs(t, b, d=0):
+        if not d:
+            mm(bank(b), whole("WN"), vec(t, 0), t > 0, False)
+        mm(bank(b), whole("WP"), vec(t, 1), d == 1, True)
+
+    def half(x, h, n=C):
+        return x if h is None else x[:-2] + (x[-2] + n * h, x[-2] + n * h + n)
+
+    def ids(r, t, side, h, q):
+        x = ("TI", 0, 2 * V1, "K1", 24 * side, 24 * side + 24) if t == 1 else ("TI", V1, V1 + L + B * t) + kids(r, t, side)
+        relu(q, half(si(t, side), h), half(x, h, 12))
+
+    merged = set()
+
+    def merge(t, side, b, h=None):
+        m = ("MG", 128 * side, 128 * side + 128) if t == 1 else mat("M2", 7 + 8 * side)
+        mm(half(bank(b), h), m, half(si(t, side), h), b not in merged, b in merged)
+        merged.symmetric_difference_update({b})
+
+    def keep(t, b, h=None):
+        tt(half(ti(t), h), half(bank(b), h), half(rg(t) if t < 3 else whole("AL"), h), A.min if t < 3 else A.mult)
+
+    def choose(i):
+        tt(("PR", 512 * i, 512 * i + 512), ("TI", V1, V1 + L + NT * B, "UN", 32 * i, 32 * i + 32), ("KM", 512 * i, 512 * i + 512), A.mult)
+
+    def chosen(i, n, b):
+        extract(b, "SUM", ("PR", 512 * i), 32 * n)
+
+    def leaf_at(i, n, b, step):
+        lo, hi = 32 * i, 32 * (i + n)
+        if step == 0:
+            copy("v", ("QA", lo, hi), bank(b, 32 * n))
+        elif step == 1:
+            ts(("QB", lo, hi), ("QA", lo, hi), L - 1, A.bitwise_and)
+        else:
+            copy("v", ("QL", lo, hi), ("QB", lo, hi))
+
+    def engines(src, d):
+        s = cores[src]
+        far = [c for c in cores if topo.chip(c) != topo.chip(s)]
+        if cores[d] in far:
+            return topo.engines(s, cores[d])
+        return [e for e in topo.engines(s, cores[d]) if e not in topo.engines(s, far[0])]
+
+    def turns(src):
+        s = cores[src]
+        return sorted(range(4), key=lambda d: (d == src, topo.chip(cores[d]) == topo.chip(s), topo.die(cores[d]) != topo.die(s)))
+
+    def shared(src):
+        far1, far2, near = turns(src)[:3]
+        es = engines(src, far1)
+        return {far1: es[:len(es) // 2], far2: es[len(es) // 2:], near: engines(src, near)}
+
+    def send(wb, dst, sem, to):
+        tr = []
+        for d, es in to.items():
+            rid, pid, _se = topo.addr(cores[d])
+            tr.append(RemoteDMATransfer(dst_ids=[DstId(rid=rid, pnc=pid)], dma_engine_mask=sum(1 << e for e in es),
+                                        remote_sem=T.sem[sem], src=T[wb][:, 512 * d:512 * d + 512],
+                                        dst=T[dst][:, 512 * me:512 * me + 512]))
+        sync_for("g", [(wb, 512 * d, 512 * d + 512) for d in to], [])
+        g.remote_dma_fused(tr, local_sem=T.sem["sent"])
+        total["sent"] = total.get("sent", 0) + sum(len(es) for es in to.values())
+
+    def exchange():
+        send("WB0", "H1", "arr0", shared(me))
+        mine = ("H1", 512 * me, 512 * me + 512)
+        dma("y", ["WB0"], [mine], ap(mine), T.WB0[:, 512 * me:512 * me + 512])
+
+    def fetch(i, q):
+        d = turns(me)[i]
+        o = ("WB1", 512 * d, 512 * d + 512)
+        copy(q, o, ("H1", 0, L, "QL", 32 * i, 32 * i + 32))
+        if d != me:
+            send("WB1", "YL", "arr1_%d" % me, {d: engines(me, d)})
+        else:
+            dma("s", [o], [], T.y[:, 512 * me:512 * me + 512], ap(o))
+
+    others = [s for s in range(4) if s != me]
+    total["arr0"] = sum(len(shared(s)[me]) for s in others)
+    for s in others:
+        total["arr1_%d" % s] = len(engines(s, me))
+        for b, sem in (("H1", "arr0"), ("YL", "arr1_%d" % s)):
+            acc.setdefault(b, []).append(("w", 512 * s, 512 * s + 512, "x", sem, total[sem], {}))
 
     def node(b, t):
         c = L + B * t - (CUT if b == "TAB" else 0)
         return (b, c, c + B)
 
-    def edge(side):
-        return node("TAB", 3 + side)
-
     def sr(t, side):
         c = N3 * side + B * (t - 1)
         return ("SR", c, c + B)
 
-    def rg(t):
-        return ("RG", B * (t - 1), B * t)
-
-    def vec(t, side):
-        return ("G%d" % t, B * side, B * side + B)
-
-    IDN, BLK, TRI, CN = whole("IDN"), whole("BLK"), whole("TRI"), whole("CN")
-
     def ym(i):
         return ("YM", 128 * i, 128 * i + 128)
 
-    def eq(q):
-        return ("EQ", 128 * q, 128 * q + 128)
+    def own(t, q):
+        lin(q, node("M", t), whole("STEP"), co(E0), co(I0 + t))
 
-    def lists(r):
-        x = ("KI", 192 * r, 192 * r + 192)
-        copy("v", ("K16",) + x[1:], x)
+    def turn(t, q):
+        lin(q, whole("PRE"), node("M", t), 1.0, co(AT + t))
 
-    def tab_lists(r):
-        x = ("KI", 192 * r + 48, 192 * r + 192)
-        ts(("KS",) + x[1:], x, float(CUT), A.subtract)
-
-    def own(t):
-        scan(node("M0", t), whole("STEP"), whole("STEP"), co(I0) if t == 0 else ("M0", L + B * t - 1, L + B * t))
-
-    def turn(r, t, q):
-        lin(q, whole("PRE"), node("M%d" % r, t), 1.0, co(AT + t))
-
-    def hand(r, t, side, q):
-        m = "M%d" % r
-        x = node("M0", 3 + side) if t == 3 else whole("PRE") if side else node(m, t)
+    def hand(t, side, q):
+        x = node("M", 3 + side) if t == 3 else whole("PRE") if side else node("M", t)
         if q == "s":
-            act((m, 0, L + B * t) + kids(r, t, side), x, AF.Silu)
+            act(("M", 0, L + B * t) + kids(0, t, side), x, AF.Silu)
         else:
-            copy(q, (m, 0, L + B * t) + kids(r, t, side), x)
+            copy(q, ("M", 0, L + B * t) + kids(0, t, side), x)
 
-    def narrow(r, k):
+    def narrow(k, q):
         lo, hi = PART[k]
-        ts(("MB", 16 * lo, 16 * hi), ("M%d" % r, 16 * lo, 16 * hi), co(NB), A.add, 0.0, A.max)
+        relu(q, ("MB", 16 * lo, 16 * hi), ("M", 16 * lo, 16 * hi), None, co(MB))
 
     def leaf_codes(b, k):
         lo, hi = PART[k]
@@ -304,14 +547,6 @@ def rank_program(g, core, T, topo):
     def runs(t):
         return [(q, max(B * t - RUN * q, 0), min(B * t + B - RUN * q, RUN), max(RUN * q - B * t, 0))
                 for q in range(B * t // RUN, -(-(B * t + B) // RUN))]
-
-    def node_codes(r):
-        m = "M%d" % r
-        dma("y", [(m, L, EDGE)], ["NC"], T.NC[:, :], T[m][SIZE:128:16, L:EDGE])
-
-    def sizes(t):
-        for side in range(2):
-            mm(bank("b7"), mat("Z1", SIZE), sr(t, side), side == 0, side == 1)
 
     def node_sizes(t):
         if t == 0:
@@ -323,518 +558,518 @@ def rank_program(g, core, T, topo):
                 c += sr(t, side)[1]
                 mm(bank("b6", hi - lo, lo), mat("DQZ", q), ("SR", c, c + hi - lo), False, side + q == 16)
 
-    def node_flags():
-        tt(("F", 0, RUN), whole("NC"), whole("OWH"), A.is_lt)
-        mm(bank("b5", RUN + 1), BLK, ("F", 0, RUN + 1), True, True)
-
-    def root_leaves():
-        reduce(("OFS", 0, 1), bank("b5", RUN + 1), A.add, True)
-
-    def root_sizes():
-        tt(whole("RS"), ("F", 0, RUN), bank("b6", RUN), A.mult)
-
-    def run_sums():
-        scan(("INC", 1, RUN + 1), whole("RS"), whole("RS"), 0.0)
-        mm(bank("b6", 1, 300), whole("TRS"), ("INC", RUN, RUN + 1), True, True)
-        mm(bank("b6", 1, 301), BLK, ("INC", RUN, RUN + 1), True, True)
-
-    def node_starts(r):
-        ts(whole("RL%d" % r), ("INC", 0, RUN), bank("b6", 1, 300), A.add, ("OFS", 0, 1), A.add)
-        ts(("OFS", 1, 2), bank("b6", 1, 301), ("OFS", 0, 1), A.add, -1.0 if r else 1 / 256, A.mult)
-
-    def start_rows(b, t):
-        for q, lo, hi, c in runs(t):
-            mm(bank(b, hi - lo, c), eq(q), ("RL1", lo, hi), False, False)
-
-    def leaf_list(r, b, k):
+    def leaf_list(b, k):
         lo, hi = PART[k]
-        ts(("PT%d" % r, lo, hi), bank(b, hi - lo, lo), float(CODE), A.subtract)
+        ts(("PT", lo, hi), bank(b, hi - lo, lo), float(CODE), A.subtract)
 
-    def leaf_flag(b, lo, hi):
+    def leaf_flag(b, k):
+        lo, hi = PART[k]
         ts(("FL", lo, hi), bank(b, hi - lo, lo), float(CODE), A.is_lt)
 
-    def leaf_flags(b, done=0):
-        leaf_flag(b, done, 128)
-        mm(bank(b, 128, 128), BLK, whole("FL"), True, True)
-        mm(bank(b, 128, 256), TRI, whole("FL"), True, True)
+    def rows(t, side, q):
+        c = 48 * t + 24 * side
+        copy(q, sr(t, side), ("TAB", 0, L + B * t - CUT, "KS", c, c + 24))
 
-    def leaf_starts(r, b, step):
-        if step == 0:
-            scan(whole("IL"), bank(b, 128, 128), whole("FL"), 0.0)
-        elif step == 1:
-            tt(whole("IL"), whole("IL"), bank(b, 128, 256), A.subtract)
-        else:
-            tt(whole("RM%d" % r), whole("IL"), whole("FL"), A.mult)
+    def diff(t, b, d=0):
+        if not d:
+            mm(bank(b), whole("WN0"), vec(t, 0), t > 0, False)
+        mm(bank(b), whole("WP0"), vec(t, 1), d == 1, True)
 
-    def gather(r, t, side, h, q):
-        o = B * side + C * h
-        x = ("H%d" % r, 0, L + B * t) + kids(r, t, side, h)
-        if q == "d":
-            tt(("G%d" % t, o, o + C), x, ("G%d" % t, o - B, o - B + C), A.subtract)
-        else:
-            copy(q, ("G%d" % t, o, o + C), x)
-
-    def rows(r, t, side, q, o=None):
-        copy(q, o or sr(t, side), ("TAB", 0, L + B * t - CUT) + kids(r, t, side, None, "KS"))
-
-    def sums(t, h):
+    def pick(t, b):
         for side in range(2):
-            o = B * side + C * h
-            mm(bank("b%d" % h, C), ("MM", 128 * side, 128 * side + 128), ("G%d" % t, o, o + C), side == 0, side == 1)
-
-    def diff(t, b, start=True):
-        mm(bank(b), whole("WN"), vec(t, 0), start, False)
-        mm(bank(b), whole("WP"), vec(t, 1), False, True)
-
-    def floor(h):
-        ts(("F16", C * h, C * h + C), bank("b%d" % h, C), 1536 - 0.375, A.add, 1536.0 - 127, A.max)
-
-    def clamp(r, t, h):
-        lo = L + B * t + C * h
-        ts(("H%d" % r, lo, lo + C), ("F16", C * h, C * h + C), 1536.0 + 127, A.min, 1536.0, A.subtract)
-
-    def tie_break():
-        mm(bank("b2"), whole("SGB"), CN, True, False)
-
-    def store0():
-        ts(node("TAB", 0), bank("b2"), co(LO), A.max, co(HC), A.min)
-
-    def others1(b):
-        mm(bank(b), mat("Z1", EVEN), sr(1, 0), True, False)
-        mm(bank(b), mat("Z1", ODD), sr(1, 1), False, True)
-
-    def pick(t, b, start, stop=False, y=0):
-        for side in range(2):
-            mm(bank(b), ym(2 * (t - 1) + y + side), sr(t, side), start and side == 0, stop and side == 1)
-
-    def edge_sizes(b, stop):
-        for side in range(2):
-            mm(bank(b), mat(("S3L", "S3R")[side]), sr(3, side), side == 0, stop and side == 1)
-
-    def edge_sums(r):
-        if r == 0:
-            scan(whole("IX"), sr(3, 0), sr(3, 1), ("OFS", 1, 2), A.add)
-        else:
-            scan(whole("IX"), bank("b0"), ("ONE", 0, B), ("OFS", 1, 2), A.min)
-
-    def edge_starts(r):
-        mm(bank("b5"), mat("ST") if r else mat("DQZ", START), whole("IX"), False, r == 1)
+            mm(bank(b), ym(2 * (t - 1) + side), sr(t, side), side == 0, False)
 
     def edge_store(side, b):
-        tt(edge(side), edge(side), bank(b), A.max)
+        tt(node("TAB", 3 + side), sr(3, side), bank(b), A.max)
 
-    def sum_up(r, k):
+    def sum_up(k):
         lo, hi = PART[k]
-        tt(("PR", 16 * lo, 16 * hi), ("TAB", 0, TW, "PT%d" % r, lo, hi), ("MB", 16 * lo, 16 * hi), A.mult)
+        tt(("PR", 16 * lo, 16 * hi), ("TAB", 0, TW, "PT", lo, hi), ("MB", 16 * lo, 16 * hi), A.mult)
+
+    def summed(k):
+        lo, hi = PART[k]
         for q in range(16):
             mm(bank("b%d" % k, hi - lo), mat("DQS", q), ("PR", 16 * lo + q, 16 * hi, 16), q == 0, False)
 
-    def add_roots(r, k):
+    def add_roots(k):
         lo, hi = PART[k]
-        mm(bank("b%d" % k, hi - lo), IDN, ("RM%d" % r, lo, hi), False, True)
+        mm(bank("b%d" % k, hi - lo), IDN, ("RM", lo, hi), False, True)
 
-    def places(r, k):
+    def places(k, step):
         lo, hi = PART[k]
-        ts(("QA", lo, hi), bank("b%d" % k, hi - lo), 2049.0, A.mult)
-        ts(("QB", lo, hi), ("QA", lo, hi), 2, A.arith_shift_right, 2047, A.bitwise_and)
-        copy("v", ("QL", lo, hi), ("QB", lo, hi))
-        copy("v", ("WB%d" % r, 0, L, "QL", lo, hi), ("H%d" % r, 16 * lo, 16 * hi))
+        if step == 0:
+            ts(("QA", lo, hi), bank("b%d" % k, hi - lo), 2049.0, A.mult)
+        elif step == 1:
+            ts(("QB", lo, hi), ("QA", lo, hi), 2, A.arith_shift_right, 2047, A.bitwise_and)
+        else:
+            copy("v", ("QL", lo, hi), ("QB", lo, hi))
 
-    def plan(src):
-        s = cores[src]
-        off = [d for d in range(4) if d != src and topo.chip(cores[d]) != topo.chip(s)]
-        on = [d for d in range(4) if d != src and topo.chip(cores[d]) == topo.chip(s)]
-        oe = topo.engines(s, cores[off[0]])
-        n = len(oe) // len(off)
-        res = {d: oe[n * i:n * i + n] for i, d in enumerate(off)}
-        for d in on:
-            res[d] = [e for e in topo.engines(s, cores[d]) if e not in oe]
-        return res
-
-    def exchange(r):
-        wb = "WB%d" % r
-        dst = ("H1", "YL")[r]
-        sem = "arr0" if r == 0 else "arr1_%d" % me
-        tr = []
-        n = 0
-        for d, es in plan(me).items():
-            rid, pid, _se = topo.addr(cores[d])
-            m = sum(1 << e for e in es)
-            n += len(es)
-            tr.append(RemoteDMATransfer(dst_ids=[DstId(rid=rid, pnc=pid)], dma_engine_mask=m, remote_sem=T.sem[sem],
-                                        src=T[wb][:, 512 * d:512 * d + 512], dst=T[dst][:, 512 * me:512 * me + 512]))
-        sync_for("g", [wb], [])
-        g.remote_dma_fused(tr, local_sem=T.sem["sent"])
-        total["sent"] = total.get("sent", 0) + n
-        note("g", [wb], [], "sent", total["sent"])
-        others = [s for s in range(4) if s != me]
-        got = sum(len(plan(s)[me]) for s in others)
-        for s in others:
-            sem, n = ("arr0", got) if r == 0 else ("arr1_%d" % s, len(plan(s)[me]))
-            total[sem] = n
-            acc.setdefault(dst, []).append(("w", 512 * s, 512 * s + 512, "x", sem, n, {}))
-        if r == 0:
-            dma("y", [wb], [(dst, 512 * me, 512 * me + 512)], T[dst][:, 512 * me:512 * me + 512], T[wb][:, 512 * me:512 * me + 512])
+    def scatter(lo, hi):
+        copy("v", ("WB0", 0, L, "QL", lo, hi), ("H0", 16 * lo, 16 * hi))
 
     dma("y", [], [("KI", 0, 192)], T.KI[:, 0:192], T.kids[:, 0:192])
-    dma("y", [], [("H0", 0, L)], T.H0[:, 0:L], T.x[:, :])
-    dma("y", [], [("MI", 0, 128)], T.MI[:, 0:128], T.ml[:, :])
-    dma("y", [], [("MI", 128, 256)], T.MI[:, 128:256], T.mr[:, :])
-    dma("y", [], ["WI"], T.WI[:, :], T.w[:, :])
-    dma("y", [], [("KI", 192, 384)], T.KI[:, 192:384], T.kids[:, 192:384])
-
-    R = ("PI", 5, 6)
-    ones = ("ONE", 0, 128)
-    fill(whole("ONE"), 1.0)
     iota(("PI", 0, 1), [[0, 1]], 0, 1)
-    iota(whole("S0"), [[0, RUN]], 2, 0)
+    iota(whole("STEP"), [[1, B]], 0, 0)
+    iota(whole("ZB"), [[0, K]], 0, 0)
+    fill(whole("ONE"), 1.0)
     select(whole("BLA"), ones, [[-16, 8], [0, 16]], A.is_ge, 0.0, 0, 1)
+    iota(("LN", 0, 8), [[0, 8]], 0, 0)
+    iota(("LA", 0, 16), [[0, 16]], 0, 0)
+    iota(whole("BJ"), [[16, 8]], 0, 0)
     select(BLK, whole("BLA"), [[16, 8], [0, 16]], A.is_ge, 0.0, 15, -1)
+    iota(whole("S0"), [[0, RUN]], 2, 0)
     select(whole("BLS"), BLK, [[0, 8], [1, 16]], A.is_ge, 0.0, -EVEN, 0)
+    dma("y", [], [("MI", 0, 128)], T.MI[:, 0:128], T.ml[:, :])
+    dma("y", [], ["WI"], T.WI[:, :], T.w[:, :])
+    dma("y", [], [("MI", 128, 256)], T.MI[:, 128:256], T.mr[:, :])
+    dma("y", [], [("H0", 0, L)], T.H0[:, 0:L], T.x[:, :])
+    dma("y", [], [("KI", 192, 384)], T.KI[:, 192:384], T.kids[:, 192:384])
+    zero("MAT", 0, 144 * 8)
+    paint(mat("Z1"), SIZE, 15, 1.0)
     select(IDN, ones, [[-1, 128]], A.is_equal, 0.0, 0, 1)
     iota(whole("OWN"), [[1, RUN]], 16 + CODE, 0)
-    iota(whole("B72"), [[0, 640]], int(BASE), 0)
-    iota(("MAT", 0, EARLY), [[0, EARLY]], 0, 0)
-    paint(mat("Z1"), SIZE, 15, 1.0)
+    select(mat("DM1"), mat("DM1"), [[-16, 8], [1, 4], [0, 4]], A.not_equal, 1.0, -11, 1)
     for i, (pattern, base) in enumerate((([[0, 8], [1, 4], [0, 4]], -2), ([[0, 8], [1, 4], [0, 4]], -3),
                                          ([[0, 32], [1, 2], [0, 2]], 0), ([[0, 32], [1, 2], [0, 2]], -1))):
         select(ym(i), IDN, pattern, A.is_equal, 0.0, base, 0)
-        if i != 2:
-            paint(ym(i), SIZE, SIZE, 1.0)
-    select(mat("DM1"), mat("DM1"), [[-16, 8], [1, 4], [0, 4]], A.not_equal, 1.0, -11, 1)
-    paint(mat("DQZ"), SIZE, 15, 256.0)
-    paint(ym(2), SIZE, D2R, 1.0)
-    paint(ym(3), START, START, 0.0)
-    paint(ym(3), SIZE, D2L, 1.0)
-    paint(mat("NR2"), EVEN, D2L, -1.0)
-    paint(mat("NR2"), ODD, D2R, -1.0)
+    for i, src, dst, c in ((0, SIZE, SIZE, 1.0), (1, SIZE, SIZE, 1.0), (3, SIZE, SIZE, 1.0), (2, SIZE, D2R, 1.0), (3, START, START, 0.0)):
+        paint(ym(i), src, dst, c)
     iota(("F", RUN, RUN + 8), [[0, 8]], -8, 0)
-    select(whole("TRS"), BLK, [[1, 128]], A.is_gt, 0.0, 0, -1)
-    for m, row in (("S3L", D3R), ("S3R", D3L)):
-        paint(mat(m), SIZE, row, 1.0)
-        paint(mat(m), SIZE, START, -256.0)
-    paint(mat("ST"), START, START, -1.0)
-    paint(mat("NR3"), EVEN, D3L, -1.0)
-    paint(mat("NR3"), ODD, D3R, -1.0)
-    select(TRI, BLK, [[-1, 128]], A.is_ge, 0.0, 0, 1)
-    iota(("MAT", EARLY, 144 * len(MATS)), [[0, 144 * len(MATS) - EARLY]], 0, 0)
-    select(mat("X1L"), mat("X1L"), [[-16, 8], [1000, 4], [0, 4]], A.not_equal, 1.0, -3000, 1)
-    select(mat("X1R"), mat("X1R"), [[-16, 8], [1000, 4], [0, 4]], A.not_equal, 1.0, -2000, 1)
-    paint(mat("BI2"), SIZE, D2R, -1.0)
-    iota(whole("EQ"), [[0, 16 * 128]], 0, 0)
-    select(("EQ", START, 16 * 128, 16), ("EQ", START, 16 * 128, 16), [[-1, 16], [-16, 8]], A.not_equal, 1.0, 0, 1)
-    select(mat("BI3"), mat("BI3"), [[-16, 8], [0, 16]], A.not_equal, -32 * BIG, 0, 1)
-    paint(mat("BI3"), SIZE, D3L, 0.0)
-    paint(mat("BI3"), SIZE, D3R, -1.0)
-    select(ym(4), IDN, [[0, 32], [1, 2], [0, 2]], A.is_equal, 0.0, 0, 0)
-    select(ym(5), IDN, [[0, 32], [1, 2], [0, 2]], A.is_equal, 0.0, -1, 0)
-    paint(ym(5), START, START, 0.0)
+    iota(whole("ONF"), [[0, 256]], 1, 0)
+    paint(mat("DQZ"), SIZE, 15, 256.0)
+    paint(ym(3), SIZE, D2L, 1.0)
+    select(TRS, BLK, [[1, 128]], A.is_gt, 0.0, 0, -1)
+    for m, src, dst, c in (("NR2", EVEN, D2L, -1.0), ("S3L", SIZE, D3R, 1.0), ("NR2", ODD, D2R, -1.0), ("S3R", SIZE, D3L, 1.0),
+                           ("S3L", SIZE, START, -256.0), ("NR3", EVEN, D3L, -1.0), ("S3R", SIZE, START, -256.0), ("NR3", ODD, D3R, -1.0)):
+        paint(mat(m), src, dst, c)
+    iota(("SZ", 0, 16 + B), [[0, 16 + B]], 1, 0)
+    select(("TRB", 0, 128), TRS, [[-1, 128]], A.not_equal, RANK + 1, 0, 1)
+    select(whole("VB"), ("ONE", 0, 256), [[-1, 16], [1, 16]], A.is_equal, 0.0, 67, -1)
+    select(whole("VA"), ones, [[0, 8], [1, 16]], A.is_equal, 0.0, 4, -1)
 
+    act(("M", 0, 512), whole("ONE"), AF.Silu, BASE)
+    ts(("PI", 6, 7), ("PI", 0, 1), 13, A.bitwise_and)
+    lin("v", ("M", 1024, 1536), whole("ONE"), BASE)
+    ts(R, ("PI", 0, 1), 15, A.bitwise_and)
     for j, bit in enumerate((0, 2, 1, 3)):
         ts(("PI", 1 + j, 2 + j), ("PI", 0, 1), bit, A.arith_shift_right, 1, A.bitwise_and)
-    ts(R, ("PI", 0, 1), 15, A.bitwise_and)
-    ts(("PI", 6, 7), ("PI", 0, 1), 13, A.bitwise_and)
-    copy("v", co(BF, 4), ("PI", 1, 5))
+    ts(co(I0, 5), ("STEP", 0, 5), float(B), A.mult, CODE + 16 - BASE, A.add)
     ts(co(E0), R, float(SIZE), A.is_equal)
-    fill(CN, -1 / 32)
-    ts(whole("STEP"), ("ONE", 0, B), co(E0), A.mult)
-    ts(co(I0), co(E0), CODE + 15 - BASE, A.mult, BASE, A.add)
+    lin("v", ("M", 512, 1024), whole("ONE"), BASE)
     ts(co(SS + 3), ("PI", 6, 7), 1.0, A.is_equal, TURN, A.mult)
-    act(("M0", 0, 512), whole("ONE"), AF.Silu, BASE)
-    tt(co(SS + 2), co(BF + 3), co(BF + 1), A.max)
-    own(0)
-    lin("s", ("M0", 1536, 2048), whole("ONE"), BASE)
+    ts(co(I0, 5), co(I0, 5), co(E0), A.mult, BASE, A.add)
+    own(2, "s")
     ts(co(U, 4), ("PI", 1, 5), 2.0, A.mult, -1.0, A.add)
-    lin("s", ("M0", 512, 1024), whole("ONE"), BASE)
-    lin("s", co(SS, 2), co(BF, 2), 0.0, co(BF + 3))
-    ts(co(RF), R, float(RUN), A.mult)
-    own(1)
     lin("s", co(AT + 3), co(SS + 3), co(U + 2))
+    own(0, "s")
+    lin("s", co(E1), co(E0), 1 / 256)
+    copy("v", co(BF, 4), ("PI", 1, 5))
+    own(1, "s")
+    lin("v", ("M", 1536, 2048), whole("ONE"), BASE)
+    fill(CN, -1 / 32)
+    lin("v", ("MM", 0, 256), whole("MI"), 0.25)
+    own(3, "v")
     lists(0)
-    own(2)
-    lin("v", ("SGB", 0, 128, 2), ("BLS", 0, 128, 2), -1 / 16)
-    lin("s", ("M0", 1024, 1536), whole("ONE"), BASE)
-    own(3)
-    lin("s", ("SGB", 1, 128, 2), ("BLS", 1, 128, 2), 1 / 16)
+    lin("v", co(I0 + 4), co(I0 + 4), 1.0, co(AT + 3))
+    lin("v", co(LO), co(E0), 2 / 256)
 
-    hand(0, 3, 0, "s")
-    lin("v", co(A3), co(E0), float(B), co(AT + 3))
-    lin("s", co(LO), co(E0), 2 / 256)
-    ts(co(E2), R, float(START), A.is_equal, BIG, A.mult)
-    ts(whole("OWH"), whole("OWN"), co(RF), A.add, 0.5, A.add)
-    tt(co(VV, 3), co(SS, 3), co(U, 3), A.mult)
-    lin("v", node("M0", 4), node("M0", 3), 1.0, co(A3))
-    tab_lists(0)
-    tie_break()
-    hand(0, 3, 1, "s")
-    lin("s", co(HT), co(BF + 3), 1 / 256, co(LO))
-    ts(co(Z0), R, float(SIZE), A.not_equal)
-    lin("s", co(CR), co(U), -1 / 32)
-    gather(0, 0, 0, 0, "v")
-    gather(0, 0, 0, 1, "v")
-    lin("v", whole("MM"), whole("MI"), 0.25)
-    gather(0, 0, 1, 0, "v")
-    sums(0, 0)
-    lin("s", co(AT + 1, 2), co(VV + 1, 2), TURN)
-    lin("s", co(AT), co(VV), -TURN)
-    lin("s", co(HC), co(HT), 1.0, co(E2))
-    ts(whole("WP"), whole("SGB"), whole("WI"), A.mult)
+    hand(3, 0, "v")
+    own(4, "s")
+    gather(0, 0, 0, 0, "s")
+    gather(0, 0, 0, 1, "s")
+    lin("s", co(SS, 2), co(BF, 2), 0.0, co(BF + 3))
+    lin("s", ("SGB", 0, 128, 2), ("BLS", 0, 128, 2), -1 / 16)
+    gather(0, 0, 1, 0, "s")
+    hand(3, 1, "s")
+    zero("MAT", 144 * 8, 144 * len(MATS))
     gather(0, 0, 1, 1, "v")
-    lin("s", ("TAB", 0, 16), ("STEP", 0, 16), 1 / 256)
-    ts(co(Z2), R, float(START), A.not_equal, 256 / MASK, A.mult)
-    lin("v", whole("WN"), whole("WP"), -1.0)
     sums(0, 1)
-    turn(0, 2, "s")
-    lin("s", whole("OWN"), whole("OWN"), 1.0, co(RF))
-    floor(0)
+    tt(co(SS + 2), co(BF + 3), co(BF + 1), A.max)
+    lin("v", ("SGB", 1, 128, 2), ("BLS", 1, 128, 2), 1 / 16)
+    ts(("KS", 48, 192), ki(0, 48, 192), float(CUT), A.subtract)
+    ts(whole("WP0"), whole("SGB"), whole("WI"), A.mult)
+    tt(co(VV, 3), co(SS, 3), co(U, 3), A.mult)
     floor(1)
-    diff(0, "b2", False)
-    clamp(0, 0, 0)
-    node_sizes(0)
-    clamp(0, 0, 1)
-    gather(0, 1, 0, 0, "s")
-    hand(0, 2, 0, "v")
-    gather(0, 1, 0, 1, "v")
-    gather(0, 1, 1, 0, "s")
-    gather(0, 1, 1, 1, "s")
-    store0()
-    sums(1, 0)
-    floor(0)
-    hand(0, 2, 1, "s")
-    rows(0, 1, 0, "v")
-    sums(1, 1)
-    floor(1)
-    diff(1, "b7")
-    rows(0, 1, 1, "s")
-    clamp(0, 1, 0)
-    lin("s", co(WG), whole("WI"), -1 / 16)
-    relu("s", rg(1), bank("b7"), co(CR))
-    clamp(0, 1, 1)
-    others1("b2")
-    pick(1, "b3", True)
-    hand(0, 1, 0, "v")
-    relu("s", co(AP, 4), co(AT, 4))
-    tt(whole("DG"), rg(1), bank("b2"), A.min)
-    mm(bank("b3"), mat("DM1"), whole("DG"), False, True)
-    turn(0, 1, "s")
-    gather(0, 2, 1, 0, "v")
-    gather(0, 2, 0, 0, "s")
-    hand(0, 1, 1, "s")
-    gather(0, 2, 0, 1, "v")
-    gather(0, 2, 1, 1, "v")
-    ts(("INC", 0, 1), co(E0), 0.0, A.mult)
-    copy("s", node("TAB", 1), bank("b3"))
-    ts(co(WS), co(Z2), 1 / MASK, A.max, co(Z0), A.mult)
-    reduce(co(TS), co(AP, 4), A.add)
-    sums(2, 0)
-    turn(0, 0, "s")
-    rows(0, 2, 0, "s")
-    for c in range(0, EDGE, 640):
-        dma("y", ["B72"], [("M1", c, c + 640)], T.M1[:, c:c + 640], T.B72[:, :])
-    sums(2, 1)
-    floor(0)
-    diff(2, "b7")
-    rows(0, 2, 1, "s")
-    node_sizes(1)
-    floor(1)
-    relu("s", rg(2), bank("b7"), co(CR))
-    pick(2, "b4", True)
-    node_codes(0)
-    clamp(0, 2, 0)
-    hand(0, 0, 0, "v")
-    lin("s", co(TB), co(TS), -1.0, MASK - BASE)
-    clamp(0, 2, 1)
-    mm(bank("b4"), mat("NR2"), rg(2), False, True)
-    node_sizes(2)
-    gather(0, 3, 1, 0, "s")
-    hand(0, 0, 1, "v")
-    node_flags()
-    relu("s", node("TAB", 2), bank("b4"))
-    gather(0, 3, 0, 1, "v")
-    gather(0, 3, 1, 1, "v")
-    lin("v", co(NB), co(TB), co(Z0))
-    gather(0, 3, 0, 0, "s")
-    rows(0, 3, 0, "s")
-    root_sizes()
-    root_leaves()
-    diff(3, "b7")
-    run_sums()
-    narrow(0, 0)
-    node_starts(0)
-    dma("y", ["OWN"], [("M1", L, EDGE)], T.M1[SIZE:128:16, L:EDGE], T.OWN[:, :])
-    rows(0, 3, 1, "s")
-    edge_sizes("b5", False)
-    lists(1)
-    rows(0, 3, 1, "s", edge(1))
-    rows(0, 3, 0, "s", edge(0))
-    dma("y", ["RL0"], [("TAB", 16, 16 + N3)], T.TAB[START:128:16, 16:16 + N3], T.RL0[:, :])
-    edge_sums(0)
-    column(mat("DQS"), 15, co(WS))
-    narrow(0, 1)
-    relu("s", rg(3), bank("b7"), co(CR))
-    tab_lists(1)
-    leaf_codes("b2", 0)
-    edge_starts(0)
-    hand(1, 3, 0, "s")
-    mm(bank("b5"), mat("NR3"), rg(3), False, True)
-    ts(co(BH), R, float(D2L), A.not_equal, BIG, A.mult)
-    edge_store(0, "b5")
-    ts(co(BG), R, float(D2R), A.not_equal, co(BH), A.mult)
-    lin("v", whole("SD1"), IDN, co(VV + 1))
-    leaf_codes("b4", 1)
-    edge_store(1, "b5")
-    leaf_list(0, "b2", 0)
-    leaf_list(0, "b4", 1)
-    node_sizes(0)
-    mm(bank("b3"), mat("ZM"), CN, True, False)
-    lin("s", co(NCR), co(U + 1), -1 / 32)
-    leaf_flag("b2", 0, 64)
-    leaf_flags("b4", 64)
-
-    sum_up(0, 0)
-    hand(1, 3, 1, "s")
-    leaf_starts(0, "b4", 0)
-    rows(1, 1, 0, "s")
-    turn(1, 2, "s")
-    hand(1, 2, 0, "s")
-    leaf_starts(0, "b4", 1)
-    leaf_starts(0, "b4", 2)
-    lin("s", co(WF), whole("WI"), 1 / 16)
-    hand(1, 2, 1, "s")
-    mm(bank("b4", 128), BLK, whole("SD1"), True, True)
-    rows(1, 1, 1, "s")
-    add_roots(0, 0)
-    lin("s", whole("WP1"), bank("b4", 128), co(WG))
-    hand(1, 1, 0, "s")
-    sizes(1)
-    sum_up(0, 1)
-    mm(bank("b2"), mat("X1L"), sr(1, 0), True, False)
-    add_roots(0, 1)
-    lin("s", whole("WN1"), bank("b4", 128), co(WF))
-    copy("s", node("TAB", 1), bank("b7"))
-    places(0, 0)
-    turn(1, 1, "s")
-    rows(1, 2, 0, "s")
-    node_sizes(1)
-    hand(1, 1, 1, "s")
-    places(0, 1)
-    rows(1, 2, 1, "s")
-    mm(bank("b4"), mat("Z1", D2R), sr(2, 0), True, False)
-    node_sizes(2)
-    node_codes(1)
-    exchange(0)
-    hand(1, 0, 0, "s")
-    sizes(2)
-    mm(bank("b4"), mat("Z1", D2L), sr(2, 1), False, True)
-    node_flags()
-    mm(bank("b2"), mat("X1R"), sr(1, 1), False, True)
-    copy("v", node("TAB", 2), bank("b7"))
-    turn(1, 0, "s")
-    lin("s", whole("XB2"), bank("b4"), 1.0, co(BG))
-    mm(bank("b4"), mat("BI2"), CN, True, False)
-    hand(1, 0, 1, "s")
-    root_sizes()
-    rows(1, 3, 0, "v")
-    run_sums()
-    root_leaves()
-    rows(1, 3, 1, "v")
-    column(mat("WN2"), D2L, co(WG))
-    node_starts(1)
-    edge_sizes("b0", True)
-    edge_sizes("b5", False)
-    narrow(1, 0)
-    lin("s", whole("XS"), bank("b2"), 1.0, co(NCR))
-    narrow(1, 1)
-    edge_sums(1)
-    start_rows("b3", 1)
-    start_rows("b4", 2)
-    lin("v", co(C1), co(U + 1), 1 / 32)
-    column(mat("WP2"), D2L, co(WF))
-    tie_break()
-    leaf_codes("b6", 0)
-    leaf_codes("b6", 1)
-    edge_starts(1)
-
-    gather(1, 0, 1, 0, "s")
-    leaf_list(1, "b6", 0)
-    leaf_list(1, "b6", 1)
-    start_rows("b2", 0)
-    gather(1, 0, 1, 1, "s")
-    leaf_flags("b6")
-    gather(1, 0, 0, 0, "v")
-    gather(1, 0, 0, 1, "v")
-    leaf_starts(1, "b6", 0)
-    column(mat("WN2"), D2R, co(WF))
-    copy("s", whole("XB3"), bank("b5"))
     sums(0, 0)
+    lin("v", whole("WN0"), whole("WP0"), -1.0)
+    lin("v", co(HT), co(BF + 3), 1 / 256, co(LO))
+    ts(co(E2), R, float(START), A.is_equal, BIG, A.mult)
     floor(0)
-    sums(0, 1)
-    clamp(1, 0, 0)
-    floor(1)
-    diff(0, "b2", False)
-    column(mat("WP3"), D3L, co(WF))
-    mm(bank("b5"), mat("BI3"), CN, True, False)
-    clamp(1, 0, 1)
-    gather(1, 1, 0, 0, "v")
-    store0()
-    gather(1, 1, 1, 0, "s")
-    gather(1, 1, 0, 1, "s")
+    lin("v", co(AT + 1, 2), co(VV + 1, 2), TURN)
+    lin("v", co(AT), co(VV), -TURN)
+    lin("v", co(HC), co(HT), 1.0, co(E2))
+    clamp(0, 0, 0)
+    clamp(0, 0, 1)
+    hand(2, 0, "v")
+    lin("s", ("TAB", 0, 16), ("ONE", 0, 16), co(E1))
+    lin("s", co(CR), co(U), -1 / 32)
+    turn(2, "s")
+    mm(bank("b2"), whole("SGB"), CN, True, False)
+    diff(0, "b2")
+    ts(node("TAB", 0), bank("b2"), co(LO), A.max, co(HC), A.min)
+    hand(2, 1, "v")
+    gather(0, 1, 1, 0, "s")
+    gather(0, 1, 0, 0, "s")
+    node_sizes(0)
     sums(1, 0)
-    gather(1, 1, 1, 1, "v")
+    gather(0, 1, 0, 1, "s")
+    gather(0, 1, 1, 1, "s")
+    diff(1, "b7")
+    rows(1, 0, "s")
+    relu("s", rg(1), bank("b7"), None, co(CR))
+    hand(1, 0, "s")
+    turn(1, "s")
+    rows(1, 1, "v")
+    ts(co(RF), R, float(RUN), A.mult)
+    ts(whole("OWH"), whole("OWN"), co(RF), A.add, 0.5, A.add)
+    floor(0)
     sums(1, 1)
-    leaf_starts(1, "b6", 1)
-    floor(0)
-    leaf_starts(1, "b6", 2)
+    ts(co(Z0), R, float(SIZE), A.not_equal)
     floor(1)
-    clamp(1, 1, 0)
-    rows(1, 1, 0, "s")
-    rows(1, 1, 1, "s")
-    mm(bank("b7"), whole("WN1"), vec(1, 0), True, False)
-    clamp(1, 1, 1)
-    mm(bank("b7"), whole("WP1"), vec(1, 1), False, True)
-    tt(whole("XS"), bank("b7"), whole("XS"), A.min)
-    gather(1, 2, 0, 1, "v")
-    pick(1, "b3", False, True)
-    gather(1, 2, 0, 0, "s")
-    relu("v", whole("DG"), whole("XS"), co(C1))
-    tt(node("TAB", 1), whole("DG"), bank("b3"), A.add)
-    gather(1, 2, 1, 0, "s")
-    sums(2, 0)
-    gather(1, 2, 1, 1, "s")
+    clamp(0, 1, 0)
+    lin("v", co(NC), co(BF + 2), -1.0, 1.0)
+    relu("v", co(AP, 4), co(AT, 4))
+    mm(bank("b2"), mat("Z1", EVEN), sr(1, 0), True, False)
+    mm(bank("b2"), mat("Z1", ODD), sr(1, 1), False, True)
+    clamp(0, 1, 1)
+    tt(whole("DG"), rg(1), bank("b2"), A.min)
+    reduce(co(TS), co(AP, 4), A.add)
+    gather(0, 2, 1, 1, "s")
+    lin("s", co(TB), co(TS), -1.0, MASK - BASE)
+    hand(1, 1, "s")
+    dma("y", [("M", L, EDGE)], ["NCO"], T.NCO[:, :], T.M[SIZE:128:16, L:EDGE])
+    dma("y", ["ONF"], ["FS"], T.FS[0:128:16, :], T.ONF[:, :])
+    zero("EQ", 0, 16 + 16 * 128)
+
+    select(("EQ", 16, 16 + 16 * 128, 16), ("EQ", 16, 16 + 16 * 128, 16), [[-1, 16], [-16, 8]], A.not_equal, 1.0, 0, 1)
+    select(TRI, BLK, [[-1, 128]], A.is_ge, 0.0, 0, 1)
+    iota(whole("ZF"), [[0, K]], 0, 0)
+    iota(("SCN", 0, 4), [[0, 4]], 0, 0)
+    for j, (blk, src, d, c) in enumerate(((0, 4, 1, LOW), (1, 35, -1, HIGH), (2, 36, 1, HIGH), (3, 67, -1, LOW),
+                                          (0, 100, 1, HIGH), (1, 67, -1, LOW), (2, 4, 1, LOW), (3, 99, -1, HIGH))):
+        diagonal("LA", blk, src, d, c / 2)
+        if j < 2:
+            diagonal("LN", j, (4, 35)[j], 1 - 2 * j, LOW)
+    second_view()
+    for j, (m, src, dst, c) in enumerate((("TB", 0, 1, 1.0), ("TB", 1, 2, 1.0), ("TB", 2, 2, 1.0), ("TB", 3, 3, 1.0), ("TB", 2, 1, -1.0),
+                                          ("TA", 0, 0, 1.0), ("TB", 3, 2, -1.0), ("TA", 1, 1, 1.0))):
+        x = (mat(m, 7)[0], mat(m, 7)[1] + dst, mat(m, 7)[2], 4)
+        select(x, x, [[-16, 8], [1000, 2], [-4, 2]], A.not_equal, c, -src, 1)
+        m, src, dst, c = (("UL", 0, 2, 1.0), ("UR", 0, 2, 8.0), ("SL", 0, 2, -1.0), ("SL", 0, 3, 1.0), ("SL", 1, 1, 1.0), ("SR", 0, 2, -8.0),
+                          ("SR", 0, 3, 1.0), ("SC", 0, 0, -1.0))[j]
+        paint(mat(m), src, dst, c)
+    for h in range(2):
+        select(("VC", 512 * h, 512 * h + 512), whole("ONE"), [[-1, 4], [0, 8], [1, 16]], A.is_equal, 0.0, 99 - 4 * h, -1)
+    select(whole("DUP"), ones, [[-16, 8], [0, 2], [-1, 8]], A.is_equal, 0.0, 0, 1)
+    for j in range(2):
+        x = (mat("M0")[0], mat("M0")[1] + j, mat("M0")[2], 2)
+        select(x, x, [[-16, 8], [2 * j - 1, 2], [0, 4]], A.not_equal, 0.5, -1 - j, 1)
+        select(mat("M2", 7), mat("M2", 7), [[-16, 8], [1000, 2], [-1, 8]], A.not_equal, 2.0, -8 * j, 1)
+    select(("TRB", 128, 256), TRI, [[-1, 128]], A.not_equal, -RANK, 0, 1)
+
+    gather(0, 2, 0, 1, "v")
+    gather(0, 2, 0, 0, "v")
+    gather(0, 2, 1, 0, "v")
+    pick(1, "b3")
+    mm(bank("b3"), mat("DM1"), whole("DG"), False, True)
     sums(2, 1)
-    floor(0)
-    mm(bank("b4"), mat("WN2"), vec(2, 0), False, False)
-    column(mat("WP3"), D3R, co(WG))
+    node_sizes(1)
+    sums(2, 0)
+    column("v", "SS", 2, -1.0)
     floor(1)
-    column(mat("WP2"), D2R, co(WG))
+    turn(0, "v")
+    copy("v", node("TAB", 1), bank("b3"))
+    flag_lists(1, 0)
+    rows(2, 0, "v")
+    tt(("F", 0, RUN), whole("NCO"), whole("OWH"), A.is_lt)
+    clamp(0, 2, 1)
+    floor(0)
+    lin("s", co(MB), co(TB), co(Z0))
+    hand(0, 0, "s")
+    rows(2, 1, "s")
+    diff(2, "b7")
+    node_sizes(2)
+    pick(2, "b4")
+    mm(bank("b5", RUN + 1), BLK, ("F", 0, RUN + 1))
+    ts(("INC", 0, 1), co(E0), 0.0, A.mult)
+    clamp(0, 2, 0)
+    flag_lists(1, 1)
+    ts(co(WA), whole("WI"), -2.0, A.mult)
+    tt(whole("RS"), ("F", 0, RUN), bank("b6", RUN), A.mult)
+    gather(0, 3, 0, 0, "v")
+    ts(co(TN), co(U + 3), co(U + 1), A.mult, 2048.0, A.mult)
+    scan(("INC", 1, RUN + 1), whole("RS"), whole("RS"), A.max)
+    gather(0, 3, 1, 0, "d")
+    hand(0, 1, "s")
+    relu("s", rg(2), bank("b7"), None, co(CR))
+    gather(0, 3, 0, 1, "s")
+    gather(0, 3, 1, 1, "d")
+    mm(bank("b4"), mat("NR2"), rg(2), False, True)
+    relu("v", node("TAB", 2), bank("b4"))
+    reduce(("OFS", 0, 1), bank("b5", RUN + 1), A.add, True)
+    ts(co(Z2), R, float(START), A.not_equal, 256 / MASK, A.mult)
+    ts(whole("KF"), ki(1, 0, 48), 1.0, A.mult)
+    narrow(1, "s")
+    rows(3, 0, "s")
+    mm(bank("b6", 1, 300), TRS, ("INC", RUN, RUN + 1))
+    mm(bank("b6", 1, 301), BLK, ("INC", RUN, RUN + 1))
+    diff(3, "b7", 1)
+    leaf_codes("b4", 1)
+    mm(bank("b5"), mat("S3L"), sr(3, 0), True, False)
+    ts(whole("RL"), ("INC", 0, RUN), bank("b6", 1, 300), A.add, ("OFS", 0, 1), A.add)
+    ts(co(WS), co(Z2), 1 / MASK, A.max, co(Z0), A.mult)
+    ts(co(WB), whole("WI"), 2.0, A.mult)
+    rows(3, 1, "v")
+    mm(bank("b5"), mat("S3R"), sr(3, 1), False, False)
+    ts(("OFS", 1, 2), bank("b6", 1, 301), ("OFS", 0, 1), A.add, 1 / 256, A.mult)
+    leaf_list("b4", 1)
+    flag_lists(1, 2)
+    scan(whole("IX"), sr(3, 0), sr(3, 1), A.add, ("OFS", 1, 2))
+    mm(bank("b5"), mat("DQZ", START), whole("IX"), False, False)
+    relu("v", rg(3), bank("b7"), None, co(CR))
+    mm(bank("b5"), mat("NR3"), rg(3), False, True)
+    ts(co(RW), R, 1.0, A.mult)
+    ts(("PI", 7, 8), ("PI", 0, 1), 4, A.arith_shift_right)
+    ts(co(RH), ("PI", 7, 8), float(L), A.mult)
+    ts(co(E1), R, 1.0, A.is_equal)
+    level1_sizes(1)
+    edge_store(0, "b5")
+    ts(("CP", 0, 1), co(E1), 0.0, A.mult)
+    edge_store(1, "b5")
+    leaf_flag("b4", 1)
+    column("s", "US", 2, 1.0)
+    narrow(0, "s")
+    leaf_codes("b2", 0)
+    column("v", "SUM", 15, 128.0)
+    leaf_list("b2", 0)
+    double("v", "LN", 8)
+    leaf_flag("b2", 0)
+    to_rows("b3", 0)
+    mm(bank("b4", 128, 128), BLK, whole("FL"))
+    mm(bank("b4", 128, 256), TRI, whole("FL"))
+    to_rows("b5", 1)
+    dma("y", ["RL"], [("TAB", 16, 16 + N3)], T.TAB[START:128:16, 16:16 + N3], T.RL[:, :])
+
+    sum_up(0)
+    column("v", "DQS", 15, co(WS))
+    summed(0)
+    scan(whole("IL"), bank("b4", 128, 128), whole("FL"), A.max)
+    tt(whole("IL"), whole("IL"), bank("b4", 128, 256), A.subtract)
+    tt(whole("RM"), whole("IL"), whole("FL"), A.mult)
+    add_roots(0)
+    ts(whole("KZ"), ki(1, 96, 192), float(CUT), A.subtract)
+    sum_up(1)
+    places(0, 0)
+    flags(0)
+    flags(1)
+    column("s", "SS", 3, 1.0)
+    lin("s", co(RN), co(RW), -1.0)
+    ts(whole("BJ"), whole("BJ"), co(RW), A.add, 0.5, A.add)
+    double("v", "LA", 16)
+    column("v", "SP", 1, co(RN))
+    places(0, 1)
+    places(0, 2)
+    scatter(0, 32)
+    to_rows("b5", 2)
+    summed(1)
+    add_roots(1)
+    places(1, 0)
+    scatter(32, 64)
+    flags(2)
+    zero("WD", 0, L)
+    dma("y", ["S0"], [sz(0)], T.SZ[0:128:16, 16:16 + B], T.S0[:, 0:24])
+    zero("TI", 0, L, "ZF")
+    zero("TI", V1, V1 + L, "ZF")
+    views()
+    lin("s", sz(1), bank("b3"), co(E0), co(E1))
+    kid_sizes(2, "s")
+    copy("s", whole("LR"), bank("b5"))
+    lin("s", co(TH), co(TN), -1.0)
+    double("s", "LN", 16)
+    double("s", "LN", 32)
+    lin("s", whole("NG"), IDN, co(TN))
+    double("s", "LN", 64)
+    flags(3)
+    dma("y", ["FS"], ["FB"], T.FB[:, :], T.FS[0:128:16, :])
+    places(1, 1)
+    double("v", "LA", 32)
+    places(1, 2)
+    scatter(64, 96)
+    column("v", "UP", 1, co(RW))
+    scatter(96, 128)
+    exchange()
+    iota(("CC", 128, 144), [[0, 16]], NB, 0)
+    iota(whole("CT"), [[1, 208]], 0, 0)
+    select(("IM", 128, 256), IDN, [[-1, 128]], A.not_equal, 48.0, 0, 1)
+    iota(("MT", 0, 17), [[0, 17]], 0, 0)
+    iota(("SZB", 0, 128), [[0, 128]], 1, 0)
+    iota(("SZB", 128, 152), [[0, 24]], 2, 0)
+    iota(whole("RAMP"), [[1, 128]], 0, 128)
+    iota(whole("JJ"), [[1, 128]], int(RANK) + 1, 0)
+    paint(mat("Z3"), 3, 15, 1.0)
+    select(("IM", 0, 128), IDN, [[-1, 128]], A.not_equal, -63.0, 0, 1)
+    for j, c in enumerate((32768.0, 2048.0, 16.0, -1.0)):
+        paint(mat("EX"), j, 15, c)
+    iota(("MT", 1169, 1184), [[0, 15]], 0, 0)
+
+    mm(bank("b7"), mat("Z1", SIZE), ("SG", 0, B), True, False)
+    mm(bank("b7"), mat("Z1", SIZE), ("SG", B, K), False, True)
+    merging("b2")
+    lin("s", sz(2), bank("b7"), co(E0), co(E1))
+    copy("s", whole("MG"), bank("b2", 256))
+    extract("b4", "Z1", sz(2), 24)
+    double("s", "LA", 64)
+    mm(bank("b0", 512), whole("LA"), ("VC", 0, 512))
+    mm(bank("b2", 128), whole("LN"), whole("VA"))
+    kid_sizes(3, "s")
+    mm(bank("b5"), mat("M0"), whole("LR"))
+    scan(("CP", 1, NB + 1), ("FB", 0, NB), ("FB", 0, NB), A.max)
+    lists(1)
+    level1_lists(1)
+    tt(("MM", 256, 384), ("MM", 0, 128), ("MM", 128, 256), A.add)
+    ranks("b6", "b3")
+    mm(bank("b1", 512), whole("LA"), ("VC", 512, 1024))
+    copy("v", ("RK", 0, NB), bank("b3", NB))
+    copy("v", ("MT", 17, 145), bank("b2", 128))
+    copy("v", ("MT", 145, 657), bank("b0", 512))
+    steps("b7", 0)
+    mm(bank("b2"), whole("NG"), ("ONE", 0, B), True, False)
+    copy("v", ("SZB", 176, 200), bank("b4", 24))
+    copy("v", ("MT", 657, 1169), bank("b1", 512))
+    mm(bank("b3", 128), BLK, whole("NG"))
+    count("b6", 0, 4)
+    count("b6", 4, 8)
+    ts(whole("CL"), whole("CA"), 0.5, A.mult, NB / 2, A.add)
+    tt(whole("OH"), ("RK", 0, NB, "CL", 0, 8), whole("JJ"), A.is_equal)
+    ts(whole("RAMP"), whole("RAMP"), co(RH), A.subtract, 0.5, A.mult)
+    copy("s", ("CC", 0, 128), ("CT", 0, NB, "CL", 0, 8))
+    steps("b7", 1)
+    steps("b7", 2)
+    tt(whole("SO"), ("SZB", 0, NB, "CL", 0, 8), whole("OH"), A.mult)
+    steps("b7", 3)
+    lin("s", whole("WP"), bank("b3", 128), co(WA))
+    lin("v", whole("WN"), bank("b3", 128), co(WB))
+
+    gather(1, 0, 1, 1, "v")
+    gather(1, 0, 0, 1, "s")
+    gather(1, 0, 0, 0, "s")
+    gather(1, 0, 1, 0, "v")
+    sums(0, 1)
+    copy("s", whole("DS"), bank("b7", 512))
+    sums(0, 0)
+    floor(1)
+    copy("s", whole("X0"), bank("b5"))
+    signs(0, "b2")
+    floor(0)
+    clamp(1, 0, 1)
+    scan(whole("SV"), whole("DS"), ("ZB", 0, 512))
+    clamp(1, 0, 0)
+    extract("b4", "Z3", ("SV", 0), 32)
+    gather(1, 1, 0, 0, "s")
+    gather(1, 1, 0, 1, "s")
+    ramps(0, (0, 2, 4, 6))
+    ramps(1, (0, 4))
+    copy("s", ("TRF", 0, 128), TRS)
+    relu("v", ("TRF", 128, 256), ("TRB", 128, 256))
+    tt(ti(0, 0), bank("b2"), whole("X0"), A.min)
+    relu("s", ti(0), ti(0, 0), co(NC))
+    ids(1, 1, 0, 1, "s")
+    gather(1, 1, 1, 0, "d")
+    sums(1, 0, 1)
+    spots("b4", 0)
+    spots("b4", 1)
+    gather(1, 1, 1, 1, "d")
+    sums(1, 1, 1)
+    signs(1, "b7", 1)
+    spots("b4", 2)
+    ids(1, 1, 0, 0, "v")
+    ids(1, 1, 1, 0, "s")
+    merge(1, 0, "b3", 0)
+    merge(1, 1, "b3", 0)
+    merge(1, 0, "b5", 1)
+    ids(1, 1, 1, 1, "s")
+    merge(1, 1, "b5", 1)
+    drop()
+    relu("s", rg(1), bank("b7"), None, co(TN))
+    floor(1)
+    keep(1, "b3", 0)
+    floor(0)
+    clamp(1, 1, 1)
+    keep(1, "b5", 1)
+    dropped("b6", 0, 4)
+    ids(1, 2, 0, 1, "s")
+    clamp(1, 1, 0)
+    dropped("b6", 4, 8)
+    gather(1, 2, 0, 0, "v")
+    gather(1, 2, 0, 1, "s")
+    ids(1, 2, 1, 1, "s")
+    ids(1, 2, 0, 0, "s")
+    gather(1, 2, 1, 0, "d")
+    dropped("b6", 8, 12)
+    merge(2, 0, "b5", 1)
+    gather(1, 2, 1, 1, "d")
+    sums(2, 0, 1)
+    signs(2, "b2", 1)
+    floor(0)
+    ids(1, 2, 1, 0, "v")
+    sums(2, 1, 1)
+    relu("s", rg(2), bank("b2"), None, co(TN))
+    merge(2, 1, "b5", 1)
+    floor(1)
+    keep(2, "b5", 1)
     clamp(1, 2, 0)
     clamp(1, 2, 1)
-    rows(1, 2, 1, "v")
-    rows(1, 2, 0, "s")
-    mm(bank("b4"), mat("WP2"), vec(2, 1), False, False)
-    gather(1, 3, 0, 1, "s")
-    pick(2, "b4", False, True, 2)
+    merge(2, 0, "b3", 0)
+    merge(2, 1, "b3", 0)
+    dropped("b6", 12, 16)
+    keep(2, "b3", 0)
+    gather(1, 3, 0, 1, "v")
     gather(1, 3, 0, 0, "s")
+    scan(("SCN", 4, 132), bank("b6", 128), ones)
+    before("b4")
     gather(1, 3, 1, 1, "d")
     gather(1, 3, 1, 0, "d")
-    tt(node("TAB", 2), bank("b4"), whole("XB2"), A.min)
-    rows(1, 3, 0, "s", edge(0))
-    rows(1, 3, 1, "s", edge(1))
-    mm(bank("b5"), mat("WP3"), vec(3, 1), False, True)
-    relu("s", node("TAB", 2), node("TAB", 2))
-    tt(bank("b7"), bank("b5"), whole("XB3"), A.min)
-    edge_store(0, "b7")
-    edge_store(1, "b7")
-    for k in range(2):
-        sum_up(1, k)
-        add_roots(1, k)
-    places(1, 0)
-    places(1, 1)
-    exchange(1)
-    dma("s", [("WB1", 512 * me, 512 * me + 512)], [], T.y[:, 512 * me:512 * me + 512], T.WB1[:, 512 * me:512 * me + 512])
-    for i, s in enumerate([s for s in range(4) if topo.chip(cores[s]) == topo.chip(core) and s != me] +
-                          [s for s in range(4) if topo.chip(cores[s]) != topo.chip(core)]):
-        dma("ysy"[i], [("YL", 512 * s, 512 * s + 512)], [], T.y[:, 512 * s:512 * s + 512], T.YL[:, 512 * s:512 * s + 512])
+    ids(1, 3, 0, 1, "s")
+    ids(1, 3, 1, 1, "s")
+    ids(1, 3, 1, 0, "s")
+    ids(1, 3, 0, 0, "s")
+    totals("b4")
+    merge(3, 0, "b5", 1)
+    signs(3, "b7", 1)
+    merge(3, 1, "b5", 1)
+    ts(whole("YA"), whole("YI"), L - 1, A.bitwise_and)
+    ts(whole("YB"), whole("YI"), 11, A.arith_shift_right)
+    copy("v", whole("CK"), whole("YA"))
+    ts(whole("AL"), bank("b7"), co(TH), A.is_ge, SMALL, A.max)
+    copy("v", whole("UN"), whole("YB"))
+    keep(3, "b5", 1)
+    for i in range(4):
+        masks(i, "s")
+    merge(3, 0, "b3", 0)
+    merge(3, 1, "b3", 0)
+    keep(3, "b3", 0)
+
+    choose(0)
+    chosen(0, 1, "b0")
+    choose(1)
+    choose(2)
+    leaf_at(0, 1, "b0", 0)
+    chosen(1, 2, "b1")
+    leaf_at(0, 1, "b0", 1)
+    leaf_at(0, 1, "b0", 2)
+    choose(3)
+    chosen(3, 1, "b2")
+    leaf_at(1, 2, "b1", 0)
+    fetch(0, "s")
+    leaf_at(1, 2, "b1", 1)
+    leaf_at(1, 2, "b1", 2)
+    fetch(1, "v")
+    fetch(2, "s")
+    for step in range(3):
+        leaf_at(3, 1, "b2", step)
+    fetch(3, "s")
+    for i, s in enumerate(sorted(others, key=lambda s: turns(s).index(me))):
+        dma("yys"[i], [("YL", 512 * s, 512 * s + 512)], [], T.y[:, 512 * s:512 * s + 512], T.YL[:, 512 * s:512 * s + 512])
     for sem in sorted(total):
         if known["g"].get(sem, 0) < total[sem]:
             g.wait_ge(T.sem[sem], total[sem])

from concourse.bass import DstId, RemoteDMATransfer
from concourse.mybir import dt, AluOpType, ActivationFunctionType, AxisListType

A = AluOpType
AF = ActivationFunctionType
L, NT, B, RO = 2048, 4, 384, 2
K = 2 * B
C = B // 2
N3 = 3 * B
NB = (L + N3) // 16
CUT = L - 16
V1 = L + B
RANK = 128.0
LOW, HIGH, SMALL = 2.0 ** -7, 2.0 ** 5, 2.0 ** -12
MATS = ["Z1", "DM1", "DQZ", "DQS", "NR2", "NR3", "S3L", "S3R",
        "UL", "SL", "UR", "SR", "UP", "SP", "US", "SS", "SC", "Z3", "EX", "SUM", "M0", "TA", "TB", "M2"]
EDGE = L + N3
TW = EDGE + K - CUT
BASE, TURN, MASK = 72.0, 16.0, 8.0
CODE = 96
BIG = 4096.0
RUN = N3 // 16
PART = ((0, 64), (64, 128))
SIZE, D3L, START, D3R, D2L, D2R, EVEN, ODD = 0, 1, 2, 3, 4, 6, 8, 9
U, BF, SS, VV, AT, AP = 0, 4, 8, 12, 16, 20
WS, E0, LO, Z0, Z2, E2, HC, CR, RF, HT, MB, TS, TB, E1, RW, RN, RH, TN, TH, NC, WA, WB, I0 = range(24, 47)

SCRATCH = {
    "KI": ("sbuf", [128, 384], "int32"), "K16": ("sbuf", [128, 384], "uint16"), "KS": ("sbuf", [128, 192], "uint16"),
    "KZ": ("sbuf", [128, 96], "uint16"), "M": ("sbuf", [128, EDGE + K], "float32"), "MB": ("sbuf", [128, L], "float16"),
    "PRE": ("sbuf", [128, B], "float32"), "STEP": ("sbuf", [128, B], "float32"), "S0": ("sbuf", [128, RUN], "bfloat16"),
    "NCO": ("sbuf", [128, RUN], "float32"), "OWH": ("sbuf", [128, RUN], "float32"), "RL": ("sbuf", [128, RUN], "float32"),
    "OWN": ("sbuf", [128, RUN], "float32"), "TAB": ("sbuf", [128, TW], "float32"), "YM": ("sbuf", [128, 4 * 128], "bfloat16"),
    "BLS": ("sbuf", [128, 128], "bfloat16"), "SGB": ("sbuf", [128, 128], "bfloat16"), "CN": ("sbuf", [128, B], "bfloat16"),
    "WP0": ("sbuf", [128, 128], "bfloat16"), "WN0": ("sbuf", [128, 128], "bfloat16"), "SR": ("sbuf", [128, 2 * N3], "bfloat16"),
    "DG": ("sbuf", [128, B], "bfloat16"), "F": ("sbuf", [128, RUN + 8], "bfloat16"), "RS": ("sbuf", [128, RUN], "bfloat16"),
    "OFS": ("sbuf", [128, 8], "float32"), "INC": ("sbuf", [128, RUN + 8], "float16"), "IX": ("sbuf", [128, B], "float16"),
    "PT": ("sbuf", [128, 128], "uint16"), "RM": ("sbuf", [128, 128], "float16"), "FL": ("sbuf", [128, 128], "bfloat16"),
    "IL": ("sbuf", [128, 128], "float32"), "FS": ("sbuf", [128, 4096], "float32"),
    "KA": ("sbuf", [128, 192], "int32"), "KB": ("sbuf", [128, 192], "int32"), "KP": ("sbuf", [128, 192], "uint16"),
    "KF": ("sbuf", [128, 48], "float16"), "GE": ("sbuf", [128, 48], "bfloat16"), "KT": ("sbuf", [128, 48], "float32"),
    "KU": ("sbuf", [128, 48], "int32"), "K1": ("sbuf", [128, 48], "uint16"),
    "PI": ("sbuf", [128, 8], "int32"), "CO": ("sbuf", [128, 52], "float32"),
    "ONE": ("sbuf", [128, 512], "bfloat16"), "ONF": ("sbuf", [128, 256], "float32"),
    "ZF": ("sbuf", [128, K], "float32"), "ZB": ("sbuf", [128, K], "bfloat16"),
    "MAT": ("sbuf", [128, 144 * len(MATS)], "bfloat16"), "EQ": ("sbuf", [128, 16 + 16 * 128], "bfloat16"),
    "IDN": ("sbuf", [128, 128], "bfloat16"), "BLA": ("sbuf", [128, 128], "bfloat16"), "BLK": ("sbuf", [128, 128], "bfloat16"),
    "TRI": ("sbuf", [128, 128], "bfloat16"), "TRS": ("sbuf", [128, 128], "bfloat16"), "TRB": ("sbuf", [128, 256], "bfloat16"),
    "TRF": ("sbuf", [128, 256], "float32"), "IM": ("sbuf", [128, 256], "bfloat16"), "NG": ("sbuf", [128, 128], "bfloat16"),
    "DUP": ("sbuf", [128, 128], "bfloat16"), "MG": ("sbuf", [128, 256], "bfloat16"),
    "LA": ("sbuf", [128, 128], "bfloat16"), "LN": ("sbuf", [128, 128], "bfloat16"),
    "VA": ("sbuf", [128, 128], "bfloat16"), "VB": ("sbuf", [128, 256], "bfloat16"), "VC": ("sbuf", [128, 1024], "bfloat16"),
    "MT": ("sbuf", [128, 1184], "bfloat16"), "CT": ("sbuf", [128, 208], "bfloat16"), "JJ": ("sbuf", [128, 128], "bfloat16"),
    "BJ": ("sbuf", [128, 8], "float32"), "RAMP": ("sbuf", [128, 128], "float32"),
    "MI": ("sbuf", [128, 256], "bfloat16"), "WI": ("sbuf", [128, 1], "bfloat16"), "MM": ("sbuf", [128, 384], "bfloat16"),
    "WP": ("sbuf", [128, 128], "bfloat16"), "WN": ("sbuf", [128, 128], "bfloat16"),
    "FB": ("sbuf", [128, 256], "float32"),
    "CP": ("sbuf", [128, 208], "float16"), "RK": ("sbuf", [128, 208], "bfloat16"), "JK": ("sbuf", [128, 8 * NB], "bfloat16"),
    "CA": ("sbuf", [128, 8], "float32"), "CL": ("sbuf", [128, 8], "uint16"),
    "SZ": ("sbuf", [128, 16 + N3], "bfloat16"), "SZB": ("sbuf", [128, 208], "bfloat16"), "SG": ("sbuf", [128, K], "bfloat16"),
    "OH": ("sbuf", [128, 128], "bfloat16"), "SO": ("sbuf", [128, 128], "bfloat16"), "CC": ("sbuf", [128, 144], "bfloat16"),
    "DS": ("sbuf", [128, 512], "bfloat16"), "SV": ("sbuf", [128, 512], "float16"), "AB": ("sbuf", [128, 96], "float16"),
    "PL": ("sbuf", [128, 32], "uint16"), "SCN": ("sbuf", [128, 136], "float32"), "YI": ("sbuf", [128, 128], "int32"),
    "YA": ("sbuf", [128, 128], "int32"), "YB": ("sbuf", [128, 128], "int32"),
    "UN": ("sbuf", [128, 128], "uint16"), "CK": ("sbuf", [128, 128], "uint16"), "KM": ("sbuf", [128, L], "bfloat16"),
    "LR": ("sbuf", [128, B], "float16"), "X0": ("sbuf", [128, B], "float16"),
    "TI": ("sbuf", [128, V1 + L + NT * B], "float32"), "SI": ("sbuf", [128, 2 * N3], "float16"),
    "F16": ("sbuf", [128, B], "float16"), "RG": ("sbuf", [128, N3], "bfloat16"), "AL": ("sbuf", [128, B], "bfloat16"),
    "PR": ("sbuf", [128, L], "float16"), "QA": ("sbuf", [128, 128], "int32"), "QB": ("sbuf", [128, 128], "int32"),
    "QL": ("sbuf", [128, 128], "uint16"), "YL": ("sbuf", [128, L], "bfloat16"), "WD": ("sbuf", [128, L], "bfloat16"),
}
for _t in range(NT):
    SCRATCH["G%d" % _t] = ("sbuf", [128, K], "bfloat16")
for _r in range(RO):
    SCRATCH.update({"H%d" % _r: ("sbuf", [128, L + N3], "bfloat16"), "WB%d" % _r: ("sbuf", [128, L], "bfloat16")})
for _b in range(8):
    SCRATCH["b%d" % _b] = ("psum", [128, 512], "float32")
PSUM = ["b%d" % i for i in range(8)]

SEMAPHORES = ["qv", "qs", "qp", "qg", "sent", "arr0"] + ["arr1_%d" % i for i in range(4)] + ["d%d" % i for i in range(40)]


def rank_program(g, core, T, topo):
    me = T.rank_of(core)
    if me is None:
        return
    cores = list(T.cores)
    eng = {"v": g.vector, "s": g.scalar, "p": g.tensor, "g": g, "y": g.sync}
    known = {q: {} for q in eng}
    total = {}
    acc = {}
    ndma = [0]

    def span(x):
        if isinstance(x, str):
            return x, 0, SCRATCH[x][1][1]
        return x

    def learn(q, sem, n, snap):
        k = known[q]
        if k.get(sem, 0) < n:
            k[sem] = n
        for s2, n2 in snap.items():
            if k.get(s2, 0) < n2:
                k[s2] = n2

    def sync_for(q, reads, writes):
        need = {}
        for kind, lst in (("r", reads), ("w", writes)):
            for x in lst:
                b, lo, hi = span(x)
                ps = b in PSUM
                for rk, rlo, rhi, rq, sem, n, snap in acc.get(b, []):
                    if ps:
                        if rq == q and (q == "p" or (kind == "r" and rk == "r")):
                            continue
                    elif rhi <= lo or rlo >= hi or (kind == "r" and rk == "r"):
                        continue
                    if known[q].get(sem, 0) >= n:
                        continue
                    if sem not in need or need[sem][0] < n:
                        need[sem] = (n, snap)
        for sem in sorted(need, key=lambda s: -len(need[s][1])):
            n, snap = need[sem]
            if known[q].get(sem, 0) < n:
                eng[q].wait_ge(T.sem[sem], n)
                learn(q, sem, n, snap)

    def note(q, reads, writes, sem, n):
        snap = dict(known[q])
        for kind, lst in (("r", reads), ("w", writes)):
            for x in lst:
                b, lo, hi = span(x)
                old = acc.setdefault(b, [])
                if kind == "w" and b not in PSUM:
                    old[:] = [o for o in old if not (o[1] >= lo and o[2] <= hi)]
                old.append((kind, lo, hi, q, sem, n, snap))

    def op(q, reads, writes, call):
        sync_for(q, reads, writes)
        sem = "q" + q
        total[sem] = total.get(sem, 0) + 1
        call().then_inc(T.sem[sem], 1)
        note(q, reads, writes, sem, total[sem])

    def beside(q, reads, writes, copies):
        sync_for(q, reads, writes)
        sem = "d%d" % ndma[0]
        ndma[0] += 1
        total[sem] = 16 * len(copies)
        for out, in_ in copies:
            eng[q].dma_start(out=out, in_=in_).then_inc(T.sem[sem], 16)
        note(q, reads, writes, sem, total[sem])

    def dma(q, reads, writes, out, in_):
        beside(q, reads, writes, [(out, in_)])

    V, S, P = g.vector, g.scalar, g.tensor

    def ap(x):
        if len(x) == 6:
            return T[x[0]][:, x[1]:x[2]].indirect(T[x[3]][:, x[4]:x[5]])
        return T[x[0]][:, x[1]:x[2]:x[3]] if len(x) == 4 else T[x[0]][:, x[1]:x[2]]

    def use(*xs):
        r = []
        for x in xs:
            if isinstance(x, tuple):
                r.append(x[:3])
                if len(x) == 6:
                    r.append(x[3:])
        return r

    def outs(o):
        return [o[:3]]

    def ins(o, *xs):
        return use(*xs) + ([o[3:]] if len(o) == 6 else [])

    def val(x):
        return ap(x) if isinstance(x, tuple) else x

    def co(j, n=1):
        return ("CO", j, j + n)

    def ts(o, x, s1, o0, s2=None, o1=None):
        if o1 is None:
            op("v", ins(o, x, s1), outs(o), lambda: V.tensor_scalar(ap(o), ap(x), val(s1), None, o0))
        else:
            op("v", ins(o, x, s1, s2), outs(o), lambda: V.tensor_scalar(ap(o), ap(x), val(s1), val(s2), o0, o1))

    def tt(o, x, y, o0):
        op("v", ins(o, x, y), outs(o), lambda: V.tensor_tensor(ap(o), ap(x), ap(y), o0))

    def scan(o, x, y, o1=A.add, init=0.0):
        op("v", use(x, y, init), outs(o), lambda: V.tensor_tensor_scan(ap(o), ap(x), ap(y), val(init), A.add, o1))

    def reduce(o, x, o0, neg=False):
        op("v", use(x), outs(o), lambda: V.tensor_reduce(ap(o), ap(x), AxisListType.X, o0, negate=neg))

    def fill(o, c):
        op("v", [], outs(o), lambda: V.memset(ap(o), c))

    def act(o, x, func, scale=1.0, bias=None):
        if bias is None and scale == 1.0:
            op("s", ins(o, x), outs(o), lambda: S.activation(ap(o), ap(x), func))
        elif bias is None:
            op("s", ins(o, x, scale), outs(o), lambda: S.activation(ap(o), ap(x), func, scale=val(scale)))
        else:
            op("s", ins(o, x, scale, bias), outs(o), lambda: S.activation(ap(o), ap(x), func, bias=val(bias), scale=val(scale)))

    def copy(q, o, x):
        if q == "v":
            op("v", ins(o, x), outs(o), lambda: V.tensor_copy(ap(o), ap(x)))
        else:
            act(o, x, AF.Copy)

    def lin(q, o, x, a, b=None):
        if q == "s":
            act(o, x, AF.Identity, a, b)
        elif b is None:
            ts(o, x, a, A.mult)
        else:
            ts(o, x, a, A.mult, b, A.add)

    def relu(q, o, x, scale=None, bias=None):
        if q == "s":
            act(o, x, AF.Relu, scale or 1.0, bias)
        elif scale or bias:
            ts(o, x, scale or bias, A.mult if scale else A.add, 0.0, A.max)
        else:
            ts(o, x, 0.0, A.max)

    def mm(o, lhs, x, start=True, stop=True):
        op("p", use(lhs, x), outs(o), lambda: P.matmul(ap(o), ap(lhs), ap(x), start, stop))

    def iota(o, pattern, base, cm):
        if SCRATCH[o[0]][2] == "int32":
            op("g", [], outs(o), lambda: g.iota(ap(o), pattern, base, cm))
        else:
            op("g", [], outs(o), lambda: g.iota(ap(o), pattern, base, cm, allow_small_or_imprecise_dtypes=True))

    def select(o, x, pattern, cmp, c, base, cm):
        op("g", use(x), outs(o), lambda: g.affine_select(ap(o), ap(x), pattern, cmp, c, base, cm))

    def mat(name, to=15):
        c = 144 * MATS.index(name) + 15 - to
        return ("MAT", c, c + 128)

    def paint(m, src, dst, c):
        x = (m[0], m[1] + dst, m[1] + 128, 16)
        select(x, x, [[-16, 8]], A.not_equal, c, -src, 1)

    def column(q, name, row, c):
        m = mat(name)
        lin(q, (m[0], m[1] + row, m[1] + 128, 16), ("BLK", row, 128, 16), c)

    def whole(b):
        return (b, 0, SCRATCH[b][1][1])

    def bank(b, n=B, lo=0):
        return (b, lo, lo + n)

    def kids(r, t, side, h=None):
        c = 192 * r + 48 * t + 24 * side
        return ("K16", c, c + 24) if h is None else ("K16", c + 12 * h, c + 12 * h + 12)

    def ki(r, lo, hi):
        return ("KI", 192 * r + lo, 192 * r + hi)

    def vec(t, side):
        return ("G%d" % t, B * side, B * side + B)

    def ti(t, v=1):
        c = V1 * v + L + B * t
        return ("TI", c, c + B)

    def si(t, side):
        c = N3 * side + B * (t - 1)
        return ("SI", c, c + B)

    def sz(t):
        return ("SZ", 16 + B * t, 16 + B * t + B)

    def rg(t):
        return ("RG", B * (t - 1), B * t)

    IDN, BLK, TRI, TRS = whole("IDN"), whole("BLK"), whole("TRI"), whole("TRS")
    ones = ("ONE", 0, 128)
    CN = whole("CN")
    R = ("PI", 5, 6)

    def zero(b, lo, hi, z="ZB"):
        beside("y", [z], [(b, lo, hi)], [(T[b][:, c:min(c + K, hi)], T[z][:, 0:min(K, hi - c)]) for c in range(lo, hi, K)])

    def ramps(v, rows):
        beside("y", ["RAMP"], [("TI", V1 * v, V1 * v + L)], [(T.TI[row:128:16, V1 * v:V1 * v + L], T.RAMP[:, :]) for row in rows])

    def diagonal(m, blk, src, d, c):
        x = (m, 4 * blk, 4 * blk + 4)
        select(x, x, [[-d, 4]], A.not_equal, c, -src, 1)

    def double(q, m, n):
        copy(q, (m, n, 2 * n), (m, 0, n))

    def second_view():
        g.wait_ge(T.sem["qg"], total["qg"])
        learn("g", "qg", total["qg"], {})
        op("g", ["ONE"], ["VA"], lambda: g.affine_select(T.VA[32:64, :], T.ONE[32:64, 0:128], [[-1, 8], [1, 16]], A.is_equal, 0.0, 3, -1))
        g.wait_ge(T.sem["qg"], total["qg"])
        learn("g", "qg", total["qg"], {})

    def views():
        beside("y", ["VA", "VB"], ["VC"], [x for j in range(8) for x in (
            (T.VC[0:64, 128 * j:128 * j + 128], T.VA[0:64, :]), (T.VC[64:96, 128 * j:128 * j + 128], T.VB[64:96, 16 * j + 16:16 * j + 144]))])

    def merging(b):
        for side in range(2):
            for j, m in enumerate(("TA", "TB")):
                mm(bank(b, 128, 128 * side), whole("DUP"), mat(m, 7 + 8 * (side ^ j)), side + j == 0, side + j == 2)

    def lists(r):
        copy("v", ("K16", 192 * r, 192 * r + 192), ki(r, 0, 192))

    def flag_lists(r, step):
        if step == 0:
            ts(whole("KA"), ki(r, 0, 192), 4097.0, A.mult)
        elif step == 1:
            ts(whole("KB"), whole("KA"), 4, A.arith_shift_right, 4095, A.bitwise_and)
        else:
            copy("v", whole("KP"), whole("KB"))

    def flags(t):
        act(("FS", 0, 4096, "KP", 48 * t, 48 * t + 48), whole("ZF"), AF.Silu)

    def level1_sizes(r):
        ts(whole("GE"), ki(r, 48, 96), float(L), A.is_ge, 1.0, A.add)
        tt(("SZB", 152, 176), ("GE", 0, 24), ("GE", 24, 48), A.add)

    def level1_lists(r):
        for side in range(2):
            ts(("KT", 24 * side, 24 * side + 24), ki(r, 72 - 24 * side, 96 - 24 * side), float(L), A.is_lt, float(V1), A.mult)
        tt(whole("KU"), ki(r, 48, 96), whole("KT"), A.add)
        copy("v", whole("K1"), whole("KU"))

    def to_rows(b, i):
        x = (("SZB", 152, 176), ("KF", 0, 24), ("KF", 24, 48))[i]
        for q in range(16):
            c = 16 + 128 * q - i
            mm((b, q, B, 16), ("EQ", c, c + 128), x, i < 2 and q == 0, i != 1 and q == 15)

    def extract(b, m, x, n, lo=0, hi=16):
        for q in range(lo, hi):
            mm(bank(b, n), mat(m, q), (x[0], x[1] + q, x[1] + 16 * n, 16), q == 0, q == 15)

    def kid_sizes(t, q):
        copy(q, whole("SG"), ("SZ", 0, 16 + B * t, "KZ", 48 * (t - 2), 48 * (t - 1)))

    def ranks(b1, b2):
        mm(bank(b1, NB), BLK, ("CP", 1, NB + 1))
        mm(bank(b2, NB), ("TRB", 0, 128), ("CP", 1, NB + 1), True, False)
        mm(bank(b2, NB), ("TRB", 128, 256), ("CP", 0, NB), False, True)

    def count(b, lo, hi):
        for m in range(lo, hi):
            o = ("JK", NB * m, NB * m + NB)
            op("s", [b, "BJ"], [o, ("CA", m, m + 1)],
               lambda: S.activation(ap(o), T[b][:, 0:NB], AF.Sign, bias=T.BJ[:, m:m + 1], scale=-1.0, accum_out=T.CA[:, m:m + 1]))

    def steps(b, part):
        if part == 0:
            for side, (m0, m1) in enumerate((("UL", "SL"), ("UR", "SR"))):
                mm(bank(b, B, 128), mat(m0), ("SG", B * side, B * side + B), side == 0, False)
                mm(bank(b, B - 1, 129), mat(m1), ("SG", B * side, B * side + B - 1), False, False)
            return
        m0, m1, x = ((mat("UP"), mat("SP"), "OH"), (mat("Z1", 0), mat("SC"), "CC"), (mat("US"), mat("SS"), "SO"))[part - 1]
        n = 129 if x == "CC" else 128
        mm(bank(b, n), m0, (x, 0, n), False, False)
        mm(bank(b, 128, 1), m1, (x, 0, 128), False, part == 3)

    def spots(b, step):
        if step == 0:
            ts(("AB", 0, 32), bank(b, 32), 16.0, A.mult)
            ts(("AB", 32, 64), bank(b, 32), 0.25, A.mult, 1025 - 0.375, A.add)
            ts(("AB", 64, 96), bank(b, 32), 1 / 64, A.mult, 1025 - 63 / 128, A.add)
        elif step == 1:
            for j, m in enumerate((IDN, ("IM", 0, 128), ("IM", 128, 256))):
                mm(bank(b, 32), m, ("AB", 32 * j, 32 * j + 32), j == 0, j == 2)
        else:
            ts(whole("PL"), bank(b, 32), 15 * 1025.0, A.add)

    def drop():
        copy("v", ("WD", 0, L, "PL", 0, 32), whole("DS"))

    def dropped(b, lo, hi):
        extract(b, "EX", ("WD", 0), 128, lo, hi)

    def before(b):
        mm(bank(b, 32), ("TRF", 0, 128), ("SCN", 7, 132, 4), True, False)
        mm(bank(b, 32), ("TRF", 128, 256), ("SCN", 3, 128, 4), False, True)

    def totals(b):
        for i, d in enumerate(turns(me)):
            tt(("YI", 32 * i, 32 * i + 32), ("SCN", 4 + d, 132, 4), bank(b, 32), A.add)

    def masks(i, q):
        copy(q, ("KM", 512 * i, 512 * i + 512), ("MT", 0, 1184, "CK", 32 * i, 32 * i + 32))

    def gather(r, t, side, h, q):
        o = B * side + C * h
        x = ("H%d" % r, 0, L + B * t) + kids(r, t, side, h)
        if q == "d":
            tt(("G%d" % t, o, o + C), x, ("G%d" % t, o - B, o - B + C), A.subtract)
        else:
            copy(q, ("G%d" % t, o, o + C), x)

    def sums(t, h, d=0):
        for side in range(2):
            o, m = B * side + C * h, 128 * side or 256 * d
            mm(bank("b%d" % h, C), ("MM", m, m + 128), ("G%d" % t, o, o + C), side == 0, side == 1)

    def floor(h):
        ts(("F16", C * h, C * h + C), bank("b%d" % h, C), 1536 - 0.375, A.add, 1536.0 - 127, A.max)

    def clamp(r, t, h):
        lo = L + B * t + C * h
        ts(("H%d" % r, lo, lo + C), ("F16", C * h, C * h + C), 1536.0 + 127, A.min, 1536.0, A.subtract)

    def signs(t, b, d=0):
        if not d:
            mm(bank(b), whole("WN"), vec(t, 0), t > 0, False)
        mm(bank(b), whole("WP"), vec(t, 1), d == 1, True)

    def half(x, h, n=C):
        return x if h is None else x[:-2] + (x[-2] + n * h, x[-2] + n * h + n)

    def ids(r, t, side, h, q):
        x = ("TI", 0, 2 * V1, "K1", 24 * side, 24 * side + 24) if t == 1 else ("TI", V1, V1 + L + B * t) + kids(r, t, side)
        relu(q, half(si(t, side), h), half(x, h, 12))

    merged = set()

    def merge(t, side, b, h=None):
        m = ("MG", 128 * side, 128 * side + 128) if t == 1 else mat("M2", 7 + 8 * side)
        mm(half(bank(b), h), m, half(si(t, side), h), b not in merged, b in merged)
        merged.symmetric_difference_update({b})

    def keep(t, b, h=None):
        tt(half(ti(t), h), half(bank(b), h), half(rg(t) if t < 3 else whole("AL"), h), A.min if t < 3 else A.mult)

    def choose(i):
        tt(("PR", 512 * i, 512 * i + 512), ("TI", V1, V1 + L + NT * B, "UN", 32 * i, 32 * i + 32), ("KM", 512 * i, 512 * i + 512), A.mult)

    def chosen(i, n, b):
        extract(b, "SUM", ("PR", 512 * i), 32 * n)

    def leaf_at(i, n, b, step):
        lo, hi = 32 * i, 32 * (i + n)
        if step == 0:
            copy("v", ("QA", lo, hi), bank(b, 32 * n))
        elif step == 1:
            ts(("QB", lo, hi), ("QA", lo, hi), L - 1, A.bitwise_and)
        else:
            copy("v", ("QL", lo, hi), ("QB", lo, hi))

    def engines(src, d):
        s = cores[src]
        far = [c for c in cores if topo.chip(c) != topo.chip(s)]
        if cores[d] in far:
            return topo.engines(s, cores[d])
        return [e for e in topo.engines(s, cores[d]) if e not in topo.engines(s, far[0])]

    def turns(src):
        s = cores[src]
        return sorted(range(4), key=lambda d: (d == src, topo.chip(cores[d]) == topo.chip(s), topo.die(cores[d]) != topo.die(s)))

    def shared(src):
        far1, far2, near = turns(src)[:3]
        es = engines(src, far1)
        return {far1: es[:len(es) // 2], far2: es[len(es) // 2:], near: engines(src, near)}

    def send(wb, dst, sem, to):
        tr = []
        for d, es in to.items():
            rid, pid, _se = topo.addr(cores[d])
            tr.append(RemoteDMATransfer(dst_ids=[DstId(rid=rid, pnc=pid)], dma_engine_mask=sum(1 << e for e in es),
                                        remote_sem=T.sem[sem], src=T[wb][:, 512 * d:512 * d + 512],
                                        dst=T[dst][:, 512 * me:512 * me + 512]))
        sync_for("g", [(wb, 512 * d, 512 * d + 512) for d in to], [])
        g.remote_dma_fused(tr, local_sem=T.sem["sent"])
        total["sent"] = total.get("sent", 0) + sum(len(es) for es in to.values())

    def exchange():
        send("WB0", "H1", "arr0", shared(me))
        mine = ("H1", 512 * me, 512 * me + 512)
        dma("y", ["WB0"], [mine], ap(mine), T.WB0[:, 512 * me:512 * me + 512])

    def fetch(i, q):
        d = turns(me)[i]
        o = ("WB1", 512 * d, 512 * d + 512)
        copy(q, o, ("H1", 0, L, "QL", 32 * i, 32 * i + 32))
        if d != me:
            send("WB1", "YL", "arr1_%d" % me, {d: engines(me, d)})
        else:
            dma("s", [o], [], T.y[:, 512 * me:512 * me + 512], ap(o))

    others = [s for s in range(4) if s != me]
    total["arr0"] = sum(len(shared(s)[me]) for s in others)
    for s in others:
        total["arr1_%d" % s] = len(engines(s, me))
        for b, sem in (("H1", "arr0"), ("YL", "arr1_%d" % s)):
            acc.setdefault(b, []).append(("w", 512 * s, 512 * s + 512, "x", sem, total[sem], {}))

    def node(b, t):
        c = L + B * t - (CUT if b == "TAB" else 0)
        return (b, c, c + B)

    def sr(t, side):
        c = N3 * side + B * (t - 1)
        return ("SR", c, c + B)

    def ym(i):
        return ("YM", 128 * i, 128 * i + 128)

    def own(t, q):
        lin(q, node("M", t), whole("STEP"), co(E0), co(I0 + t))

    def turn(t, q):
        lin(q, whole("PRE"), node("M", t), 1.0, co(AT + t))

    def hand(t, side, q):
        x = node("M", 3 + side) if t == 3 else whole("PRE") if side else node("M", t)
        if q == "s":
            act(("M", 0, L + B * t) + kids(0, t, side), x, AF.Silu)
        else:
            copy(q, ("M", 0, L + B * t) + kids(0, t, side), x)

    def narrow(k, q):
        lo, hi = PART[k]
        relu(q, ("MB", 16 * lo, 16 * hi), ("M", 16 * lo, 16 * hi), None, co(MB))

    def leaf_codes(b, k):
        lo, hi = PART[k]
        for q in range(16):
            mm(bank(b, hi - lo, lo), mat("Z1", q), ("MB", 16 * lo + q, 16 * hi, 16), q == 0, q == 15)

    def runs(t):
        return [(q, max(B * t - RUN * q, 0), min(B * t + B - RUN * q, RUN), max(RUN * q - B * t, 0))
                for q in range(B * t // RUN, -(-(B * t + B) // RUN))]

    def node_sizes(t):
        if t == 0:
            for q, lo, hi, c in runs(0):
                mm(bank("b6", hi), mat("Z1", q), ("S0", 0, hi), q == 0, False)
            return
        for side in range(2):
            for q, lo, hi, c in runs(t):
                c += sr(t, side)[1]
                mm(bank("b6", hi - lo, lo), mat("DQZ", q), ("SR", c, c + hi - lo), False, side + q == 16)

    def leaf_list(b, k):
        lo, hi = PART[k]
        ts(("PT", lo, hi), bank(b, hi - lo, lo), float(CODE), A.subtract)

    def leaf_flag(b, k):
        lo, hi = PART[k]
        ts(("FL", lo, hi), bank(b, hi - lo, lo), float(CODE), A.is_lt)

    def rows(t, side, q):
        c = 48 * t + 24 * side
        copy(q, sr(t, side), ("TAB", 0, L + B * t - CUT, "KS", c, c + 24))

    def diff(t, b, d=0):
        if not d:
            mm(bank(b), whole("WN0"), vec(t, 0), t > 0, False)
        mm(bank(b), whole("WP0"), vec(t, 1), d == 1, True)

    def pick(t, b):
        for side in range(2):
            mm(bank(b), ym(2 * (t - 1) + side), sr(t, side), side == 0, False)

    def edge_store(side, b):
        tt(node("TAB", 3 + side), sr(3, side), bank(b), A.max)

    def sum_up(k):
        lo, hi = PART[k]
        tt(("PR", 16 * lo, 16 * hi), ("TAB", 0, TW, "PT", lo, hi), ("MB", 16 * lo, 16 * hi), A.mult)

    def summed(k):
        lo, hi = PART[k]
        for q in range(16):
            mm(bank("b%d" % k, hi - lo), mat("DQS", q), ("PR", 16 * lo + q, 16 * hi, 16), q == 0, False)

    def add_roots(k):
        lo, hi = PART[k]
        mm(bank("b%d" % k, hi - lo), IDN, ("RM", lo, hi), False, True)

    def places(k, step):
        lo, hi = PART[k]
        if step == 0:
            ts(("QA", lo, hi), bank("b%d" % k, hi - lo), 2049.0, A.mult)
        elif step == 1:
            ts(("QB", lo, hi), ("QA", lo, hi), 2, A.arith_shift_right, 2047, A.bitwise_and)
        else:
            copy("v", ("QL", lo, hi), ("QB", lo, hi))

    def scatter(lo, hi):
        copy("v", ("WB0", 0, L, "QL", lo, hi), ("H0", 16 * lo, 16 * hi))

    dma("y", [], [("KI", 0, 192)], T.KI[:, 0:192], T.kids[:, 0:192])
    iota(("PI", 0, 1), [[0, 1]], 0, 1)
    iota(whole("STEP"), [[1, B]], 0, 0)
    iota(whole("ZB"), [[0, K]], 0, 0)
    fill(whole("ONE"), 1.0)
    select(whole("BLA"), ones, [[-16, 8], [0, 16]], A.is_ge, 0.0, 0, 1)
    iota(("LN", 0, 8), [[0, 8]], 0, 0)
    iota(("LA", 0, 16), [[0, 16]], 0, 0)
    iota(whole("BJ"), [[16, 8]], 0, 0)
    select(BLK, whole("BLA"), [[16, 8], [0, 16]], A.is_ge, 0.0, 15, -1)
    iota(whole("S0"), [[0, RUN]], 2, 0)
    select(whole("BLS"), BLK, [[0, 8], [1, 16]], A.is_ge, 0.0, -EVEN, 0)
    dma("y", [], [("MI", 0, 128)], T.MI[:, 0:128], T.ml[:, :])
    dma("y", [], ["WI"], T.WI[:, :], T.w[:, :])
    dma("y", [], [("MI", 128, 256)], T.MI[:, 128:256], T.mr[:, :])
    dma("y", [], [("H0", 0, L)], T.H0[:, 0:L], T.x[:, :])
    dma("y", [], [("KI", 192, 384)], T.KI[:, 192:384], T.kids[:, 192:384])
    zero("MAT", 0, 144 * 8)
    paint(mat("Z1"), SIZE, 15, 1.0)
    select(IDN, ones, [[-1, 128]], A.is_equal, 0.0, 0, 1)
    iota(whole("OWN"), [[1, RUN]], 16 + CODE, 0)
    select(mat("DM1"), mat("DM1"), [[-16, 8], [1, 4], [0, 4]], A.not_equal, 1.0, -11, 1)
    for i, (pattern, base) in enumerate((([[0, 8], [1, 4], [0, 4]], -2), ([[0, 8], [1, 4], [0, 4]], -3),
                                         ([[0, 32], [1, 2], [0, 2]], 0), ([[0, 32], [1, 2], [0, 2]], -1))):
        select(ym(i), IDN, pattern, A.is_equal, 0.0, base, 0)
    for i, src, dst, c in ((0, SIZE, SIZE, 1.0), (1, SIZE, SIZE, 1.0), (3, SIZE, SIZE, 1.0), (2, SIZE, D2R, 1.0), (3, START, START, 0.0)):
        paint(ym(i), src, dst, c)
    iota(("F", RUN, RUN + 8), [[0, 8]], -8, 0)
    iota(whole("ONF"), [[0, 256]], 1, 0)
    paint(mat("DQZ"), SIZE, 15, 256.0)
    paint(ym(3), SIZE, D2L, 1.0)
    select(TRS, BLK, [[1, 128]], A.is_gt, 0.0, 0, -1)
    for m, src, dst, c in (("NR2", EVEN, D2L, -1.0), ("S3L", SIZE, D3R, 1.0), ("NR2", ODD, D2R, -1.0), ("S3R", SIZE, D3L, 1.0),
                           ("S3L", SIZE, START, -256.0), ("NR3", EVEN, D3L, -1.0), ("S3R", SIZE, START, -256.0), ("NR3", ODD, D3R, -1.0)):
        paint(mat(m), src, dst, c)
    iota(("SZ", 0, 16 + B), [[0, 16 + B]], 1, 0)
    select(("TRB", 0, 128), TRS, [[-1, 128]], A.not_equal, RANK + 1, 0, 1)
    select(whole("VB"), ("ONE", 0, 256), [[-1, 16], [1, 16]], A.is_equal, 0.0, 67, -1)
    select(whole("VA"), ones, [[0, 8], [1, 16]], A.is_equal, 0.0, 4, -1)

    act(("M", 0, 512), whole("ONE"), AF.Silu, BASE)
    ts(("PI", 6, 7), ("PI", 0, 1), 13, A.bitwise_and)
    lin("v", ("M", 1024, 1536), whole("ONE"), BASE)
    ts(R, ("PI", 0, 1), 15, A.bitwise_and)
    for j, bit in enumerate((0, 2, 1, 3)):
        ts(("PI", 1 + j, 2 + j), ("PI", 0, 1), bit, A.arith_shift_right, 1, A.bitwise_and)
    ts(co(I0, 5), ("STEP", 0, 5), float(B), A.mult, CODE + 16 - BASE, A.add)
    ts(co(E0), R, float(SIZE), A.is_equal)
    lin("v", ("M", 512, 1024), whole("ONE"), BASE)
    ts(co(SS + 3), ("PI", 6, 7), 1.0, A.is_equal, TURN, A.mult)
    ts(co(I0, 5), co(I0, 5), co(E0), A.mult, BASE, A.add)
    own(2, "s")
    ts(co(U, 4), ("PI", 1, 5), 2.0, A.mult, -1.0, A.add)
    lin("s", co(AT + 3), co(SS + 3), co(U + 2))
    own(0, "s")
    lin("s", co(E1), co(E0), 1 / 256)
    copy("v", co(BF, 4), ("PI", 1, 5))
    own(1, "s")
    lin("v", ("M", 1536, 2048), whole("ONE"), BASE)
    fill(CN, -1 / 32)
    lin("v", ("MM", 0, 256), whole("MI"), 0.25)
    own(3, "v")
    lists(0)
    lin("v", co(I0 + 4), co(I0 + 4), 1.0, co(AT + 3))
    lin("v", co(LO), co(E0), 2 / 256)

    hand(3, 0, "v")
    own(4, "s")
    gather(0, 0, 0, 0, "s")
    gather(0, 0, 0, 1, "s")
    lin("s", co(SS, 2), co(BF, 2), 0.0, co(BF + 3))
    lin("s", ("SGB", 0, 128, 2), ("BLS", 0, 128, 2), -1 / 16)
    gather(0, 0, 1, 0, "s")
    hand(3, 1, "s")
    zero("MAT", 144 * 8, 144 * len(MATS))
    gather(0, 0, 1, 1, "v")
    sums(0, 1)
    tt(co(SS + 2), co(BF + 3), co(BF + 1), A.max)
    lin("v", ("SGB", 1, 128, 2), ("BLS", 1, 128, 2), 1 / 16)
    ts(("KS", 48, 192), ki(0, 48, 192), float(CUT), A.subtract)
    ts(whole("WP0"), whole("SGB"), whole("WI"), A.mult)
    tt(co(VV, 3), co(SS, 3), co(U, 3), A.mult)
    floor(1)
    sums(0, 0)
    lin("v", whole("WN0"), whole("WP0"), -1.0)
    lin("v", co(HT), co(BF + 3), 1 / 256, co(LO))
    ts(co(E2), R, float(START), A.is_equal, BIG, A.mult)
    floor(0)
    lin("v", co(AT + 1, 2), co(VV + 1, 2), TURN)
    lin("v", co(AT), co(VV), -TURN)
    lin("v", co(HC), co(HT), 1.0, co(E2))
    clamp(0, 0, 0)
    clamp(0, 0, 1)
    hand(2, 0, "v")
    lin("s", ("TAB", 0, 16), ("ONE", 0, 16), co(E1))
    lin("s", co(CR), co(U), -1 / 32)
    turn(2, "s")
    mm(bank("b2"), whole("SGB"), CN, True, False)
    diff(0, "b2")
    ts(node("TAB", 0), bank("b2"), co(LO), A.max, co(HC), A.min)
    hand(2, 1, "v")
    gather(0, 1, 1, 0, "s")
    gather(0, 1, 0, 0, "s")
    node_sizes(0)
    sums(1, 0)
    gather(0, 1, 0, 1, "s")
    gather(0, 1, 1, 1, "s")
    diff(1, "b7")
    rows(1, 0, "s")
    relu("s", rg(1), bank("b7"), None, co(CR))
    hand(1, 0, "s")
    turn(1, "s")
    rows(1, 1, "v")
    ts(co(RF), R, float(RUN), A.mult)
    ts(whole("OWH"), whole("OWN"), co(RF), A.add, 0.5, A.add)
    floor(0)
    sums(1, 1)
    ts(co(Z0), R, float(SIZE), A.not_equal)
    floor(1)
    clamp(0, 1, 0)
    lin("v", co(NC), co(BF + 2), -1.0, 1.0)
    relu("v", co(AP, 4), co(AT, 4))
    mm(bank("b2"), mat("Z1", EVEN), sr(1, 0), True, False)
    mm(bank("b2"), mat("Z1", ODD), sr(1, 1), False, True)
    clamp(0, 1, 1)
    tt(whole("DG"), rg(1), bank("b2"), A.min)
    reduce(co(TS), co(AP, 4), A.add)
    gather(0, 2, 1, 1, "s")
    lin("s", co(TB), co(TS), -1.0, MASK - BASE)
    hand(1, 1, "s")
    dma("y", [("M", L, EDGE)], ["NCO"], T.NCO[:, :], T.M[SIZE:128:16, L:EDGE])
    dma("y", ["ONF"], ["FS"], T.FS[0:128:16, :], T.ONF[:, :])
    zero("EQ", 0, 16 + 16 * 128)

    select(("EQ", 16, 16 + 16 * 128, 16), ("EQ", 16, 16 + 16 * 128, 16), [[-1, 16], [-16, 8]], A.not_equal, 1.0, 0, 1)
    select(TRI, BLK, [[-1, 128]], A.is_ge, 0.0, 0, 1)
    iota(whole("ZF"), [[0, K]], 0, 0)
    iota(("SCN", 0, 4), [[0, 4]], 0, 0)
    for j, (blk, src, d, c) in enumerate(((0, 4, 1, LOW), (1, 35, -1, HIGH), (2, 36, 1, HIGH), (3, 67, -1, LOW),
                                          (0, 100, 1, HIGH), (1, 67, -1, LOW), (2, 4, 1, LOW), (3, 99, -1, HIGH))):
        diagonal("LA", blk, src, d, c / 2)
        if j < 2:
            diagonal("LN", j, (4, 35)[j], 1 - 2 * j, LOW)
    second_view()
    for j, (m, src, dst, c) in enumerate((("TB", 0, 1, 1.0), ("TB", 1, 2, 1.0), ("TB", 2, 2, 1.0), ("TB", 3, 3, 1.0), ("TB", 2, 1, -1.0),
                                          ("TA", 0, 0, 1.0), ("TB", 3, 2, -1.0), ("TA", 1, 1, 1.0))):
        x = (mat(m, 7)[0], mat(m, 7)[1] + dst, mat(m, 7)[2], 4)
        select(x, x, [[-16, 8], [1000, 2], [-4, 2]], A.not_equal, c, -src, 1)
        m, src, dst, c = (("UL", 0, 2, 1.0), ("UR", 0, 2, 8.0), ("SL", 0, 2, -1.0), ("SL", 0, 3, 1.0), ("SL", 1, 1, 1.0), ("SR", 0, 2, -8.0),
                          ("SR", 0, 3, 1.0), ("SC", 0, 0, -1.0))[j]
        paint(mat(m), src, dst, c)
    for h in range(2):
        select(("VC", 512 * h, 512 * h + 512), whole("ONE"), [[-1, 4], [0, 8], [1, 16]], A.is_equal, 0.0, 99 - 4 * h, -1)
    select(whole("DUP"), ones, [[-16, 8], [0, 2], [-1, 8]], A.is_equal, 0.0, 0, 1)
    for j in range(2):
        x = (mat("M0")[0], mat("M0")[1] + j, mat("M0")[2], 2)
        select(x, x, [[-16, 8], [2 * j - 1, 2], [0, 4]], A.not_equal, 0.5, -1 - j, 1)
        select(mat("M2", 7), mat("M2", 7), [[-16, 8], [1000, 2], [-1, 8]], A.not_equal, 2.0, -8 * j, 1)
    select(("TRB", 128, 256), TRI, [[-1, 128]], A.not_equal, -RANK, 0, 1)

    gather(0, 2, 0, 1, "v")
    gather(0, 2, 0, 0, "v")
    gather(0, 2, 1, 0, "v")
    pick(1, "b3")
    mm(bank("b3"), mat("DM1"), whole("DG"), False, True)
    sums(2, 1)
    node_sizes(1)
    sums(2, 0)
    column("v", "SS", 2, -1.0)
    floor(1)
    turn(0, "v")
    copy("v", node("TAB", 1), bank("b3"))
    flag_lists(1, 0)
    rows(2, 0, "v")
    tt(("F", 0, RUN), whole("NCO"), whole("OWH"), A.is_lt)
    clamp(0, 2, 1)
    floor(0)
    lin("s", co(MB), co(TB), co(Z0))
    hand(0, 0, "s")
    rows(2, 1, "s")
    diff(2, "b7")
    node_sizes(2)
    pick(2, "b4")
    mm(bank("b5", RUN + 1), BLK, ("F", 0, RUN + 1))
    ts(("INC", 0, 1), co(E0), 0.0, A.mult)
    clamp(0, 2, 0)
    flag_lists(1, 1)
    ts(co(WA), whole("WI"), -2.0, A.mult)
    tt(whole("RS"), ("F", 0, RUN), bank("b6", RUN), A.mult)
    gather(0, 3, 0, 0, "v")
    ts(co(TN), co(U + 3), co(U + 1), A.mult, 2048.0, A.mult)
    scan(("INC", 1, RUN + 1), whole("RS"), whole("RS"), A.max)
    gather(0, 3, 1, 0, "d")
    hand(0, 1, "s")
    relu("s", rg(2), bank("b7"), None, co(CR))
    gather(0, 3, 0, 1, "s")
    gather(0, 3, 1, 1, "d")
    mm(bank("b4"), mat("NR2"), rg(2), False, True)
    relu("v", node("TAB", 2), bank("b4"))
    reduce(("OFS", 0, 1), bank("b5", RUN + 1), A.add, True)
    ts(co(Z2), R, float(START), A.not_equal, 256 / MASK, A.mult)
    ts(whole("KF"), ki(1, 0, 48), 1.0, A.mult)
    narrow(1, "s")
    rows(3, 0, "s")
    mm(bank("b6", 1, 300), TRS, ("INC", RUN, RUN + 1))
    mm(bank("b6", 1, 301), BLK, ("INC", RUN, RUN + 1))
    diff(3, "b7", 1)
    leaf_codes("b4", 1)
    mm(bank("b5"), mat("S3L"), sr(3, 0), True, False)
    ts(whole("RL"), ("INC", 0, RUN), bank("b6", 1, 300), A.add, ("OFS", 0, 1), A.add)
    ts(co(WS), co(Z2), 1 / MASK, A.max, co(Z0), A.mult)
    ts(co(WB), whole("WI"), 2.0, A.mult)
    rows(3, 1, "v")
    mm(bank("b5"), mat("S3R"), sr(3, 1), False, False)
    ts(("OFS", 1, 2), bank("b6", 1, 301), ("OFS", 0, 1), A.add, 1 / 256, A.mult)
    leaf_list("b4", 1)
    flag_lists(1, 2)
    scan(whole("IX"), sr(3, 0), sr(3, 1), A.add, ("OFS", 1, 2))
    mm(bank("b5"), mat("DQZ", START), whole("IX"), False, False)
    relu("v", rg(3), bank("b7"), None, co(CR))
    mm(bank("b5"), mat("NR3"), rg(3), False, True)
    ts(co(RW), R, 1.0, A.mult)
    ts(("PI", 7, 8), ("PI", 0, 1), 4, A.arith_shift_right)
    ts(co(RH), ("PI", 7, 8), float(L), A.mult)
    ts(co(E1), R, 1.0, A.is_equal)
    level1_sizes(1)
    edge_store(0, "b5")
    ts(("CP", 0, 1), co(E1), 0.0, A.mult)
    edge_store(1, "b5")
    leaf_flag("b4", 1)
    column("s", "US", 2, 1.0)
    narrow(0, "s")
    leaf_codes("b2", 0)
    column("v", "SUM", 15, 128.0)
    leaf_list("b2", 0)
    double("v", "LN", 8)
    leaf_flag("b2", 0)
    to_rows("b3", 0)
    mm(bank("b4", 128, 128), BLK, whole("FL"))
    mm(bank("b4", 128, 256), TRI, whole("FL"))
    to_rows("b5", 1)
    dma("y", ["RL"], [("TAB", 16, 16 + N3)], T.TAB[START:128:16, 16:16 + N3], T.RL[:, :])

    sum_up(0)
    column("v", "DQS", 15, co(WS))
    summed(0)
    scan(whole("IL"), bank("b4", 128, 128), whole("FL"), A.max)
    tt(whole("IL"), whole("IL"), bank("b4", 128, 256), A.subtract)
    tt(whole("RM"), whole("IL"), whole("FL"), A.mult)
    add_roots(0)
    ts(whole("KZ"), ki(1, 96, 192), float(CUT), A.subtract)
    sum_up(1)
    places(0, 0)
    flags(0)
    flags(1)
    column("s", "SS", 3, 1.0)
    lin("s", co(RN), co(RW), -1.0)
    ts(whole("BJ"), whole("BJ"), co(RW), A.add, 0.5, A.add)
    double("v", "LA", 16)
    column("v", "SP", 1, co(RN))
    places(0, 1)
    places(0, 2)
    scatter(0, 32)
    to_rows("b5", 2)
    summed(1)
    add_roots(1)
    places(1, 0)
    scatter(32, 64)
    flags(2)
    zero("WD", 0, L)
    dma("y", ["S0"], [sz(0)], T.SZ[0:128:16, 16:16 + B], T.S0[:, 0:24])
    zero("TI", 0, L, "ZF")
    zero("TI", V1, V1 + L, "ZF")
    views()
    lin("s", sz(1), bank("b3"), co(E0), co(E1))
    kid_sizes(2, "s")
    copy("s", whole("LR"), bank("b5"))
    lin("s", co(TH), co(TN), -1.0)
    double("s", "LN", 16)
    double("s", "LN", 32)
    lin("s", whole("NG"), IDN, co(TN))
    double("s", "LN", 64)
    flags(3)
    dma("y", ["FS"], ["FB"], T.FB[:, :], T.FS[0:128:16, :])
    places(1, 1)
    double("v", "LA", 32)
    places(1, 2)
    scatter(64, 96)
    column("v", "UP", 1, co(RW))
    scatter(96, 128)
    exchange()
    iota(("CC", 128, 144), [[0, 16]], NB, 0)
    iota(whole("CT"), [[1, 208]], 0, 0)
    select(("IM", 128, 256), IDN, [[-1, 128]], A.not_equal, 48.0, 0, 1)
    iota(("MT", 0, 17), [[0, 17]], 0, 0)
    iota(("SZB", 0, 128), [[0, 128]], 1, 0)
    iota(("SZB", 128, 152), [[0, 24]], 2, 0)
    iota(whole("RAMP"), [[1, 128]], 0, 128)
    iota(whole("JJ"), [[1, 128]], int(RANK) + 1, 0)
    paint(mat("Z3"), 3, 15, 1.0)
    select(("IM", 0, 128), IDN, [[-1, 128]], A.not_equal, -63.0, 0, 1)
    for j, c in enumerate((32768.0, 2048.0, 16.0, -1.0)):
        paint(mat("EX"), j, 15, c)
    iota(("MT", 1169, 1184), [[0, 15]], 0, 0)

    mm(bank("b7"), mat("Z1", SIZE), ("SG", 0, B), True, False)
    mm(bank("b7"), mat("Z1", SIZE), ("SG", B, K), False, True)
    merging("b2")
    lin("s", sz(2), bank("b7"), co(E0), co(E1))
    copy("s", whole("MG"), bank("b2", 256))
    extract("b4", "Z1", sz(2), 24)
    double("s", "LA", 64)
    mm(bank("b0", 512), whole("LA"), ("VC", 0, 512))
    mm(bank("b2", 128), whole("LN"), whole("VA"))
    kid_sizes(3, "s")
    mm(bank("b5"), mat("M0"), whole("LR"))
    scan(("CP", 1, NB + 1), ("FB", 0, NB), ("FB", 0, NB), A.max)
    lists(1)
    level1_lists(1)
    tt(("MM", 256, 384), ("MM", 0, 128), ("MM", 128, 256), A.add)
    ranks("b6", "b3")
    mm(bank("b1", 512), whole("LA"), ("VC", 512, 1024))
    copy("v", ("RK", 0, NB), bank("b3", NB))
    copy("v", ("MT", 17, 145), bank("b2", 128))
    copy("v", ("MT", 145, 657), bank("b0", 512))
    steps("b7", 0)
    mm(bank("b2"), whole("NG"), ("ONE", 0, B), True, False)
    copy("v", ("SZB", 176, 200), bank("b4", 24))
    copy("v", ("MT", 657, 1169), bank("b1", 512))
    mm(bank("b3", 128), BLK, whole("NG"))
    count("b6", 0, 4)
    count("b6", 4, 8)
    ts(whole("CL"), whole("CA"), 0.5, A.mult, NB / 2, A.add)
    tt(whole("OH"), ("RK", 0, NB, "CL", 0, 8), whole("JJ"), A.is_equal)
    ts(whole("RAMP"), whole("RAMP"), co(RH), A.subtract, 0.5, A.mult)
    copy("s", ("CC", 0, 128), ("CT", 0, NB, "CL", 0, 8))
    steps("b7", 1)
    steps("b7", 2)
    tt(whole("SO"), ("SZB", 0, NB, "CL", 0, 8), whole("OH"), A.mult)
    steps("b7", 3)
    lin("s", whole("WP"), bank("b3", 128), co(WA))
    lin("v", whole("WN"), bank("b3", 128), co(WB))

    gather(1, 0, 1, 1, "v")
    gather(1, 0, 0, 1, "s")
    gather(1, 0, 0, 0, "s")
    gather(1, 0, 1, 0, "v")
    sums(0, 1)
    copy("s", whole("DS"), bank("b7", 512))
    sums(0, 0)
    floor(1)
    copy("s", whole("X0"), bank("b5"))
    signs(0, "b2")
    floor(0)
    clamp(1, 0, 1)
    scan(whole("SV"), whole("DS"), ("ZB", 0, 512))
    clamp(1, 0, 0)
    extract("b4", "Z3", ("SV", 0), 32)
    gather(1, 1, 0, 0, "s")
    gather(1, 1, 0, 1, "s")
    ramps(0, (0, 2, 4, 6))
    ramps(1, (0, 4))
    copy("s", ("TRF", 0, 128), TRS)
    relu("v", ("TRF", 128, 256), ("TRB", 128, 256))
    tt(ti(0, 0), bank("b2"), whole("X0"), A.min)
    relu("s", ti(0), ti(0, 0), co(NC))
    ids(1, 1, 0, 1, "s")
    gather(1, 1, 1, 0, "d")
    sums(1, 0, 1)
    spots("b4", 0)
    spots("b4", 1)
    gather(1, 1, 1, 1, "d")
    sums(1, 1, 1)
    signs(1, "b7", 1)
    spots("b4", 2)
    ids(1, 1, 0, 0, "v")
    ids(1, 1, 1, 0, "s")
    merge(1, 0, "b3", 0)
    merge(1, 1, "b3", 0)
    merge(1, 0, "b5", 1)
    ids(1, 1, 1, 1, "s")
    merge(1, 1, "b5", 1)
    drop()
    relu("s", rg(1), bank("b7"), None, co(TN))
    floor(1)
    keep(1, "b3", 0)
    floor(0)
    clamp(1, 1, 1)
    keep(1, "b5", 1)
    dropped("b6", 0, 4)
    ids(1, 2, 0, 1, "s")
    clamp(1, 1, 0)
    dropped("b6", 4, 8)
    gather(1, 2, 0, 0, "v")
    gather(1, 2, 0, 1, "s")
    ids(1, 2, 1, 1, "s")
    ids(1, 2, 0, 0, "s")
    gather(1, 2, 1, 0, "d")
    dropped("b6", 8, 12)
    merge(2, 0, "b5", 1)
    gather(1, 2, 1, 1, "d")
    sums(2, 0, 1)
    signs(2, "b2", 1)
    floor(0)
    ids(1, 2, 1, 0, "v")
    sums(2, 1, 1)
    relu("s", rg(2), bank("b2"), None, co(TN))
    merge(2, 1, "b5", 1)
    floor(1)
    keep(2, "b5", 1)
    clamp(1, 2, 0)
    clamp(1, 2, 1)
    merge(2, 0, "b3", 0)
    merge(2, 1, "b3", 0)
    dropped("b6", 12, 16)
    keep(2, "b3", 0)
    gather(1, 3, 0, 1, "v")
    gather(1, 3, 0, 0, "s")
    scan(("SCN", 4, 132), bank("b6", 128), ones)
    before("b4")
    gather(1, 3, 1, 1, "d")
    gather(1, 3, 1, 0, "d")
    ids(1, 3, 0, 1, "s")
    ids(1, 3, 1, 1, "s")
    ids(1, 3, 1, 0, "s")
    ids(1, 3, 0, 0, "s")
    totals("b4")
    merge(3, 0, "b5", 1)
    signs(3, "b7", 1)
    merge(3, 1, "b5", 1)
    ts(whole("YA"), whole("YI"), L - 1, A.bitwise_and)
    ts(whole("YB"), whole("YI"), 11, A.arith_shift_right)
    copy("v", whole("CK"), whole("YA"))
    ts(whole("AL"), bank("b7"), co(TH), A.is_ge, SMALL, A.max)
    copy("v", whole("UN"), whole("YB"))
    keep(3, "b5", 1)
    for i in range(4):
        masks(i, "s")
    merge(3, 0, "b3", 0)
    merge(3, 1, "b3", 0)
    keep(3, "b3", 0)

    choose(0)
    chosen(0, 1, "b0")
    choose(1)
    choose(2)
    leaf_at(0, 1, "b0", 0)
    chosen(1, 2, "b1")
    leaf_at(0, 1, "b0", 1)
    leaf_at(0, 1, "b0", 2)
    choose(3)
    chosen(3, 1, "b2")
    leaf_at(1, 2, "b1", 0)
    fetch(0, "s")
    leaf_at(1, 2, "b1", 1)
    leaf_at(1, 2, "b1", 2)
    fetch(1, "v")
    fetch(2, "s")
    for step in range(3):
        leaf_at(3, 1, "b2", step)
    fetch(3, "s")
    for i, s in enumerate(sorted(others, key=lambda s: turns(s).index(me))):
        dma("yys"[i], [("YL", 512 * s, 512 * s + 512)], [], T.y[:, 512 * s:512 * s + 512], T.YL[:, 512 * s:512 * s + 512])
    for sem in sorted(total):
        if known["g"].get(sem, 0) < total[sem]:
            g.wait_ge(T.sem[sem], total[sem])
